import numpy as np
import ml_dtypes


def mxq(x, axis, fmt="e4m3"):
    dtype, down = {"e4m3": (ml_dtypes.float8_e4m3fn, 7), "e5m2": (ml_dtypes.float8_e5m2, 14)}[fmt]
    v = np.moveaxis(np.asarray(x, np.float32).astype(ml_dtypes.bfloat16).astype(np.float64), axis, -1)
    blocks = v.reshape(v.shape[:-1] + (-1, 32))
    amax = np.abs(blocks).max(-1, keepdims=True)
    byte = np.maximum(np.where(amax > 0, np.frexp(amax)[1] - 1 + 127, 0) - down, 1)
    scale = np.exp2(byte - 127.0)
    codes = (blocks / scale).astype(np.float32).astype(dtype).astype(np.float64)
    return np.moveaxis((codes * scale).reshape(v.shape), -1, axis)


WIDE = False


def mx_kscale(k):
    if not WIDE:
        return np.ones(k)
    levels = np.array([10, -10, 5, -5, 0])
    if k % 512:
        return np.exp2(np.random.permutation(np.resize(levels, k // 32))).repeat(32)
    a = np.empty((k // 512, 16))
    for p in range(k // 512):
        a[p, :8] = np.random.permutation(np.resize(levels, 8))
        for g in range(8):
            far = levels[np.abs(levels - a[p, g]) >= 10]
            a[p, g + 8] = far[np.random.randint(len(far))]
    return np.exp2(a.ravel()).repeat(32)


def f64(x):
    return np.asarray(x).astype(np.float64)


def striped(idx):
    return np.tile(idx.reshape(-1, 16).T, (8, 1)).astype(np.uint16)


def unstriped(offs):
    return offs[:16].T.reshape(-1).astype(np.int64)


E2M1 = np.array([0.0, 0.5, 1.0, 1.5, 2.0, 3.0, 4.0, 6.0, -0.0, -0.5, -1.0, -1.5, -2.0, -3.0, -4.0, -6.0])


def pack_weight(w, fmt):
    k, n = w.shape
    w = f64(np.asarray(w, np.float32).astype(ml_dtypes.bfloat16)).reshape(k // 32, 32, n)
    amax = np.abs(w).max(1)
    if fmt == "e4m3":
        byte = np.frexp(amax)[1] - 1 + 127 - 7
    else:
        mant, ex = np.frexp(amax / 6.0)
        byte = np.where(mant > 0.5, ex, ex - 1) + 127
    byte = np.clip(np.where(amax > 0, byte, 1), 1, 254)
    scaled = (w * np.exp2(127.0 - byte)[:, None, :]).reshape(k, n).astype(np.float32)
    by_word = np.ascontiguousarray(scaled.reshape(k // 512, 128, 4, n).transpose(0, 1, 3, 2))
    if fmt == "e4m3":
        words = by_word.astype(ml_dtypes.float8_e4m3fn).view(np.uint8)
    else:
        c = by_word.astype(ml_dtypes.float4_e2m1fn).view(np.uint8) & 0xF
        words = (c[..., 0::2] | (c[..., 1::2] << 4)).reshape(k // 512, 128, 2 * n)
    return np.ascontiguousarray(words), np.ascontiguousarray(byte.astype(np.uint8).reshape(k // 512, 16, n))


def unpack_weight(words, scales, fmt):
    g, _, n = scales.shape
    words = np.ascontiguousarray(words).reshape(g, 128, n, -1)
    if fmt == "e4m3":
        vals = words.view(ml_dtypes.float8_e4m3fn).astype(np.float64)
    else:
        nib = np.empty((g, 128, n, 4), np.uint8)
        nib[..., 0::2] = words & 0xF
        nib[..., 1::2] = words >> 4
        vals = E2M1[nib]
    vals = vals * np.repeat(np.exp2(scales.astype(np.float64) - 127.0), 8, axis=1)[..., None]
    return vals.transpose(0, 1, 3, 2).reshape(g * 512, n)


def relu2(v):
    return np.maximum(v, 0.0) ** 2


def sigmoid(v):
    return 1.0 / (1.0 + np.exp(-np.maximum(v, -700.0)))


K, T, E, C, H, N, TOP = 1024, 640, 15, 128, 512, 256, 3


def by_expert(wq, xq):
    return np.concatenate([wq[e].T @ xq[:, e * C:(e + 1) * C] for e in range(E)], axis=1)


def setup_inputs():
    n = np.random.standard_normal
    s = mx_kscale(K)
    u = mx_kscale(H)
    deal = np.repeat(np.arange(E), C).reshape(TOP, T)[:, np.random.permutation(T)]
    deal = np.take_along_axis(deal, np.argsort(np.random.rand(TOP, T), axis=0), axis=0)
    for _ in range(8):
        s_, t_ = np.random.permutation(T).reshape(2, -1); r = np.random.randint(TOP, size=T // 2); x, y = deal[r, s_].copy(), deal[r, t_].copy()
        ok = ~((deal[:, s_] == y).any(0) | (deal[:, t_] == x).any(0)); deal[r[ok], s_[ok]] = y[ok]; deal[r[ok], t_[ok]] = x[ok]
    order = np.argsort(deal.reshape(-1) + 0.5 * np.random.rand(TOP * T))
    slot_token = order % T; pos = np.empty(TOP * T, np.int64); pos[order] = np.arange(TOP * T); pos = pos.reshape(TOP, T)
    g = np.random.uniform(0.5, 1.5, (TOP, T)); g = g / g.sum(0)
    x = pack_weight(n((K, T)) * s[:, None], "e4m3")
    wg = pack_weight(n((K, N)) / np.sqrt(K) / s[:, None], "e4m3")
    w1 = [pack_weight(m, "e2m1") for m in n((E, K, H)) / np.sqrt(K) / s[None, :, None] * u]
    w2 = [pack_weight(m, "e2m1") for m in n((E, H, N)) / np.sqrt(H) / u[None, :, None] ** 2]
    return {
        "x_words": x[0],
        "x_scales": x[1],
        "wg_words": wg[0],
        "wg_scales": wg[1],
        "w1_words": np.stack([m[0] for m in w1]),
        "w1_scales": np.stack([m[1] for m in w1]),
        "w2_words": np.stack([m[0] for m in w2]),
        "w2_scales": np.stack([m[1] for m in w2]),
        "gate": np.stack([np.tile(r, (128, 1)) for r in g]).astype(np.float32),
        "offs": striped(slot_token),
        "pos1": striped(pos[0]),
        "pos2": striped(pos[1]),
        "pos3": striped(pos[2]),
    }


def reference(x_words, x_scales, wg_words, wg_scales, w1_words, w1_scales, w2_words, w2_scales, gate, offs, pos1, pos2, pos3):
    wg = unpack_weight(wg_words, wg_scales, "e4m3")
    w1 = np.stack([unpack_weight(w1_words[e], w1_scales[e], "e2m1") for e in range(E)])
    w2 = np.stack([unpack_weight(w2_words[e], w2_scales[e], "e2m1") for e in range(E)])
    idx = unstriped(offs)
    x = unpack_weight(x_words, x_scales, "e4m3")
    o = sigmoid(wg.T @ x)
    h = relu2(by_expert(w1, x[:, idx]))
    y = by_expert(w2, mxq(h, 0, "e4m3"))
    c = sum(f64(gate[r, :1]) * y[:, unstriped(p)] for r, p in enumerate((pos1, pos2, pos3)))
    return o * c

@@ -1,0 +1,217 @@
+from contextlib import ExitStack
+
+import concourse.mybir as mybir
+from concourse.masks import make_identity
+
+K, T, E, C, H, N, TOP = 1024, 640, 15, 128, 512, 256, 3
+S = E * C
+P = 128
+PASSES = K // 512
+HALVES = N // P
+FLOPS = 2 * K * N * T + 2 * S * (K * H + H * N)
+
+F32 = mybir.dt.float32
+BF16 = mybir.dt.bfloat16
+I32 = mybir.dt.int32
+U32 = mybir.dt.uint32
+U16 = mybir.dt.uint16
+U8 = mybir.dt.uint8
+FP8X4 = mybir.dt.float8_e4m3fn_x4
+FP4X4 = mybir.dt.float4_e2m1fn_x4
+ACT = mybir.ActivationFunctionType
+ALU = mybir.AluOpType
+
+GATHER_GROUPS = [(0, 1), (1, 3), (3, 5), (5, 7), (7, 9), (9, 11), (11, 13), (13, 15)]
+SCALE_GROUPS = [(0, 5), (5, 15)]
+W1_GROUPS = [(0, 1), (1, 3), (3, 5), (5, 7), (7, 9), (9, 11), (11, 13), (13, 15)]
+W2_GROUPS = [(0, 5), (5, 15)]
+W2_LOAD_AFTER = {1: (0, 5), 5: (5, 15)}
+Y_GROUPS = [(0, 2), (2, 4), (4, 6), (6, 8), (8, 10), (10, 12), (12, 14), (14, 15)]
+RELU_ON_VECTOR_FROM = 12
+TOKEN_PIECES = [(0, 320), (320, 640)]
+
+
+def group_of(groups, e):
+    return [g for g in groups if g[0] <= e < g[1]][0]
+
+
+def tile_moe_ogt_relu2_sigmoid_kernel(tc, x_words, x_scales, wg_words, wg_scales, w1_words, w1_scales, w2_words, w2_scales, gate, offs, pos1, pos2, pos3, out):
+    nc = tc.nc
+    with ExitStack() as ctx:
+        keep = ctx.enter_context(tc.tile_pool(name="keep", bufs=1))
+        ring = ctx.enter_context(tc.tile_pool(name="ring", bufs=4))
+        picked = ctx.enter_context(tc.tile_pool(name="picked", bufs=3))
+        ps_pre = ctx.enter_context(tc.psum_pool(name="ps_pre", bufs=3))
+        ps_turn = ctx.enter_context(tc.psum_pool(name="ps_turn", bufs=3))
+        ps_y = ctx.enter_context(tc.psum_pool(name="ps_y", bufs=2))
+
+        def zeroed_plane(name, count, width):
+            plane = keep.tile([P, count, width], U8, name=name, align_bytes=64)
+            nc.vector.memset(plane[:].rearrange("p m w -> p (m w)").bitcast(I32), 0)
+            return plane
+
+        def load_scale_rows(plane, rows, queue, quadrants=range(4)):
+            for q in quadrants:
+                queue.dma_start(out=plane[32 * q : 32 * q + 4].bitcast(I32), in_=rows[4 * q : 4 * q + 4].bitcast(I32))
+            return plane
+
+        def scale_plane(name, rows, width, queue):
+            return load_scale_rows(zeroed_plane(name, rows.shape[1], width), rows, queue)
+
+        slot_list = keep.tile([P, S // 16], U16, name="slot_list")
+        nc.sync.dma_start(slot_list[:], offs)
+
+        xs_rows = x_scales.rearrange("s b t -> b s t")
+        xs = load_scale_rows(zeroed_plane("xs", PASSES, T), xs_rows, nc.sync, range(3))
+        xw = keep.tile([P, PASSES, T], I32, name="xw", align_bytes=64)
+        nc.sync.dma_start(out=xw[:], in_=x_words.rearrange("s p t d -> p s (t d)").bitcast(I32))
+        load_scale_rows(xs, xs_rows, nc.sync, range(3, 4))
+
+        mask = keep.tile([P, P], F32, name="mask")
+        make_identity(nc, mask[:])
+        ident = keep.tile([P, P], F32, name="ident")
+        nc.scalar.activation(ident[:], mask[:], ACT.Square)
+
+        w1s_rows = w1_scales.rearrange("e s b i -> b (e s) i")
+        w2s_rows = w2_scales.rearrange("e s b n -> b (e s) n")
+        w1s, w1, w2 = {}, {}, {}
+
+        def load_w1(g):
+            t = keep.tile([P, (g[1] - g[0]) * PASSES, 2 * H], U8, name="w1_%d" % g[0], align_bytes=64)
+            nc.sync.dma_start(out=t[:].bitcast(I32), in_=w1_words.rearrange("e s p b -> p (e s) b")[:, PASSES * g[0] : PASSES * g[1], :].bitcast(I32))
+            w1[g] = t
+
+        def load_w2(g):
+            t = keep.tile([P, g[1] - g[0], 2 * N], U8, name="w2_%d" % g[0], align_bytes=64)
+            nc.sync.dma_start(out=t[:].bitcast(I32), in_=w2_words.rearrange("e s p b -> p (e s) b")[:, g[0] : g[1], :].bitcast(I32))
+            w2[g] = t
+
+        load_w1(W1_GROUPS[0])
+        w1s[SCALE_GROUPS[0]] = scale_plane("w1s_a", w1s_rows[:, 0 : PASSES * SCALE_GROUPS[0][1], :], H, nc.sync)
+        w2s = scale_plane("w2s", w2s_rows, N, nc.gpsimd)
+        w1s[SCALE_GROUPS[1]] = scale_plane("w1s_b", w1s_rows[:, PASSES * SCALE_GROUPS[1][0] :, :], H, nc.gpsimd)
+        for g in W1_GROUPS[1:]:
+            load_w1(g)
+            if g[0] in W2_LOAD_AFTER:
+                load_w2(W2_LOAD_AFTER[g[0]])
+
+        pos = []
+        for r, src in enumerate((pos1, pos2, pos3)):
+            t = keep.tile([P, T // 16], U16, name="pos%d" % r)
+            nc.sync.dma_start(t[:], src)
+            pos.append(t)
+        gates = keep.tile([P, TOP, T], F32, name="gates")
+        nc.sync.dma_start(out=gates[:], in_=gate.rearrange("r p t -> p r t"))
+        wg = keep.tile([P, PASSES, N], I32, name="wg", align_bytes=64)
+        nc.sync.dma_start(out=wg[:], in_=wg_words.rearrange("s p n d -> p s (n d)").bitcast(I32))
+        wgs = scale_plane("wgs", wg_scales.rearrange("s b n -> b s n"), N, nc.sync)
+
+        xg, sg = {}, {}
+
+        def gather(g):
+            n = (g[1] - g[0]) * C
+            cols = slot_list[:, g[0] * C // 16 : g[1] * C // 16]
+            for s in range(PASSES):
+                sg[g, s] = picked.tile([P, n], U8, name="sg%d" % s, align_bytes=64)
+                nc.vector.tensor_copy(sg[g, s][:], xs[:, s, :].indirect(cols))
+            for s in range(PASSES):
+                xg[g, s] = picked.tile([P, n], U32, name="xg%d" % s, align_bytes=64)
+                nc.vector.tensor_copy(xg[g, s][:], xw[:, s, :].bitcast(U32).indirect(cols))
+
+        y = [keep.tile([P, S], F32, name="y%d" % h) for h in range(HALVES)]
+        pre, relu, turned, hb, hq, hs, ybank = {}, {}, {}, {}, {}, {}, {}
+
+        def first_product(e):
+            g, gw, gs = group_of(GATHER_GROUPS, e), group_of(W1_GROUPS, e), group_of(SCALE_GROUPS, e)
+            if g[0] == e:
+                gather(g)
+            cols = slice((e - g[0]) * C, (e - g[0] + 1) * C)
+            pre[e] = ps_pre.tile([P, H], F32, name="pre")
+            for s in range(PASSES):
+                nc.tensor.matmul_mx(
+                    out=pre[e][:],
+                    lhsT=xg[g, s][:, cols].bitcast(FP8X4),
+                    lhsT_scale=sg[g, s][:, cols],
+                    rhs=w1[gw][:, (e - gw[0]) * PASSES + s, :].bitcast(FP4X4),
+                    rhs_scale=w1s[gs][:, (e - gs[0]) * PASSES + s, :],
+                    start=(s == 0),
+                    stop=(s == PASSES - 1),
+                )
+
+        def relu_and_turn(e):
+            relu[e] = ring.tile([P, 4, P], F32, name="relu")
+            src = pre[e][:].rearrange("u (p d) -> u d p", d=4)
+            if e >= RELU_ON_VECTOR_FROM:
+                nc.vector.tensor_scalar_max(relu[e][:], src, 0.0)
+            else:
+                nc.scalar.activation(relu[e][:], src, ACT.Relu)
+            turned[e] = ps_turn.tile([P, 4, C], F32, name="turned")
+            for d in range(4):
+                nc.tensor.transpose(turned[e][:, d, :], relu[e][:, d, :], ident[:])
+
+        def square_and_quantise(e):
+            hb[e] = ring.tile([P, C, 4], BF16, name="hb", align_bytes=64)
+            nc.scalar.activation(hb[e][:], turned[e][:].rearrange("p d u -> p u d"), ACT.Square)
+            hq[e] = ring.tile([P, C], U32, name="hq", align_bytes=64)
+            hs[e] = ring.tile([P, C], U8, name="hs", align_bytes=64)
+            nc.vector.quantize_mx(out=hq[e][:].bitcast(FP8X4), scales=hs[e][:], in_=hb[e][:].rearrange("p u d -> p (u d)"))
+
+        def second_product(e):
+            g, gw = group_of(Y_GROUPS, e), group_of(W2_GROUPS, e)
+            if g[0] == e:
+                ybank[g] = ps_y.tile([P, HALVES, 2 * C], F32, name="ybank")
+            for h in range(HALVES):
+                nc.tensor.matmul_mx(
+                    out=ybank[g][:, h, (e - g[0]) * C : (e - g[0] + 1) * C],
+                    lhsT=w2[gw][:, e - gw[0], 2 * P * h : 2 * P * (h + 1)].bitcast(FP4X4),
+                    lhsT_scale=w2s[:, e, P * h : P * (h + 1)],
+                    rhs=hq[e][:].bitcast(FP8X4),
+                    rhs_scale=hs[e][:],
+                    start=True,
+                    stop=True,
+                )
+            if e == g[1] - 1:
+                n = (g[1] - g[0]) * C
+                for h in range(HALVES):
+                    nc.scalar.copy(y[h][:, g[0] * C : g[1] * C], ybank[g][:, h, 0:n])
+
+        for step in range(E + 3):
+            if 0 <= step - 3 < E:
+                second_product(step - 3)
+            if 0 <= step - 2 < E:
+                square_and_quantise(step - 2)
+            if 0 <= step - 1 < E:
+                relu_and_turn(step - 1)
+            if step < E:
+                first_product(step)
+
+        o = keep.tile([P, HALVES, T], F32, name="o")
+        for h in range(HALVES):
+            for t0, t1 in ((0, 512), (512, T)):
+                bank = ps_pre.tile([P, H], F32, name="pre")
+                for s in range(PASSES):
+                    nc.tensor.matmul_mx(
+                        out=bank[:, 0 : t1 - t0],
+                        lhsT=wg[:, s, P * h : P * (h + 1)].bitcast(FP8X4),
+                        lhsT_scale=wgs[:, s, P * h : P * (h + 1)],
+                        rhs=xw[:, s, t0:t1].bitcast(FP8X4),
+                        rhs_scale=xs[:, s, t0:t1],
+                        start=(s == 0),
+                        stop=(s == PASSES - 1),
+                    )
+                nc.scalar.activation(o[:, h, t0:t1], bank[:, 0 : t1 - t0], ACT.Sigmoid)
+
+        for h in range(HALVES):
+            for t0, t1 in TOKEN_PIECES:
+                parts = []
+                for r in range(TOP):
+                    a = ring.tile([P, t1 - t0], F32, name="part%d" % r)
+                    nc.vector.tensor_tensor(a[:], y[h][:].indirect(pos[r][:, t0 // 16 : t1 // 16]), gates[:, r, t0:t1], ALU.mult)
+                    parts.append(a)
+                s12 = ring.tile([P, t1 - t0], F32, name="s12")
+                nc.vector.tensor_tensor(s12[:], parts[0][:], parts[1][:], ALU.add)
+                s123 = ring.tile([P, t1 - t0], F32, name="s123")
+                nc.vector.tensor_tensor(s123[:], s12[:], parts[2][:], ALU.add)
+                res = ring.tile([P, t1 - t0], F32, name="res")
+                nc.vector.tensor_tensor(res[:], s123[:], o[:, h, t0:t1], ALU.mult)
+                nc.sync.dma_start(out=out[P * h : P * (h + 1), t0:t1], in_=res[:])

@@ -21,12 +21,12 @@ FP4X4 = mybir.dt.float4_e2m1fn_x4
 ACT = mybir.ActivationFunctionType
 ALU = mybir.AluOpType
 
-GATHER_GROUPS = [(0, 1), (1, 3), (3, 5), (5, 7), (7, 9), (9, 11), (11, 13), (13, 15)]
-SCALE_GROUPS = [(0, 5), (5, 15)]
-W1_GROUPS = [(0, 1), (1, 3), (3, 5), (5, 7), (7, 9), (9, 11), (11, 13), (13, 15)]
-W2_GROUPS = [(0, 5), (5, 15)]
-W2_LOAD_AFTER = {1: (0, 5), 5: (5, 15)}
-Y_GROUPS = [(0, 2), (2, 4), (4, 6), (6, 8), (8, 10), (10, 12), (12, 14), (14, 15)]
+PAIRS = [(e, min(e + 2, E)) for e in range(0, E, 2)]
+SCALE_GROUPS = [(0, 2), (2, 6), (6, 10), (10, 15)]
+W1_GROUPS = [(0, 1), (1, 2)] + PAIRS[1:]
+W2_GROUPS = PAIRS
+Y_GROUPS = PAIRS
+LAG = 2
 RELU_ON_VECTOR_FROM = 12
 TOKEN_PIECES = [(0, 320), (320, 640)]
 
@@ -40,7 +40,8 @@ def tile_moe_ogt_relu2_sigmoid_kernel(tc, x_words, x_scales, wg_words, wg_scales
     with ExitStack() as ctx:
         keep = ctx.enter_context(tc.tile_pool(name="keep", bufs=1))
         ring = ctx.enter_context(tc.tile_pool(name="ring", bufs=4))
-        picked = ctx.enter_context(tc.tile_pool(name="picked", bufs=3))
+        picked = ctx.enter_context(tc.tile_pool(name="picked", bufs=2))
+        coded = ctx.enter_context(tc.tile_pool(name="coded", bufs=2 * LAG + 2))
         ps_pre = ctx.enter_context(tc.psum_pool(name="ps_pre", bufs=3))
         ps_turn = ctx.enter_context(tc.psum_pool(name="ps_turn", bufs=3))
         ps_y = ctx.enter_context(tc.psum_pool(name="ps_y", bufs=2))
@@ -51,8 +52,8 @@ def tile_moe_ogt_relu2_sigmoid_kernel(tc, x_words, x_scales, wg_words, wg_scales
             return plane
 
         def load_scale_rows(plane, rows, queue, quadrants=range(4)):
-            for q in quadrants:
-                queue.dma_start(out=plane[32 * q : 32 * q + 4].bitcast(I32), in_=rows[4 * q : 4 * q + 4].bitcast(I32))
+            for r in quadrants:
+                queue.dma_start(out=plane[r:P:32].bitcast(I32), in_=rows[r:16:4].bitcast(I32))
             return plane
 
         def scale_plane(name, rows, width, queue):
@@ -86,14 +87,19 @@ def tile_moe_ogt_relu2_sigmoid_kernel(tc, x_words, x_scales, wg_words, wg_scales
             nc.sync.dma_start(out=t[:].bitcast(I32), in_=w2_words.rearrange("e s p b -> p (e s) b")[:, g[0] : g[1], :].bitcast(I32))
             w2[g] = t
 
-        load_w1(W1_GROUPS[0])
-        w1s[SCALE_GROUPS[0]] = scale_plane("w1s_a", w1s_rows[:, 0 : PASSES * SCALE_GROUPS[0][1], :], H, nc.sync)
-        w2s = scale_plane("w2s", w2s_rows, N, nc.gpsimd)
-        w1s[SCALE_GROUPS[1]] = scale_plane("w1s_b", w1s_rows[:, PASSES * SCALE_GROUPS[1][0] :, :], H, nc.gpsimd)
-        for g in W1_GROUPS[1:]:
-            load_w1(g)
-            if g[0] in W2_LOAD_AFTER:
-                load_w2(W2_LOAD_AFTER[g[0]])
+        for j, pair in enumerate(PAIRS):
+            for g in SCALE_GROUPS:
+                if g[0] == pair[0]:
+                    w1s[g] = scale_plane("w1s_%d" % g[0], w1s_rows[:, PASSES * g[0] : PASSES * g[1], :], H, nc.sync)
+            for g in W1_GROUPS:
+                if pair[0] <= g[0] < pair[1]:
+                    load_w1(g)
+            if j == LAG:
+                w2s = scale_plane("w2s", w2s_rows, N, nc.sync)
+            if j >= LAG:
+                load_w2(PAIRS[j - LAG])
+        for pair in PAIRS[-LAG:]:
+            load_w2(pair)
 
         pos = []
         for r, src in enumerate((pos1, pos2, pos3)):
@@ -110,19 +116,22 @@ def tile_moe_ogt_relu2_sigmoid_kernel(tc, x_words, x_scales, wg_words, wg_scales
 
         def gather(g):
             n = (g[1] - g[0]) * C
-            cols = slot_list[:, g[0] * C // 16 : g[1] * C // 16]
             for s in range(PASSES):
                 sg[g, s] = picked.tile([P, n], U8, name="sg%d" % s, align_bytes=64)
-                nc.vector.tensor_copy(sg[g, s][:], xs[:, s, :].indirect(cols))
-            for s in range(PASSES):
                 xg[g, s] = picked.tile([P, n], U32, name="xg%d" % s, align_bytes=64)
-                nc.vector.tensor_copy(xg[g, s][:], xw[:, s, :].bitcast(U32).indirect(cols))
+            step = C if g[0] == 0 else n
+            for c0 in range(0, n, step):
+                cols = slot_list[:, (g[0] * C + c0) // 16 : (g[0] * C + c0 + step) // 16]
+                for s in range(PASSES):
+                    nc.vector.tensor_copy(xg[g, s][:, c0 : c0 + step], xw[:, s, :].bitcast(U32).indirect(cols))
+                for s in range(PASSES):
+                    nc.vector.tensor_copy(sg[g, s][:, c0 : c0 + step], xs[:, s, :].indirect(cols))
 
         y = [keep.tile([P, S], F32, name="y%d" % h) for h in range(HALVES)]
         pre, relu, turned, hb, hq, hs, ybank = {}, {}, {}, {}, {}, {}, {}
 
         def first_product(e):
-            g, gw, gs = group_of(GATHER_GROUPS, e), group_of(W1_GROUPS, e), group_of(SCALE_GROUPS, e)
+            g, gw, gs = group_of(PAIRS, e), group_of(W1_GROUPS, e), group_of(SCALE_GROUPS, e)
             if g[0] == e:
                 gather(g)
             cols = slice((e - g[0]) * C, (e - g[0] + 1) * C)
@@ -152,8 +161,8 @@ def tile_moe_ogt_relu2_sigmoid_kernel(tc, x_words, x_scales, wg_words, wg_scales
         def square_and_quantise(e):
             hb[e] = ring.tile([P, C, 4], BF16, name="hb", align_bytes=64)
             nc.scalar.activation(hb[e][:], turned[e][:].rearrange("p d u -> p u d"), ACT.Square)
-            hq[e] = ring.tile([P, C], U32, name="hq", align_bytes=64)
-            hs[e] = ring.tile([P, C], U8, name="hs", align_bytes=64)
+            hq[e] = coded.tile([P, C], U32, name="hq", align_bytes=64)
+            hs[e] = coded.tile([P, C], U8, name="hs", align_bytes=64)
             nc.vector.quantize_mx(out=hq[e][:].bitcast(FP8X4), scales=hs[e][:], in_=hb[e][:].rearrange("p u d -> p (u d)"))
 
         def second_product(e):
@@ -173,17 +182,22 @@ def tile_moe_ogt_relu2_sigmoid_kernel(tc, x_words, x_scales, wg_words, wg_scales
             if e == g[1] - 1:
                 n = (g[1] - g[0]) * C
                 for h in range(HALVES):
-                    nc.scalar.copy(y[h][:, g[0] * C : g[1] * C], ybank[g][:, h, 0:n])
+                    if g == PAIRS[-1]:
+                        nc.vector.tensor_copy(y[h][:, g[0] * C : g[1] * C], ybank[g][:, h, 0:n])
+                    else:
+                        nc.scalar.copy(y[h][:, g[0] * C : g[1] * C], ybank[g][:, h, 0:n])
 
-        for step in range(E + 3):
-            if 0 <= step - 3 < E:
-                second_product(step - 3)
-            if 0 <= step - 2 < E:
-                square_and_quantise(step - 2)
-            if 0 <= step - 1 < E:
-                relu_and_turn(step - 1)
-            if step < E:
-                first_product(step)
+        for j in range(len(PAIRS) + LAG):
+            now = range(*PAIRS[j]) if j < len(PAIRS) else ()
+            for e in now:
+                first_product(e)
+            for e in now:
+                relu_and_turn(e)
+            if j >= LAG:
+                for e in range(*PAIRS[j - LAG]):
+                    second_product(e)
+            for e in now:
+                square_and_quantise(e)
 
         o = keep.tile([P, HALVES, T], F32, name="o")
         for h in range(HALVES):

@@ -21,14 +21,13 @@ FP4X4 = mybir.dt.float4_e2m1fn_x4
 ACT = mybir.ActivationFunctionType
 ALU = mybir.AluOpType
 
-PAIRS = [(e, min(e + 2, E)) for e in range(0, E, 2)]
-SCALE_GROUPS = [(0, 2), (2, 6), (6, 10), (10, 15)]
-W1_GROUPS = [(0, 1), (1, 2)] + PAIRS[1:]
-W2_GROUPS = PAIRS
-Y_GROUPS = PAIRS
+GROUPS = [(0, 2), (2, 4), (4, 7), (7, 10), (10, 13), (13, 14), (14, 15)]
+SCALE_GROUPS = [(0, 2), (2, 4), (4, 10), (10, 15)]
+Y_GROUPS = GROUPS
 LAG = 2
-RELU_ON_VECTOR_FROM = 12
-TOKEN_PIECES = [(0, 320), (320, 640)]
+RELU_ON_VECTOR = (13, 14)
+COPY_ON_VECTOR = ((2, 0), (7, 0), (14, 0), (14, 1))
+LAST_PIECES = [[(0, T)], [(0, 320), (320, T)]]
 
 
 def group_of(groups, e):
@@ -41,32 +40,27 @@ def tile_moe_ogt_relu2_sigmoid_kernel(tc, x_words, x_scales, wg_words, wg_scales
         keep = ctx.enter_context(tc.tile_pool(name="keep", bufs=1))
         ring = ctx.enter_context(tc.tile_pool(name="ring", bufs=4))
         picked = ctx.enter_context(tc.tile_pool(name="picked", bufs=2))
-        coded = ctx.enter_context(tc.tile_pool(name="coded", bufs=2 * LAG + 2))
+        coded = ctx.enter_context(tc.tile_pool(name="coded", bufs=LAG + 1))
         ps_pre = ctx.enter_context(tc.psum_pool(name="ps_pre", bufs=3))
         ps_turn = ctx.enter_context(tc.psum_pool(name="ps_turn", bufs=3))
-        ps_y = ctx.enter_context(tc.psum_pool(name="ps_y", bufs=2))
+        ps_y = ctx.enter_context(tc.psum_pool(name="ps_y", bufs=1))
 
-        def zeroed_plane(name, count, width):
-            plane = keep.tile([P, count, width], U8, name=name, align_bytes=64)
-            nc.vector.memset(plane[:].rearrange("p m w -> p (m w)").bitcast(I32), 0)
-            return plane
+        def zero(engine, plane):
+            engine.memset(plane.rearrange("p m w -> p (m w)").bitcast(I32), 0)
 
-        def load_scale_rows(plane, rows, queue, quadrants=range(4)):
-            for r in quadrants:
-                queue.dma_start(out=plane[r:P:32].bitcast(I32), in_=rows[r:16:4].bitcast(I32))
-            return plane
-
-        def scale_plane(name, rows, width, queue):
-            return load_scale_rows(zeroed_plane(name, rows.shape[1], width), rows, queue)
+        def load_scale_rows(plane, rows):
+            for r in range(4):
+                nc.sync.dma_start(out=plane[r:P:32].bitcast(I32), in_=rows[r:16:4].bitcast(I32))
 
         slot_list = keep.tile([P, S // 16], U16, name="slot_list")
         nc.sync.dma_start(slot_list[:], offs)
 
         xs_rows = x_scales.rearrange("s b t -> b s t")
-        xs = load_scale_rows(zeroed_plane("xs", PASSES, T), xs_rows, nc.sync, range(3))
+        xs = keep.tile([P, PASSES, T], U8, name="xs", align_bytes=64)
+        zero(nc.vector, xs[:])
+        load_scale_rows(xs, xs_rows)
         xw = keep.tile([P, PASSES, T], I32, name="xw", align_bytes=64)
         nc.sync.dma_start(out=xw[:], in_=x_words.rearrange("s p t d -> p s (t d)").bitcast(I32))
-        load_scale_rows(xs, xs_rows, nc.sync, range(3, 4))
 
         mask = keep.tile([P, P], F32, name="mask")
         make_identity(nc, mask[:])
@@ -75,7 +69,16 @@ def tile_moe_ogt_relu2_sigmoid_kernel(tc, x_words, x_scales, wg_words, wg_scales
 
         w1s_rows = w1_scales.rearrange("e s b i -> b (e s) i")
         w2s_rows = w2_scales.rearrange("e s b n -> b (e s) n")
-        w1s, w1, w2 = {}, {}, {}
+        w1, w2 = {}, {}
+        w1s = {g: keep.tile([P, PASSES * (g[1] - g[0]), H], U8, name="w1s_%d" % g[0], align_bytes=64) for g in SCALE_GROUPS}
+        w2s = keep.tile([P, E, N], U8, name="w2s", align_bytes=64)
+        wgs = keep.tile([P, PASSES, N], U8, name="wgs", align_bytes=64)
+        for g in SCALE_GROUPS[:2]:
+            zero(nc.vector, w1s[g][:])
+        zero(nc.gpsimd, w2s[:])
+        for g in SCALE_GROUPS[2:]:
+            zero(nc.gpsimd, w1s[g][:])
+        zero(nc.gpsimd, wgs[:])
 
         def load_w1(g):
             t = keep.tile([P, (g[1] - g[0]) * PASSES, 2 * H], U8, name="w1_%d" % g[0], align_bytes=64)
@@ -87,51 +90,34 @@ def tile_moe_ogt_relu2_sigmoid_kernel(tc, x_words, x_scales, wg_words, wg_scales
             nc.sync.dma_start(out=t[:].bitcast(I32), in_=w2_words.rearrange("e s p b -> p (e s) b")[:, g[0] : g[1], :].bitcast(I32))
             w2[g] = t
 
-        for j, pair in enumerate(PAIRS):
-            for g in SCALE_GROUPS:
-                if g[0] == pair[0]:
-                    w1s[g] = scale_plane("w1s_%d" % g[0], w1s_rows[:, PASSES * g[0] : PASSES * g[1], :], H, nc.sync)
-            for g in W1_GROUPS:
-                if pair[0] <= g[0] < pair[1]:
-                    load_w1(g)
+        for j in range(len(GROUPS) + LAG):
+            if j < len(GROUPS):
+                for g in SCALE_GROUPS:
+                    if g[0] == GROUPS[j][0]:
+                        load_scale_rows(w1s[g], w1s_rows[:, PASSES * g[0] : PASSES * g[1], :])
+                load_w1(GROUPS[j])
             if j == LAG:
-                w2s = scale_plane("w2s", w2s_rows, N, nc.sync)
+                load_scale_rows(w2s, w2s_rows)
             if j >= LAG:
-                load_w2(PAIRS[j - LAG])
-        for pair in PAIRS[-LAG:]:
-            load_w2(pair)
-
-        pos = []
-        for r, src in enumerate((pos1, pos2, pos3)):
-            t = keep.tile([P, T // 16], U16, name="pos%d" % r)
-            nc.sync.dma_start(t[:], src)
-            pos.append(t)
-        gates = keep.tile([P, TOP, T], F32, name="gates")
-        nc.sync.dma_start(out=gates[:], in_=gate.rearrange("r p t -> p r t"))
-        wg = keep.tile([P, PASSES, N], I32, name="wg", align_bytes=64)
-        nc.sync.dma_start(out=wg[:], in_=wg_words.rearrange("s p n d -> p s (n d)").bitcast(I32))
-        wgs = scale_plane("wgs", wg_scales.rearrange("s b n -> b s n"), N, nc.sync)
+                load_w2(GROUPS[j - LAG])
 
         xg, sg = {}, {}
 
         def gather(g):
             n = (g[1] - g[0]) * C
+            cols = slot_list[:, g[0] * C // 16 : g[1] * C // 16]
             for s in range(PASSES):
                 sg[g, s] = picked.tile([P, n], U8, name="sg%d" % s, align_bytes=64)
+                nc.vector.tensor_copy(sg[g, s][:], xs[:, s, :].indirect(cols))
+            for s in range(PASSES):
                 xg[g, s] = picked.tile([P, n], U32, name="xg%d" % s, align_bytes=64)
-            step = C if g[0] == 0 else n
-            for c0 in range(0, n, step):
-                cols = slot_list[:, (g[0] * C + c0) // 16 : (g[0] * C + c0 + step) // 16]
-                for s in range(PASSES):
-                    nc.vector.tensor_copy(xg[g, s][:, c0 : c0 + step], xw[:, s, :].bitcast(U32).indirect(cols))
-                for s in range(PASSES):
-                    nc.vector.tensor_copy(sg[g, s][:, c0 : c0 + step], xs[:, s, :].indirect(cols))
+                nc.vector.tensor_copy(xg[g, s][:], xw[:, s, :].bitcast(U32).indirect(cols))
 
         y = [keep.tile([P, S], F32, name="y%d" % h) for h in range(HALVES)]
-        pre, relu, turned, hb, hq, hs, ybank = {}, {}, {}, {}, {}, {}, {}
+        pre, relu, turned, hq, hs, ybank = {}, {}, {}, {}, {}, {}
 
         def first_product(e):
-            g, gw, gs = group_of(PAIRS, e), group_of(W1_GROUPS, e), group_of(SCALE_GROUPS, e)
+            g, gs = group_of(GROUPS, e), group_of(SCALE_GROUPS, e)
             if g[0] == e:
                 gather(g)
             cols = slice((e - g[0]) * C, (e - g[0] + 1) * C)
@@ -141,7 +127,7 @@ def tile_moe_ogt_relu2_sigmoid_kernel(tc, x_words, x_scales, wg_words, wg_scales
                     out=pre[e][:],
                     lhsT=xg[g, s][:, cols].bitcast(FP8X4),
                     lhsT_scale=sg[g, s][:, cols],
-                    rhs=w1[gw][:, (e - gw[0]) * PASSES + s, :].bitcast(FP4X4),
+                    rhs=w1[g][:, (e - g[0]) * PASSES + s, :].bitcast(FP4X4),
                     rhs_scale=w1s[gs][:, (e - gs[0]) * PASSES + s, :],
                     start=(s == 0),
                     stop=(s == PASSES - 1),
@@ -150,7 +136,7 @@ def tile_moe_ogt_relu2_sigmoid_kernel(tc, x_words, x_scales, wg_words, wg_scales
         def relu_and_turn(e):
             relu[e] = ring.tile([P, 4, P], F32, name="relu")
             src = pre[e][:].rearrange("u (p d) -> u d p", d=4)
-            if e >= RELU_ON_VECTOR_FROM:
+            if e in RELU_ON_VECTOR:
                 nc.vector.tensor_scalar_max(relu[e][:], src, 0.0)
             else:
                 nc.scalar.activation(relu[e][:], src, ACT.Relu)
@@ -158,46 +144,64 @@ def tile_moe_ogt_relu2_sigmoid_kernel(tc, x_words, x_scales, wg_words, wg_scales
             for d in range(4):
                 nc.tensor.transpose(turned[e][:, d, :], relu[e][:, d, :], ident[:])
 
-        def square_and_quantise(e):
-            hb[e] = ring.tile([P, C, 4], BF16, name="hb", align_bytes=64)
-            nc.scalar.activation(hb[e][:], turned[e][:].rearrange("p d u -> p u d"), ACT.Square)
-            hq[e] = coded.tile([P, C], U32, name="hq", align_bytes=64)
-            hs[e] = coded.tile([P, C], U8, name="hs", align_bytes=64)
-            nc.vector.quantize_mx(out=hq[e][:].bitcast(FP8X4), scales=hs[e][:], in_=hb[e][:].rearrange("p u d -> p (u d)"))
+        def square_and_quantise(g):
+            n = (g[1] - g[0]) * C
+            hb = ring.tile([P, n, 4], BF16, name="hb", align_bytes=64)
+            for e in range(*g):
+                nc.scalar.activation(hb[:, (e - g[0]) * C : (e - g[0] + 1) * C, :], turned[e][:].rearrange("p d u -> p u d"), ACT.Square)
+            hq[g] = coded.tile([P, n], U32, name="hq", align_bytes=64)
+            hs[g] = coded.tile([P, n], U8, name="hs", align_bytes=64)
+            for u0 in range(0, n, 2 * C):
+                u1 = min(u0 + 2 * C, n)
+                nc.vector.quantize_mx(out=hq[g][:, u0:u1].bitcast(FP8X4), scales=hs[g][:, u0:u1], in_=hb[:, u0:u1, :].rearrange("p u d -> p (u d)"))
 
         def second_product(e):
-            g, gw = group_of(Y_GROUPS, e), group_of(W2_GROUPS, e)
-            if g[0] == e:
-                ybank[g] = ps_y.tile([P, HALVES, 2 * C], F32, name="ybank")
+            g, gy = group_of(GROUPS, e), group_of(Y_GROUPS, e)
+            n = (gy[1] - gy[0]) * C
+            if gy == Y_GROUPS[-1]:
+                bank = ps_pre.tile([P, HALVES, n], F32, name="pre")
+                ybank[gy] = [bank[:, h, :] for h in range(HALVES)]
+            elif gy[0] == e:
+                ybank[gy] = [ps_y.tile([P, n], F32, name="ybank%d" % h)[:] for h in range(HALVES)]
             for h in range(HALVES):
                 nc.tensor.matmul_mx(
-                    out=ybank[g][:, h, (e - g[0]) * C : (e - g[0] + 1) * C],
-                    lhsT=w2[gw][:, e - gw[0], 2 * P * h : 2 * P * (h + 1)].bitcast(FP4X4),
+                    out=ybank[gy][h][:, (e - gy[0]) * C : (e - gy[0] + 1) * C],
+                    lhsT=w2[g][:, e - g[0], 2 * P * h : 2 * P * (h + 1)].bitcast(FP4X4),
                     lhsT_scale=w2s[:, e, P * h : P * (h + 1)],
-                    rhs=hq[e][:].bitcast(FP8X4),
-                    rhs_scale=hs[e][:],
+                    rhs=hq[g][:, (e - g[0]) * C : (e - g[0] + 1) * C].bitcast(FP8X4),
+                    rhs_scale=hs[g][:, (e - g[0]) * C : (e - g[0] + 1) * C],
                     start=True,
                     stop=True,
                 )
-            if e == g[1] - 1:
-                n = (g[1] - g[0]) * C
+            if e == gy[1] - 1:
                 for h in range(HALVES):
-                    if g == PAIRS[-1]:
-                        nc.vector.tensor_copy(y[h][:, g[0] * C : g[1] * C], ybank[g][:, h, 0:n])
+                    if (gy[0], h) in COPY_ON_VECTOR:
+                        nc.vector.tensor_copy(y[h][:, gy[0] * C : gy[1] * C], ybank[gy][h])
                     else:
-                        nc.scalar.copy(y[h][:, g[0] * C : g[1] * C], ybank[g][:, h, 0:n])
+                        nc.scalar.copy(y[h][:, gy[0] * C : gy[1] * C], ybank[gy][h])
 
-        for j in range(len(PAIRS) + LAG):
-            now = range(*PAIRS[j]) if j < len(PAIRS) else ()
+        for j in range(len(GROUPS) + LAG):
+            now = range(*GROUPS[j]) if j < len(GROUPS) else ()
             for e in now:
                 first_product(e)
             for e in now:
                 relu_and_turn(e)
             if j >= LAG:
-                for e in range(*PAIRS[j - LAG]):
+                for e in range(*GROUPS[j - LAG]):
                     second_product(e)
-            for e in now:
-                square_and_quantise(e)
+            if j < len(GROUPS):
+                square_and_quantise(GROUPS[j])
+
+        pos = []
+        for r, src in enumerate((pos1, pos2, pos3)):
+            t = keep.tile([P, T // 16], U16, name="pos%d" % r)
+            nc.sync.dma_start(t[:], src)
+            pos.append(t)
+        wg = keep.tile([P, PASSES, N], I32, name="wg", align_bytes=64)
+        nc.sync.dma_start(out=wg[:], in_=wg_words.rearrange("s p n d -> p s (n d)").bitcast(I32))
+        load_scale_rows(wgs, wg_scales.rearrange("s b n -> b s n"))
+        gates = keep.tile([P, TOP, T], F32, name="gates")
+        nc.sync.dma_start(out=gates[:], in_=gate.rearrange("r p t -> p r t"))
 
         o = keep.tile([P, HALVES, T], F32, name="o")
         for h in range(HALVES):
@@ -215,17 +219,34 @@ def tile_moe_ogt_relu2_sigmoid_kernel(tc, x_words, x_scales, wg_words, wg_scales
                     )
                 nc.scalar.activation(o[:, h, t0:t1], bank[:, 0 : t1 - t0], ACT.Sigmoid)
 
-        for h in range(HALVES):
-            for t0, t1 in TOKEN_PIECES:
-                parts = []
+        def weighted(h, r):
+            a = keep.tile([P, T], F32, name="part%d_%d" % (h, r))
+            nc.vector.tensor_tensor(a[:], y[h][:].indirect(pos[r][:]), gates[:, r, :], ALU.mult)
+            return a
+
+        def finish(h, t0, t1, total):
+            res = ring.tile([P, t1 - t0], F32, name="res")
+            nc.vector.tensor_tensor(res[:], total, o[:, h, t0:t1], ALU.mult)
+            nc.sync.dma_start(out=out[P * h : P * (h + 1), t0:t1], in_=res[:])
+
+        parts = [weighted(0, r) for r in range(TOP)]
+        for t0, t1 in ((0, 384), (384, T)):
+            blocks = (t1 - t0) // P
+            acc = ps_turn.tile([P, blocks, P], F32, name="turned")
+            for b in range(blocks):
                 for r in range(TOP):
-                    a = ring.tile([P, t1 - t0], F32, name="part%d" % r)
-                    nc.vector.tensor_tensor(a[:], y[h][:].indirect(pos[r][:, t0 // 16 : t1 // 16]), gates[:, r, t0:t1], ALU.mult)
-                    parts.append(a)
-                s12 = ring.tile([P, t1 - t0], F32, name="s12")
-                nc.vector.tensor_tensor(s12[:], parts[0][:], parts[1][:], ALU.add)
-                s123 = ring.tile([P, t1 - t0], F32, name="s123")
-                nc.vector.tensor_tensor(s123[:], s12[:], parts[2][:], ALU.add)
-                res = ring.tile([P, t1 - t0], F32, name="res")
-                nc.vector.tensor_tensor(res[:], s123[:], o[:, h, t0:t1], ALU.mult)
-                nc.sync.dma_start(out=out[P * h : P * (h + 1), t0:t1], in_=res[:])
+                    nc.tensor.matmul(acc[:, b, :], lhsT=parts[r][:, t0 + P * b : t0 + P * (b + 1)], rhs=ident[:], is_transpose=True, start=(r == 0), stop=(r == TOP - 1))
+            summed = ring.tile([P, blocks, P], F32, name="summed")
+            nc.scalar.copy(summed[:], acc[:])
+            back = ps_turn.tile([P, blocks, P], F32, name="turned")
+            for b in range(blocks):
+                nc.tensor.transpose(back[:, b, :], summed[:, b, :], ident[:])
+            finish(0, t0, t1, back[:].rearrange("p b t -> p (b t)"))
+
+        parts = [weighted(1, r) for r in range(TOP)]
+        two = keep.tile([P, T], F32, name="two")
+        nc.vector.tensor_tensor(two[:], parts[0][:], parts[1][:], ALU.add)
+        for t0, t1 in ((0, 320), (320, T)):
+            three = ring.tile([P, t1 - t0], F32, name="three")
+            nc.vector.tensor_tensor(three[:], two[:, t0:t1], parts[2][:, t0:t1], ALU.add)
+            finish(1, t0, t1, three[:])

@@ -21,13 +21,14 @@ FP4X4 = mybir.dt.float4_e2m1fn_x4
 ACT = mybir.ActivationFunctionType
 ALU = mybir.AluOpType
 
-GROUPS = [(0, 2), (2, 4), (4, 7), (7, 10), (10, 13), (13, 14), (14, 15)]
-SCALE_GROUPS = [(0, 2), (2, 4), (4, 10), (10, 15)]
+GROUPS = [(0, 2), (2, 5), (5, 8), (8, 10), (10, 12), (12, 14), (14, 15)]
+SCALE_GROUPS = [(0, 4), (4, 8), (8, 12), (12, 15)]
 Y_GROUPS = GROUPS
-LAG = 2
+SECOND_RUN = 3
+LISTS_AT = 1
+SECOND_AT = [3, 3, 3, 6, 6, 7, 8]
 RELU_ON_VECTOR = (13, 14)
-COPY_ON_VECTOR = ((2, 0), (7, 0), (14, 0), (14, 1))
-LAST_PIECES = [[(0, T)], [(0, 320), (320, T)]]
+COPY_ON_VECTOR = ((5, 0), (8, 1), (10, 0), (14, 0), (14, 1))
 
 
 def group_of(groups, e):
@@ -40,7 +41,8 @@ def tile_moe_ogt_relu2_sigmoid_kernel(tc, x_words, x_scales, wg_words, wg_scales
         keep = ctx.enter_context(tc.tile_pool(name="keep", bufs=1))
         ring = ctx.enter_context(tc.tile_pool(name="ring", bufs=4))
         picked = ctx.enter_context(tc.tile_pool(name="picked", bufs=2))
-        coded = ctx.enter_context(tc.tile_pool(name="coded", bufs=LAG + 1))
+        picked_s = ctx.enter_context(tc.tile_pool(name="picked_s", bufs=2))
+        coded = ctx.enter_context(tc.tile_pool(name="coded", bufs=4))
         ps_pre = ctx.enter_context(tc.psum_pool(name="ps_pre", bufs=3))
         ps_turn = ctx.enter_context(tc.psum_pool(name="ps_turn", bufs=3))
         ps_y = ctx.enter_context(tc.psum_pool(name="ps_y", bufs=1))
@@ -75,10 +77,10 @@ def tile_moe_ogt_relu2_sigmoid_kernel(tc, x_words, x_scales, wg_words, wg_scales
         wgs = keep.tile([P, PASSES, N], U8, name="wgs", align_bytes=64)
         for g in SCALE_GROUPS[:2]:
             zero(nc.vector, w1s[g][:])
-        zero(nc.gpsimd, w2s[:])
+        zero(nc.vector, w2s[:])
         for g in SCALE_GROUPS[2:]:
-            zero(nc.gpsimd, w1s[g][:])
-        zero(nc.gpsimd, wgs[:])
+            zero(nc.vector, w1s[g][:])
+        zero(nc.vector, wgs[:])
 
         def load_w1(g):
             t = keep.tile([P, (g[1] - g[0]) * PASSES, 2 * H], U8, name="w1_%d" % g[0], align_bytes=64)
@@ -90,16 +92,23 @@ def tile_moe_ogt_relu2_sigmoid_kernel(tc, x_words, x_scales, wg_words, wg_scales
             nc.sync.dma_start(out=t[:].bitcast(I32), in_=w2_words.rearrange("e s p b -> p (e s) b")[:, g[0] : g[1], :].bitcast(I32))
             w2[g] = t
 
-        for j in range(len(GROUPS) + LAG):
-            if j < len(GROUPS):
-                for g in SCALE_GROUPS:
-                    if g[0] == GROUPS[j][0]:
-                        load_scale_rows(w1s[g], w1s_rows[:, PASSES * g[0] : PASSES * g[1], :])
-                load_w1(GROUPS[j])
-            if j == LAG:
+        pos = []
+        for j in range(SECOND_AT[-1] + 1):
+            if j == SECOND_RUN:
                 load_scale_rows(w2s, w2s_rows)
-            if j >= LAG:
-                load_w2(GROUPS[j - LAG])
+            if j in (0, SECOND_RUN):
+                for g in SCALE_GROUPS[:2] if j == 0 else SCALE_GROUPS[2:]:
+                    load_scale_rows(w1s[g], w1s_rows[:, PASSES * g[0] : PASSES * g[1], :])
+            if j == LISTS_AT:
+                for r, src in enumerate((pos1, pos2, pos3)):
+                    t = keep.tile([P, T // 16], U16, name="pos%d" % r)
+                    nc.sync.dma_start(t[:], src)
+                    pos.append(t)
+            if j < len(GROUPS):
+                load_w1(GROUPS[j])
+            for g, at in zip(GROUPS, SECOND_AT):
+                if at == j:
+                    load_w2(g)
 
         xg, sg = {}, {}
 
@@ -107,7 +116,7 @@ def tile_moe_ogt_relu2_sigmoid_kernel(tc, x_words, x_scales, wg_words, wg_scales
             n = (g[1] - g[0]) * C
             cols = slot_list[:, g[0] * C // 16 : g[1] * C // 16]
             for s in range(PASSES):
-                sg[g, s] = picked.tile([P, n], U8, name="sg%d" % s, align_bytes=64)
+                sg[g, s] = picked_s.tile([P, n], U8, name="sg%d" % s, align_bytes=64)
                 nc.vector.tensor_copy(sg[g, s][:], xs[:, s, :].indirect(cols))
             for s in range(PASSES):
                 xg[g, s] = picked.tile([P, n], U32, name="xg%d" % s, align_bytes=64)
@@ -180,28 +189,25 @@ def tile_moe_ogt_relu2_sigmoid_kernel(tc, x_words, x_scales, wg_words, wg_scales
                     else:
                         nc.scalar.copy(y[h][:, gy[0] * C : gy[1] * C], ybank[gy][h])
 
-        for j in range(len(GROUPS) + LAG):
+        for j in range(SECOND_AT[-1] + 1):
             now = range(*GROUPS[j]) if j < len(GROUPS) else ()
             for e in now:
                 first_product(e)
             for e in now:
                 relu_and_turn(e)
-            if j >= LAG:
-                for e in range(*GROUPS[j - LAG]):
-                    second_product(e)
+            for g, at in zip(GROUPS, SECOND_AT):
+                if at == j:
+                    for e in range(*g):
+                        second_product(e)
             if j < len(GROUPS):
                 square_and_quantise(GROUPS[j])
 
-        pos = []
-        for r, src in enumerate((pos1, pos2, pos3)):
-            t = keep.tile([P, T // 16], U16, name="pos%d" % r)
-            nc.sync.dma_start(t[:], src)
-            pos.append(t)
+        gates = keep.tile([P, TOP, T], F32, name="gates")
+        for r in range(TOP):
+            nc.sync.dma_start(out=gates[:, r, :], in_=gate[r])
         wg = keep.tile([P, PASSES, N], I32, name="wg", align_bytes=64)
         nc.sync.dma_start(out=wg[:], in_=wg_words.rearrange("s p n d -> p s (n d)").bitcast(I32))
         load_scale_rows(wgs, wg_scales.rearrange("s b n -> b s n"))
-        gates = keep.tile([P, TOP, T], F32, name="gates")
-        nc.sync.dma_start(out=gates[:], in_=gate.rearrange("r p t -> p r t"))
 
         o = keep.tile([P, HALVES, T], F32, name="o")
         for h in range(HALVES):

@@ -21,14 +21,19 @@ FP4X4 = mybir.dt.float4_e2m1fn_x4
 ACT = mybir.ActivationFunctionType
 ALU = mybir.AluOpType
 
-GROUPS = [(0, 2), (2, 5), (5, 8), (8, 10), (10, 12), (12, 14), (14, 15)]
-SCALE_GROUPS = [(0, 4), (4, 8), (8, 12), (12, 15)]
-Y_GROUPS = GROUPS
-SECOND_RUN = 3
-LISTS_AT = 1
-SECOND_AT = [3, 3, 3, 6, 6, 7, 8]
-RELU_ON_VECTOR = (13, 14)
-COPY_ON_VECTOR = ((5, 0), (8, 1), (10, 0), (14, 0), (14, 1))
+PLAIN = [(0, 2), (2, 5), (5, 8), (8, 11), (11, 13), (13, 15)]
+PACKED = []
+WORD_GROUPS = [(0, 2), (2, 5), (5, 8), (8, 11), (11, 13), (13, 15)]
+W1_GROUPS = [(0, 2), (2, 5), (5, 8), (8, 11), (11, 13), (13, 15)]
+SCALE_GROUPS = [(0, 2), (2, 5), (5, 8), (8, 11), (11, 13), (13, 15)]
+PAIRS = [(e, e + 1) for e in range(E)]
+PRE_W = 1
+Y_GROUPS = [(0, 4), (4, 8), (8, 12), (12, 14), (14, 15)]
+W2_GROUPS = [(0, 8), (8, 15)]
+RELU_ON_VECTOR_FROM = 15
+SPARE = 16
+SPLIT = 384
+Y_BOTH = 0
 
 
 def group_of(groups, e):
@@ -37,50 +42,52 @@ def group_of(groups, e):
 
 def tile_moe_ogt_relu2_sigmoid_kernel(tc, x_words, x_scales, wg_words, wg_scales, w1_words, w1_scales, w2_words, w2_scales, gate, offs, pos1, pos2, pos3, out):
     nc = tc.nc
+    LATE = nc.gpsimd
     with ExitStack() as ctx:
         keep = ctx.enter_context(tc.tile_pool(name="keep", bufs=1))
         ring = ctx.enter_context(tc.tile_pool(name="ring", bufs=4))
-        picked = ctx.enter_context(tc.tile_pool(name="picked", bufs=2))
-        picked_s = ctx.enter_context(tc.tile_pool(name="picked_s", bufs=2))
-        coded = ctx.enter_context(tc.tile_pool(name="coded", bufs=4))
         ps_pre = ctx.enter_context(tc.psum_pool(name="ps_pre", bufs=3))
-        ps_turn = ctx.enter_context(tc.psum_pool(name="ps_turn", bufs=3))
+        ps_turn = ctx.enter_context(tc.psum_pool(name="ps_turn", bufs=4))
         ps_y = ctx.enter_context(tc.psum_pool(name="ps_y", bufs=1))
 
         def zero(engine, plane):
-            engine.memset(plane.rearrange("p m w -> p (m w)").bitcast(I32), 0)
+            engine.memset(plane.bitcast(I32), 0)
 
         def load_scale_rows(plane, rows):
             for r in range(4):
                 nc.sync.dma_start(out=plane[r:P:32].bitcast(I32), in_=rows[r:16:4].bitcast(I32))
 
+        xs = keep.tile([P, PASSES, T], U8, name="xs", align_bytes=64)
+        xs_flat = xs[:].rearrange("p s t -> p (s t)")
+        zero(nc.vector, xs_flat)
+        load_scale_rows(xs, x_scales.rearrange("s b t -> b s t"))
+        x_rows = x_words.rearrange("s p t d -> s p (t d)")
+        xw = [keep.tile([P, T], I32, name="xw%d" % s, align_bytes=64) for s in range(PASSES)]
+        nc.sync.dma_start(out=xw[0][:], in_=x_rows[0].bitcast(I32))
+        nc.sync.dma_start(out=xw[1][:], in_=x_rows[1].bitcast(I32))
         slot_list = keep.tile([P, S // 16], U16, name="slot_list")
         nc.sync.dma_start(slot_list[:], offs)
 
-        xs_rows = x_scales.rearrange("s b t -> b s t")
-        xs = keep.tile([P, PASSES, T], U8, name="xs", align_bytes=64)
-        zero(nc.vector, xs[:])
-        load_scale_rows(xs, xs_rows)
-        xw = keep.tile([P, PASSES, T], I32, name="xw", align_bytes=64)
-        nc.sync.dma_start(out=xw[:], in_=x_words.rearrange("s p t d -> p s (t d)").bitcast(I32))
-
-        mask = keep.tile([P, P], F32, name="mask")
-        make_identity(nc, mask[:])
         ident = keep.tile([P, P], F32, name="ident")
-        nc.scalar.activation(ident[:], mask[:], ACT.Square)
+        make_identity(nc, ident[:])
+        warm = keep.tile([P, 1], F32, name="warm")
+        nc.scalar.activation(warm[:], ident[:, 0:1], ACT.Sigmoid)
 
         w1s_rows = w1_scales.rearrange("e s b i -> b (e s) i")
         w2s_rows = w2_scales.rearrange("e s b n -> b (e s) n")
         w1, w2 = {}, {}
         w1s = {g: keep.tile([P, PASSES * (g[1] - g[0]), H], U8, name="w1s_%d" % g[0], align_bytes=64) for g in SCALE_GROUPS}
+        moved = {g: keep.tile([P, (g[1] - g[0]) * C], U8, name="moved_%d" % g[0], align_bytes=64) for g in PACKED}
         w2s = keep.tile([P, E, N], U8, name="w2s", align_bytes=64)
         wgs = keep.tile([P, PASSES, N], U8, name="wgs", align_bytes=64)
-        for g in SCALE_GROUPS[:2]:
-            zero(nc.vector, w1s[g][:])
-        zero(nc.vector, w2s[:])
-        for g in SCALE_GROUPS[2:]:
-            zero(nc.vector, w1s[g][:])
-        zero(nc.vector, wgs[:])
+        zero(nc.vector, w1s[SCALE_GROUPS[0]][:].rearrange("p m w -> p (m w)"))
+        for g in SCALE_GROUPS[1:]:
+            zero(LATE, w1s[g][:].rearrange("p m w -> p (m w)"))
+            for gp in PACKED:
+                if gp[0] == g[0]:
+                    zero(LATE, moved[gp][:])
+        zero(LATE, w2s[:].rearrange("p m w -> p (m w)"))
+        zero(LATE, wgs[:].rearrange("p m w -> p (m w)"))
 
         def load_w1(g):
             t = keep.tile([P, (g[1] - g[0]) * PASSES, 2 * H], U8, name="w1_%d" % g[0], align_bytes=64)
@@ -92,167 +99,187 @@ def tile_moe_ogt_relu2_sigmoid_kernel(tc, x_words, x_scales, wg_words, wg_scales
             nc.sync.dma_start(out=t[:].bitcast(I32), in_=w2_words.rearrange("e s p b -> p (e s) b")[:, g[0] : g[1], :].bitcast(I32))
             w2[g] = t
 
-        pos = []
-        for j in range(SECOND_AT[-1] + 1):
-            if j == SECOND_RUN:
-                load_scale_rows(w2s, w2s_rows)
-            if j in (0, SECOND_RUN):
-                for g in SCALE_GROUPS[:2] if j == 0 else SCALE_GROUPS[2:]:
-                    load_scale_rows(w1s[g], w1s_rows[:, PASSES * g[0] : PASSES * g[1], :])
-            if j == LISTS_AT:
-                for r, src in enumerate((pos1, pos2, pos3)):
-                    t = keep.tile([P, T // 16], U16, name="pos%d" % r)
-                    nc.sync.dma_start(t[:], src)
-                    pos.append(t)
-            if j < len(GROUPS):
-                load_w1(GROUPS[j])
-            for g, at in zip(GROUPS, SECOND_AT):
-                if at == j:
-                    load_w2(g)
+        def load_w1_scales(g):
+            load_scale_rows(w1s[g], w1s_rows[:, PASSES * g[0] : PASSES * g[1], :])
+
+        def offsets(g):
+            return slot_list[:, g[0] * C // 16 : g[1] * C // 16]
 
         xg, sg = {}, {}
 
-        def gather(g):
-            n = (g[1] - g[0]) * C
-            cols = slot_list[:, g[0] * C // 16 : g[1] * C // 16]
-            for s in range(PASSES):
-                sg[g, s] = picked_s.tile([P, n], U8, name="sg%d" % s, align_bytes=64)
-                nc.vector.tensor_copy(sg[g, s][:], xs[:, s, :].indirect(cols))
-            for s in range(PASSES):
-                xg[g, s] = picked.tile([P, n], U32, name="xg%d" % s, align_bytes=64)
-                nc.vector.tensor_copy(xg[g, s][:], xw[:, s, :].bitcast(U32).indirect(cols))
+        def gather_bytes(g, s, window):
+            sg[g, s] = keep.tile([P, (g[1] - g[0]) * C], U8, name="sg%d_%d" % (g[0], s), align_bytes=64)
+            nc.vector.tensor_copy(sg[g, s][:], window.indirect(offsets(g)))
 
+        def gather_words(g):
+            for s in range(PASSES):
+                xg[g, s] = keep.tile([P, (g[1] - g[0]) * C], U32, name="xg%d_%d" % (g[0], s), align_bytes=64)
+                nc.vector.tensor_copy(xg[g, s][:], xw[s][:].bitcast(U32).indirect(offsets(g)))
+
+        def move_second_pass(g):
+            for r in range(4):
+                nc.sync.dma_start(out=moved[g][r:P:32].bitcast(I32), in_=sg[g, 0][SPARE + r : SPARE + 16 : 4].bitcast(I32))
+            sg[g, 1] = moved[g]
+
+        for g in WORD_GROUPS:
+            if g in PLAIN:
+                for s in range(PASSES):
+                    gather_bytes(g, s, xs[:, s, :])
+            for gp in PACKED:
+                if gp[0] == g[0]:
+                    gather_bytes(gp, 0, xs_flat)
+            gather_words(g)
+
+        load_w1_scales(SCALE_GROUPS[0])
+        load_w1(W1_GROUPS[0])
+        load_w1_scales(SCALE_GROUPS[1])
+        load_w1(W1_GROUPS[1])
+        load_w1_scales(SCALE_GROUPS[2])
+        load_w1(W1_GROUPS[2])
+        load_w1_scales(SCALE_GROUPS[3])
+        load_w1(W1_GROUPS[3])
+        load_w1_scales(SCALE_GROUPS[4])
+        load_w1(W1_GROUPS[4])
+        load_scale_rows(w2s, w2s_rows)
+        load_w1_scales(SCALE_GROUPS[5])
+        load_w1(W1_GROUPS[5])
+        load_w2(W2_GROUPS[0])
+        load_w2(W2_GROUPS[1])
+        wg = keep.tile([P, PASSES, N], I32, name="wg", align_bytes=64)
+        nc.sync.dma_start(out=wg[:], in_=wg_words.rearrange("s p n d -> p s (n d)").bitcast(I32))
+        load_scale_rows(wgs, wg_scales.rearrange("s b n -> b s n"))
+        pos = []
+        for r, src in enumerate((pos1, pos2, pos3)):
+            t = keep.tile([P, T // 16], U16, name="pos%d" % r)
+            nc.sync.dma_start(t[:], src)
+            pos.append(t)
+        gates = keep.tile([P, TOP, T], F32, name="gates")
+        nc.sync.dma_start(out=gates[:], in_=gate.rearrange("r p t -> p r t"))
+
+        YP = [(ps_y, "ybank"), (ps_pre, "pre"), (ps_turn, "turned")]
         y = [keep.tile([P, S], F32, name="y%d" % h) for h in range(HALVES)]
-        pre, relu, turned, hq, hs, ybank = {}, {}, {}, {}, {}, {}
+        pre, hb, hq, hs = {}, {}, {}, {}
 
         def first_product(e):
-            g, gs = group_of(GROUPS, e), group_of(SCALE_GROUPS, e)
-            if g[0] == e:
-                gather(g)
-            cols = slice((e - g[0]) * C, (e - g[0] + 1) * C)
-            pre[e] = ps_pre.tile([P, H], F32, name="pre")
+            g, gs, gw, gp = group_of(WORD_GROUPS, e), group_of(SCALE_GROUPS, e), group_of(W1_GROUPS, e), group_of(PAIRS, e)
+            gb = group_of(PLAIN + PACKED, e)
+            if gp[0] == e:
+                pre[gp] = ps_pre.tile([P, PRE_W, H], F32, name="pre")
             for s in range(PASSES):
                 nc.tensor.matmul_mx(
-                    out=pre[e][:],
-                    lhsT=xg[g, s][:, cols].bitcast(FP8X4),
-                    lhsT_scale=sg[g, s][:, cols],
-                    rhs=w1[g][:, (e - g[0]) * PASSES + s, :].bitcast(FP4X4),
+                    out=pre[gp][:, e - gp[0], :],
+                    lhsT=xg[g, s][:, (e - g[0]) * C : (e - g[0] + 1) * C].bitcast(FP8X4),
+                    lhsT_scale=sg[gb, s][:, (e - gb[0]) * C : (e - gb[0] + 1) * C],
+                    rhs=w1[gw][:, (e - gw[0]) * PASSES + s, :].bitcast(FP4X4),
                     rhs_scale=w1s[gs][:, (e - gs[0]) * PASSES + s, :],
                     start=(s == 0),
                     stop=(s == PASSES - 1),
                 )
 
-        def relu_and_turn(e):
-            relu[e] = ring.tile([P, 4, P], F32, name="relu")
-            src = pre[e][:].rearrange("u (p d) -> u d p", d=4)
-            if e in RELU_ON_VECTOR:
-                nc.vector.tensor_scalar_max(relu[e][:], src, 0.0)
+        def hidden(e):
+            gp, gy = group_of(PAIRS, e), group_of(Y_GROUPS, e)
+            relu = ring.tile([P, 4, P], F32, name="relu")
+            src = pre[gp][:, e - gp[0], :].rearrange("u (p d) -> u d p", d=4)
+            if e >= RELU_ON_VECTOR_FROM:
+                nc.vector.tensor_scalar_max(relu[:], src, 0.0)
             else:
-                nc.scalar.activation(relu[e][:], src, ACT.Relu)
-            turned[e] = ps_turn.tile([P, 4, C], F32, name="turned")
+                nc.scalar.activation(relu[:], src, ACT.Relu)
+            turned = ps_turn.tile([P, 4, C], F32, name="turned")
             for d in range(4):
-                nc.tensor.transpose(turned[e][:, d, :], relu[e][:, d, :], ident[:])
-
-        def square_and_quantise(g):
-            n = (g[1] - g[0]) * C
-            hb = ring.tile([P, n, 4], BF16, name="hb", align_bytes=64)
-            for e in range(*g):
-                nc.scalar.activation(hb[:, (e - g[0]) * C : (e - g[0] + 1) * C, :], turned[e][:].rearrange("p d u -> p u d"), ACT.Square)
-            hq[g] = coded.tile([P, n], U32, name="hq", align_bytes=64)
-            hs[g] = coded.tile([P, n], U8, name="hs", align_bytes=64)
-            for u0 in range(0, n, 2 * C):
-                u1 = min(u0 + 2 * C, n)
-                nc.vector.quantize_mx(out=hq[g][:, u0:u1].bitcast(FP8X4), scales=hs[g][:, u0:u1], in_=hb[:, u0:u1, :].rearrange("p u d -> p (u d)"))
-
-        def second_product(e):
-            g, gy = group_of(GROUPS, e), group_of(Y_GROUPS, e)
-            n = (gy[1] - gy[0]) * C
-            if gy == Y_GROUPS[-1]:
-                bank = ps_pre.tile([P, HALVES, n], F32, name="pre")
-                ybank[gy] = [bank[:, h, :] for h in range(HALVES)]
-            elif gy[0] == e:
-                ybank[gy] = [ps_y.tile([P, n], F32, name="ybank%d" % h)[:] for h in range(HALVES)]
-            for h in range(HALVES):
-                nc.tensor.matmul_mx(
-                    out=ybank[gy][h][:, (e - gy[0]) * C : (e - gy[0] + 1) * C],
-                    lhsT=w2[g][:, e - g[0], 2 * P * h : 2 * P * (h + 1)].bitcast(FP4X4),
-                    lhsT_scale=w2s[:, e, P * h : P * (h + 1)],
-                    rhs=hq[g][:, (e - g[0]) * C : (e - g[0] + 1) * C].bitcast(FP8X4),
-                    rhs_scale=hs[g][:, (e - g[0]) * C : (e - g[0] + 1) * C],
-                    start=True,
-                    stop=True,
-                )
+                nc.tensor.transpose(turned[:, d, :], relu[:, d, :], ident[:])
+            if gy[0] == e:
+                hb[gy] = keep.tile([P, (gy[1] - gy[0]) * C, 4], BF16, name="hb%d" % e, align_bytes=64)
+            nc.scalar.activation(hb[gy][:, (e - gy[0]) * C : (e - gy[0] + 1) * C, :], turned[:].rearrange("p d u -> p u d"), ACT.Square)
             if e == gy[1] - 1:
-                for h in range(HALVES):
-                    if (gy[0], h) in COPY_ON_VECTOR:
-                        nc.vector.tensor_copy(y[h][:, gy[0] * C : gy[1] * C], ybank[gy][h])
-                    else:
-                        nc.scalar.copy(y[h][:, gy[0] * C : gy[1] * C], ybank[gy][h])
+                n = (gy[1] - gy[0]) * C
+                hq[gy] = keep.tile([P, n], U32, name="hq%d" % e, align_bytes=64)
+                hs[gy] = keep.tile([P, n], U8, name="hs%d" % e, align_bytes=64)
+                nc.vector.quantize_mx(out=hq[gy][:].bitcast(FP8X4), scales=hs[gy][:], in_=hb[gy][:].rearrange("p u d -> p (u d)"))
 
-        for j in range(SECOND_AT[-1] + 1):
-            now = range(*GROUPS[j]) if j < len(GROUPS) else ()
-            for e in now:
-                first_product(e)
-            for e in now:
-                relu_and_turn(e)
-            for g, at in zip(GROUPS, SECOND_AT):
-                if at == j:
-                    for e in range(*g):
-                        second_product(e)
-            if j < len(GROUPS):
-                square_and_quantise(GROUPS[j])
-
-        gates = keep.tile([P, TOP, T], F32, name="gates")
-        for r in range(TOP):
-            nc.sync.dma_start(out=gates[:, r, :], in_=gate[r])
-        wg = keep.tile([P, PASSES, N], I32, name="wg", align_bytes=64)
-        nc.sync.dma_start(out=wg[:], in_=wg_words.rearrange("s p n d -> p s (n d)").bitcast(I32))
-        load_scale_rows(wgs, wg_scales.rearrange("s b n -> b s n"))
-
-        o = keep.tile([P, HALVES, T], F32, name="o")
-        for h in range(HALVES):
-            for t0, t1 in ((0, 512), (512, T)):
-                bank = ps_pre.tile([P, H], F32, name="pre")
-                for s in range(PASSES):
+        def second_product(g):
+            n = (g[1] - g[0]) * C
+            for h in range(HALVES):
+                pool, tag = YP[(HALVES * Y_GROUPS.index(g) + h) % len(YP)]
+                bank = pool.tile([P, n], F32, name=tag)
+                for e in range(*g):
+                    gw = group_of(W2_GROUPS, e)
+                    cols = slice((e - g[0]) * C, (e - g[0] + 1) * C)
                     nc.tensor.matmul_mx(
-                        out=bank[:, 0 : t1 - t0],
-                        lhsT=wg[:, s, P * h : P * (h + 1)].bitcast(FP8X4),
-                        lhsT_scale=wgs[:, s, P * h : P * (h + 1)],
-                        rhs=xw[:, s, t0:t1].bitcast(FP8X4),
-                        rhs_scale=xs[:, s, t0:t1],
-                        start=(s == 0),
-                        stop=(s == PASSES - 1),
+                        out=bank[:, cols],
+                        lhsT=w2[gw][:, e - gw[0], 2 * P * h : 2 * P * (h + 1)].bitcast(FP4X4),
+                        lhsT_scale=w2s[:, e, P * h : P * (h + 1)],
+                        rhs=hq[g][:, cols].bitcast(FP8X4),
+                        rhs_scale=hs[g][:, cols],
+                        start=True,
+                        stop=True,
                     )
-                nc.scalar.activation(o[:, h, t0:t1], bank[:, 0 : t1 - t0], ACT.Sigmoid)
+                if h == 0 or g[0] < Y_BOTH:
+                    nc.vector.tensor_copy(y[h][:, g[0] * C : g[1] * C], bank[:])
+                else:
+                    nc.scalar.copy(y[h][:, g[0] * C : g[1] * C], bank[:])
 
-        def weighted(h, r):
-            a = keep.tile([P, T], F32, name="part%d_%d" % (h, r))
-            nc.vector.tensor_tensor(a[:], y[h][:].indirect(pos[r][:]), gates[:, r, :], ALU.mult)
+        for gp in PAIRS:
+            for e in range(*gp):
+                first_product(e)
+            for e in range(*gp):
+                hidden(e)
+        for g in Y_GROUPS:
+            second_product(g)
+
+        CHUNKS = [(0, 0, SPLIT), (1, 0, SPLIT), (0, SPLIT, T), (1, SPLIT, T)]
+        o = {}
+        for h, t0, t1 in CHUNKS:
+            bank = ps_pre.tile([P, H], F32, name="pre")
+            for c0, c1 in ((t0, t0 + 256), (t0 + 256, t1)):
+                if c1 > c0:
+                    for s in range(PASSES):
+                        nc.tensor.matmul_mx(
+                            out=bank[:, c0 - t0 : c1 - t0],
+                            lhsT=wg[:, s, P * h : P * (h + 1)].bitcast(FP8X4),
+                            lhsT_scale=wgs[:, s, P * h : P * (h + 1)],
+                            rhs=xw[s][:, c0:c1].bitcast(FP8X4),
+                            rhs_scale=xs[:, s, c0:c1],
+                            start=(s == 0),
+                            stop=(s == PASSES - 1),
+                        )
+            o[h, t0] = keep.tile([P, t1 - t0], F32, name="o%d_%d" % (h, t0))
+            nc.scalar.activation(o[h, t0][:], bank[:, 0 : t1 - t0], ACT.Sigmoid)
+
+        def weighted(h, r, t0, t1, a):
+            nc.vector.tensor_tensor(a, y[h][:].indirect(pos[r][:, t0 // 16 : t1 // 16]), gates[:, r, t0:t1], ALU.mult)
             return a
 
         def finish(h, t0, t1, total):
             res = ring.tile([P, t1 - t0], F32, name="res")
-            nc.vector.tensor_tensor(res[:], total, o[:, h, t0:t1], ALU.mult)
+            nc.vector.tensor_tensor(res[:], total, o[h, t0][:], ALU.mult)
             nc.sync.dma_start(out=out[P * h : P * (h + 1), t0:t1], in_=res[:])
 
-        parts = [weighted(0, r) for r in range(TOP)]
-        for t0, t1 in ((0, 384), (384, T)):
-            blocks = (t1 - t0) // P
-            acc = ps_turn.tile([P, blocks, P], F32, name="turned")
+        def add_on_tensor(parts):
+            blocks = parts[0].shape[1] // P
+            acc = ps_y.tile([P, blocks, P], F32, name="ybank")
             for b in range(blocks):
                 for r in range(TOP):
-                    nc.tensor.matmul(acc[:, b, :], lhsT=parts[r][:, t0 + P * b : t0 + P * (b + 1)], rhs=ident[:], is_transpose=True, start=(r == 0), stop=(r == TOP - 1))
+                    nc.tensor.matmul(acc[:, b, :], lhsT=parts[r][:, P * b : P * (b + 1)], rhs=ident[:], is_transpose=True, start=(r == 0), stop=(r == TOP - 1))
             summed = ring.tile([P, blocks, P], F32, name="summed")
             nc.scalar.copy(summed[:], acc[:])
             back = ps_turn.tile([P, blocks, P], F32, name="turned")
             for b in range(blocks):
                 nc.tensor.transpose(back[:, b, :], summed[:, b, :], ident[:])
-            finish(0, t0, t1, back[:].rearrange("p b t -> p (b t)"))
+            return back[:].rearrange("p b t -> p (b t)")
 
-        parts = [weighted(1, r) for r in range(TOP)]
-        two = keep.tile([P, T], F32, name="two")
-        nc.vector.tensor_tensor(two[:], parts[0][:], parts[1][:], ALU.add)
-        for t0, t1 in ((0, 320), (320, T)):
-            three = ring.tile([P, t1 - t0], F32, name="three")
-            nc.vector.tensor_tensor(three[:], two[:, t0:t1], parts[2][:, t0:t1], ALU.add)
-            finish(1, t0, t1, three[:])
+        early = keep.tile([P, HALVES, TOP, SPLIT], F32, name="early")
+        first = add_on_tensor([weighted(0, r, 0, SPLIT, early[:, 0, r, :]) for r in range(TOP)])
+        second = add_on_tensor([weighted(1, r, 0, SPLIT, early[:, 1, r, :]) for r in range(TOP)])
+        finish(0, 0, SPLIT, first)
+        late = keep.tile([P, 2 * TOP - 1, T - SPLIT], F32, name="late", tag="o0_0")
+        third = add_on_tensor([weighted(0, r, SPLIT, T, late[:, r, :]) for r in range(TOP)])
+        parts = [weighted(1, r, SPLIT, T, late[:, TOP + r, :]) for r in range(TOP - 1)]
+        finish(1, 0, SPLIT, second)
+        two = keep.tile([P, T - SPLIT], F32, name="two")
+        nc.vector.tensor_tensor(two[:], parts[0], parts[1], ALU.add)
+        last = keep.tile([P, T - SPLIT], F32, name="last", tag="o1_0")
+        weighted(1, TOP - 1, SPLIT, T, last[:])
+        finish(0, SPLIT, T, third)
+        three = keep.tile([P, T - SPLIT], F32, name="three")
+        nc.vector.tensor_tensor(three[:], two[:], last[:], ALU.add)
+        finish(1, SPLIT, T, three[:])

@@ -33,6 +33,7 @@ W2_GROUPS = [(0, 8), (8, 15)]
 RELU_ON_VECTOR_FROM = 15
 SPARE = 16
 SPLIT = 384
+PACKED_AT = {g: g[0] for g in PACKED}
 Y_BOTH = 0
 
 
@@ -42,7 +43,7 @@ def group_of(groups, e):
 
 def tile_moe_ogt_relu2_sigmoid_kernel(tc, x_words, x_scales, wg_words, wg_scales, w1_words, w1_scales, w2_words, w2_scales, gate, offs, pos1, pos2, pos3, out):
     nc = tc.nc
-    LATE = nc.gpsimd
+    LATE = nc.vector
     with ExitStack() as ctx:
         keep = ctx.enter_context(tc.tile_pool(name="keep", bufs=1))
         ring = ctx.enter_context(tc.tile_pool(name="ring", bufs=4))
@@ -83,9 +84,9 @@ def tile_moe_ogt_relu2_sigmoid_kernel(tc, x_words, x_scales, wg_words, wg_scales
         zero(nc.vector, w1s[SCALE_GROUPS[0]][:].rearrange("p m w -> p (m w)"))
         for g in SCALE_GROUPS[1:]:
             zero(LATE, w1s[g][:].rearrange("p m w -> p (m w)"))
-            for gp in PACKED:
-                if gp[0] == g[0]:
-                    zero(LATE, moved[gp][:])
+
+        for gp in PACKED:
+            zero(LATE, moved[gp][:])
         zero(LATE, w2s[:].rearrange("p m w -> p (m w)"))
         zero(LATE, wgs[:].rearrange("p m w -> p (m w)"))
 
@@ -126,7 +127,7 @@ def tile_moe_ogt_relu2_sigmoid_kernel(tc, x_words, x_scales, wg_words, wg_scales
                 for s in range(PASSES):
                     gather_bytes(g, s, xs[:, s, :])
             for gp in PACKED:
-                if gp[0] == g[0]:
+                if PACKED_AT[gp] == g[0]:
                     gather_bytes(gp, 0, xs_flat)
             gather_words(g)
 

@@ -21,20 +21,14 @@ FP4X4 = mybir.dt.float4_e2m1fn_x4
 ACT = mybir.ActivationFunctionType
 ALU = mybir.AluOpType
 
-PLAIN = [(0, 2), (2, 5), (5, 8), (8, 11), (11, 13), (13, 15)]
-PACKED = []
-WORD_GROUPS = [(0, 2), (2, 5), (5, 8), (8, 11), (11, 13), (13, 15)]
-W1_GROUPS = [(0, 2), (2, 5), (5, 8), (8, 11), (11, 13), (13, 15)]
-SCALE_GROUPS = [(0, 2), (2, 5), (5, 8), (8, 11), (11, 13), (13, 15)]
-PAIRS = [(e, e + 1) for e in range(E)]
-PRE_W = 1
+GROUPS = [(0, 2), (2, 4), (4, 7), (7, 10), (10, 13), (13, 15)]
 Y_GROUPS = [(0, 4), (4, 8), (8, 12), (12, 14), (14, 15)]
 W2_GROUPS = [(0, 8), (8, 15)]
-RELU_ON_VECTOR_FROM = 15
-SPARE = 16
-SPLIT = 384
-PACKED_AT = {g: g[0] for g in PACKED}
-Y_BOTH = 0
+PRE_BANKS = (0, 1, 2)
+TURN_BANKS = (3, 4, 5, 6)
+Y_BANKS = (7, 0, 3, 1, 4, 2, 5, 7, 6, 0)
+TURNED = 4
+WIDE = TURNED * P
 
 
 def group_of(groups, e):
@@ -43,29 +37,28 @@ def group_of(groups, e):
 
 def tile_moe_ogt_relu2_sigmoid_kernel(tc, x_words, x_scales, wg_words, wg_scales, w1_words, w1_scales, w2_words, w2_scales, gate, offs, pos1, pos2, pos3, out):
     nc = tc.nc
-    LATE = nc.vector
     with ExitStack() as ctx:
         keep = ctx.enter_context(tc.tile_pool(name="keep", bufs=1))
         ring = ctx.enter_context(tc.tile_pool(name="ring", bufs=4))
-        ps_pre = ctx.enter_context(tc.psum_pool(name="ps_pre", bufs=3))
-        ps_turn = ctx.enter_context(tc.psum_pool(name="ps_turn", bufs=4))
-        ps_y = ctx.enter_context(tc.psum_pool(name="ps_y", bufs=1))
+        psum = ctx.enter_context(tc.psum_pool(name="psum", bufs=1))
 
-        def zero(engine, plane):
-            engine.memset(plane.bitcast(I32), 0)
+        def bank(b, *shape):
+            return psum.tile([P, *shape], F32, name="bank%d" % b)
+
+        def zero(plane):
+            nc.vector.memset(plane.rearrange("p m w -> p (m w)").bitcast(I32), 0)
 
         def load_scale_rows(plane, rows):
             for r in range(4):
                 nc.sync.dma_start(out=plane[r:P:32].bitcast(I32), in_=rows[r:16:4].bitcast(I32))
 
         xs = keep.tile([P, PASSES, T], U8, name="xs", align_bytes=64)
-        xs_flat = xs[:].rearrange("p s t -> p (s t)")
-        zero(nc.vector, xs_flat)
+        zero(xs[:])
         load_scale_rows(xs, x_scales.rearrange("s b t -> b s t"))
         x_rows = x_words.rearrange("s p t d -> s p (t d)")
         xw = [keep.tile([P, T], I32, name="xw%d" % s, align_bytes=64) for s in range(PASSES)]
-        nc.sync.dma_start(out=xw[0][:], in_=x_rows[0].bitcast(I32))
-        nc.sync.dma_start(out=xw[1][:], in_=x_rows[1].bitcast(I32))
+        for s in range(PASSES):
+            nc.sync.dma_start(out=xw[s][:], in_=x_rows[s].bitcast(I32))
         slot_list = keep.tile([P, S // 16], U16, name="slot_list")
         nc.sync.dma_start(slot_list[:], offs)
 
@@ -74,118 +67,88 @@ def tile_moe_ogt_relu2_sigmoid_kernel(tc, x_words, x_scales, wg_words, wg_scales
         warm = keep.tile([P, 1], F32, name="warm")
         nc.scalar.activation(warm[:], ident[:, 0:1], ACT.Sigmoid)
 
-        w1s_rows = w1_scales.rearrange("e s b i -> b (e s) i")
-        w2s_rows = w2_scales.rearrange("e s b n -> b (e s) n")
-        w1, w2 = {}, {}
-        w1s = {g: keep.tile([P, PASSES * (g[1] - g[0]), H], U8, name="w1s_%d" % g[0], align_bytes=64) for g in SCALE_GROUPS}
-        moved = {g: keep.tile([P, (g[1] - g[0]) * C], U8, name="moved_%d" % g[0], align_bytes=64) for g in PACKED}
+        w1s = {g: keep.tile([P, PASSES * (g[1] - g[0]), H], U8, name="w1s_%d" % g[0], align_bytes=64) for g in GROUPS}
         w2s = keep.tile([P, E, N], U8, name="w2s", align_bytes=64)
         wgs = keep.tile([P, PASSES, N], U8, name="wgs", align_bytes=64)
-        zero(nc.vector, w1s[SCALE_GROUPS[0]][:].rearrange("p m w -> p (m w)"))
-        for g in SCALE_GROUPS[1:]:
-            zero(LATE, w1s[g][:].rearrange("p m w -> p (m w)"))
-
-        for gp in PACKED:
-            zero(LATE, moved[gp][:])
-        zero(LATE, w2s[:].rearrange("p m w -> p (m w)"))
-        zero(LATE, wgs[:].rearrange("p m w -> p (m w)"))
-
-        def load_w1(g):
-            t = keep.tile([P, (g[1] - g[0]) * PASSES, 2 * H], U8, name="w1_%d" % g[0], align_bytes=64)
-            nc.sync.dma_start(out=t[:].bitcast(I32), in_=w1_words.rearrange("e s p b -> p (e s) b")[:, PASSES * g[0] : PASSES * g[1], :].bitcast(I32))
-            w1[g] = t
-
-        def load_w2(g):
-            t = keep.tile([P, g[1] - g[0], 2 * N], U8, name="w2_%d" % g[0], align_bytes=64)
-            nc.sync.dma_start(out=t[:].bitcast(I32), in_=w2_words.rearrange("e s p b -> p (e s) b")[:, g[0] : g[1], :].bitcast(I32))
-            w2[g] = t
-
-        def load_w1_scales(g):
-            load_scale_rows(w1s[g], w1s_rows[:, PASSES * g[0] : PASSES * g[1], :])
-
-        def offsets(g):
-            return slot_list[:, g[0] * C // 16 : g[1] * C // 16]
+        rows = keep.tile([P, TOP, P], F32, name="rows")
+        for plane in [w1s[g] for g in GROUPS] + [w2s, wgs, rows]:
+            zero(plane[:])
 
         xg, sg = {}, {}
-
-        def gather_bytes(g, s, window):
-            sg[g, s] = keep.tile([P, (g[1] - g[0]) * C], U8, name="sg%d_%d" % (g[0], s), align_bytes=64)
-            nc.vector.tensor_copy(sg[g, s][:], window.indirect(offsets(g)))
-
-        def gather_words(g):
+        for g in GROUPS:
+            offsets = slot_list[:, g[0] * C // 16 : g[1] * C // 16]
+            for s in range(PASSES):
+                sg[g, s] = keep.tile([P, (g[1] - g[0]) * C], U8, name="sg%d_%d" % (g[0], s), align_bytes=64)
+                nc.vector.tensor_copy(sg[g, s][:], xs[:, s, :].indirect(offsets))
             for s in range(PASSES):
                 xg[g, s] = keep.tile([P, (g[1] - g[0]) * C], U32, name="xg%d_%d" % (g[0], s), align_bytes=64)
-                nc.vector.tensor_copy(xg[g, s][:], xw[s][:].bitcast(U32).indirect(offsets(g)))
+                nc.vector.tensor_copy(xg[g, s][:], xw[s][:].bitcast(U32).indirect(offsets))
 
-        def move_second_pass(g):
-            for r in range(4):
-                nc.sync.dma_start(out=moved[g][r:P:32].bitcast(I32), in_=sg[g, 0][SPARE + r : SPARE + 16 : 4].bitcast(I32))
-            sg[g, 1] = moved[g]
+        w1, w2, pos = {}, {}, []
 
-        for g in WORD_GROUPS:
-            if g in PLAIN:
-                for s in range(PASSES):
-                    gather_bytes(g, s, xs[:, s, :])
-            for gp in PACKED:
-                if PACKED_AT[gp] == g[0]:
-                    gather_bytes(gp, 0, xs_flat)
-            gather_words(g)
+        def load_w1(g):
+            rows_of_g = slice(PASSES * g[0], PASSES * g[1])
+            load_scale_rows(w1s[g], w1_scales.rearrange("e s b i -> b (e s) i")[:, rows_of_g, :])
+            w1[g] = keep.tile([P, (g[1] - g[0]) * PASSES, 2 * H], U8, name="w1_%d" % g[0], align_bytes=64)
+            nc.sync.dma_start(out=w1[g][:].bitcast(I32), in_=w1_words.rearrange("e s p b -> p (e s) b")[:, rows_of_g, :].bitcast(I32))
 
-        load_w1_scales(SCALE_GROUPS[0])
-        load_w1(W1_GROUPS[0])
-        load_w1_scales(SCALE_GROUPS[1])
-        load_w1(W1_GROUPS[1])
-        load_w1_scales(SCALE_GROUPS[2])
-        load_w1(W1_GROUPS[2])
-        load_w1_scales(SCALE_GROUPS[3])
-        load_w1(W1_GROUPS[3])
-        load_w1_scales(SCALE_GROUPS[4])
-        load_w1(W1_GROUPS[4])
-        load_scale_rows(w2s, w2s_rows)
-        load_w1_scales(SCALE_GROUPS[5])
-        load_w1(W1_GROUPS[5])
+        def load_w2(g):
+            w2[g] = keep.tile([P, g[1] - g[0], 2 * N], U8, name="w2_%d" % g[0], align_bytes=64)
+            nc.sync.dma_start(out=w2[g][:].bitcast(I32), in_=w2_words.rearrange("e s p b -> p (e s) b")[:, g[0] : g[1], :].bitcast(I32))
+
+        def load_lists():
+            for r, src in enumerate((pos1, pos2, pos3)):
+                t = keep.tile([P, T // 16], U16, name="pos%d" % r)
+                nc.sync.dma_start(t[:], src)
+                pos.append(t)
+
+        wg = keep.tile([P, PASSES, N], I32, name="wg", align_bytes=64)
+        gates = keep.tile([P, TOP, T - WIDE], F32, name="gates")
+
+        def load_wg():
+            nc.sync.dma_start(out=wg[:], in_=wg_words.rearrange("s p n d -> p s (n d)").bitcast(I32))
+            load_scale_rows(wgs, wg_scales.rearrange("s b n -> b s n"))
+
+        def load_rows():
+            nc.sync.dma_start(out=rows[0:TURNED], in_=gate[:, 0, 0:WIDE].rearrange("r (b p) -> b r p", p=P))
+
+        def load_gates():
+            nc.sync.dma_start(out=gates[:], in_=gate[:, :, WIDE:T].rearrange("r p t -> p r t"))
+
+        load_w1(GROUPS[0])
+        load_w1(GROUPS[1])
+        load_w1(GROUPS[2])
+        load_w1(GROUPS[3])
+        load_w1(GROUPS[4])
+        load_lists()
+        load_scale_rows(w2s, w2_scales.rearrange("e s b n -> b (e s) n"))
+        load_w1(GROUPS[5])
         load_w2(W2_GROUPS[0])
         load_w2(W2_GROUPS[1])
-        wg = keep.tile([P, PASSES, N], I32, name="wg", align_bytes=64)
-        nc.sync.dma_start(out=wg[:], in_=wg_words.rearrange("s p n d -> p s (n d)").bitcast(I32))
-        load_scale_rows(wgs, wg_scales.rearrange("s b n -> b s n"))
-        pos = []
-        for r, src in enumerate((pos1, pos2, pos3)):
-            t = keep.tile([P, T // 16], U16, name="pos%d" % r)
-            nc.sync.dma_start(t[:], src)
-            pos.append(t)
-        gates = keep.tile([P, TOP, T], F32, name="gates")
-        nc.sync.dma_start(out=gates[:], in_=gate.rearrange("r p t -> p r t"))
+        load_wg()
+        load_rows()
+        load_gates()
 
-        YP = [(ps_y, "ybank"), (ps_pre, "pre"), (ps_turn, "turned")]
         y = [keep.tile([P, S], F32, name="y%d" % h) for h in range(HALVES)]
-        pre, hb, hq, hs = {}, {}, {}, {}
+        hb, hq, hs = {}, {}, {}
 
-        def first_product(e):
-            g, gs, gw, gp = group_of(WORD_GROUPS, e), group_of(SCALE_GROUPS, e), group_of(W1_GROUPS, e), group_of(PAIRS, e)
-            gb = group_of(PLAIN + PACKED, e)
-            if gp[0] == e:
-                pre[gp] = ps_pre.tile([P, PRE_W, H], F32, name="pre")
+        def hidden(e):
+            g, gy = group_of(GROUPS, e), group_of(Y_GROUPS, e)
+            cols = slice((e - g[0]) * C, (e - g[0] + 1) * C)
+            pre = bank(PRE_BANKS[e % len(PRE_BANKS)], H)
             for s in range(PASSES):
                 nc.tensor.matmul_mx(
-                    out=pre[gp][:, e - gp[0], :],
-                    lhsT=xg[g, s][:, (e - g[0]) * C : (e - g[0] + 1) * C].bitcast(FP8X4),
-                    lhsT_scale=sg[gb, s][:, (e - gb[0]) * C : (e - gb[0] + 1) * C],
-                    rhs=w1[gw][:, (e - gw[0]) * PASSES + s, :].bitcast(FP4X4),
-                    rhs_scale=w1s[gs][:, (e - gs[0]) * PASSES + s, :],
+                    out=pre[:],
+                    lhsT=xg[g, s][:, cols].bitcast(FP8X4),
+                    lhsT_scale=sg[g, s][:, cols],
+                    rhs=w1[g][:, (e - g[0]) * PASSES + s, :].bitcast(FP4X4),
+                    rhs_scale=w1s[g][:, (e - g[0]) * PASSES + s, :],
                     start=(s == 0),
                     stop=(s == PASSES - 1),
                 )
-
-        def hidden(e):
-            gp, gy = group_of(PAIRS, e), group_of(Y_GROUPS, e)
             relu = ring.tile([P, 4, P], F32, name="relu")
-            src = pre[gp][:, e - gp[0], :].rearrange("u (p d) -> u d p", d=4)
-            if e >= RELU_ON_VECTOR_FROM:
-                nc.vector.tensor_scalar_max(relu[:], src, 0.0)
-            else:
-                nc.scalar.activation(relu[:], src, ACT.Relu)
-            turned = ps_turn.tile([P, 4, C], F32, name="turned")
+            nc.scalar.activation(relu[:], pre[:].rearrange("u (p d) -> u d p", d=4), ACT.Relu)
+            turned = bank(TURN_BANKS[e % len(TURN_BANKS)], 4, C)
             for d in range(4):
                 nc.tensor.transpose(turned[:, d, :], relu[:, d, :], ident[:])
             if gy[0] == e:
@@ -197,16 +160,14 @@ def tile_moe_ogt_relu2_sigmoid_kernel(tc, x_words, x_scales, wg_words, wg_scales
                 hs[gy] = keep.tile([P, n], U8, name="hs%d" % e, align_bytes=64)
                 nc.vector.quantize_mx(out=hq[gy][:].bitcast(FP8X4), scales=hs[gy][:], in_=hb[gy][:].rearrange("p u d -> p (u d)"))
 
-        def second_product(g):
-            n = (g[1] - g[0]) * C
+        def second_product(j, g):
             for h in range(HALVES):
-                pool, tag = YP[(HALVES * Y_GROUPS.index(g) + h) % len(YP)]
-                bank = pool.tile([P, n], F32, name=tag)
+                acc = bank(Y_BANKS[HALVES * j + h], (g[1] - g[0]) * C)
                 for e in range(*g):
                     gw = group_of(W2_GROUPS, e)
                     cols = slice((e - g[0]) * C, (e - g[0] + 1) * C)
                     nc.tensor.matmul_mx(
-                        out=bank[:, cols],
+                        out=acc[:, cols],
                         lhsT=w2[gw][:, e - gw[0], 2 * P * h : 2 * P * (h + 1)].bitcast(FP4X4),
                         lhsT_scale=w2s[:, e, P * h : P * (h + 1)],
                         rhs=hq[g][:, cols].bitcast(FP8X4),
@@ -214,73 +175,84 @@ def tile_moe_ogt_relu2_sigmoid_kernel(tc, x_words, x_scales, wg_words, wg_scales
                         start=True,
                         stop=True,
                     )
-                if h == 0 or g[0] < Y_BOTH:
-                    nc.vector.tensor_copy(y[h][:, g[0] * C : g[1] * C], bank[:])
+                if h == 0:
+                    nc.vector.tensor_copy(y[h][:, g[0] * C : g[1] * C], acc[:])
                 else:
-                    nc.scalar.copy(y[h][:, g[0] * C : g[1] * C], bank[:])
+                    nc.scalar.copy(y[h][:, g[0] * C : g[1] * C], acc[:])
 
-        for gp in PAIRS:
-            for e in range(*gp):
-                first_product(e)
-            for e in range(*gp):
-                hidden(e)
-        for g in Y_GROUPS:
-            second_product(g)
+        by_token = keep.tile([P, TOP, TURNED], F32, name="by_token")
 
-        CHUNKS = [(0, 0, SPLIT), (1, 0, SPLIT), (0, SPLIT, T), (1, SPLIT, T)]
+        def turn_gates():
+            turned = bank(7, TOP, P)
+            for r in range(TOP):
+                nc.tensor.transpose(turned[:, r, :], rows[:, r, :], ident[:])
+            nc.scalar.copy(by_token[:], turned[:, :, 0:TURNED])
+
+        for e in range(E):
+            hidden(e)
+        for j, g in enumerate(Y_GROUPS):
+            second_product(j, g)
+
         o = {}
-        for h, t0, t1 in CHUNKS:
-            bank = ps_pre.tile([P, H], F32, name="pre")
-            for c0, c1 in ((t0, t0 + 256), (t0 + 256, t1)):
-                if c1 > c0:
-                    for s in range(PASSES):
-                        nc.tensor.matmul_mx(
-                            out=bank[:, c0 - t0 : c1 - t0],
-                            lhsT=wg[:, s, P * h : P * (h + 1)].bitcast(FP8X4),
-                            lhsT_scale=wgs[:, s, P * h : P * (h + 1)],
-                            rhs=xw[s][:, c0:c1].bitcast(FP8X4),
-                            rhs_scale=xs[:, s, c0:c1],
-                            start=(s == 0),
-                            stop=(s == PASSES - 1),
-                        )
-            o[h, t0] = keep.tile([P, t1 - t0], F32, name="o%d_%d" % (h, t0))
-            nc.scalar.activation(o[h, t0][:], bank[:, 0 : t1 - t0], ACT.Sigmoid)
 
-        def weighted(h, r, t0, t1, a):
-            nc.vector.tensor_tensor(a, y[h][:].indirect(pos[r][:, t0 // 16 : t1 // 16]), gates[:, r, t0:t1], ALU.mult)
-            return a
+        def output_gate(b, name, parts):
+            acc = bank(b, len(parts), parts[0][2] - parts[0][1])
+            for j, (h, t0, t1) in enumerate(parts):
+                for s in range(PASSES):
+                    nc.tensor.matmul_mx(
+                        out=acc[:, j, :],
+                        lhsT=wg[:, s, P * h : P * (h + 1)].bitcast(FP8X4),
+                        lhsT_scale=wgs[:, s, P * h : P * (h + 1)],
+                        rhs=xw[s][:, t0:t1].bitcast(FP8X4),
+                        rhs_scale=xs[:, s, t0:t1],
+                        start=(s == 0),
+                        stop=(s == PASSES - 1),
+                    )
+            o[name] = keep.tile([P, len(parts), parts[0][2] - parts[0][1]], F32, name="o_%s" % name)
+            nc.scalar.activation(o[name][:], acc[:], ACT.Sigmoid)
 
-        def finish(h, t0, t1, total):
-            res = ring.tile([P, t1 - t0], F32, name="res")
-            nc.vector.tensor_tensor(res[:], total, o[h, t0][:], ALU.mult)
-            nc.sync.dma_start(out=out[P * h : P * (h + 1), t0:t1], in_=res[:])
-
-        def add_on_tensor(parts):
-            blocks = parts[0].shape[1] // P
-            acc = ps_y.tile([P, blocks, P], F32, name="ybank")
-            for b in range(blocks):
+        def combine_turned(h):
+            scaled = keep.tile([P, TOP, TURNED, P], F32, name="scaled%d" % h)
+            for r in range(TOP):
+                part = keep.tile([P, WIDE], F32, name="part%d_%d" % (h, r))
+                nc.vector.tensor_copy(part[:], y[h][:].indirect(pos[r][:, 0 : WIDE // 16]))
+                turned = bank(1 + (TOP * h + r) % 2, TURNED, P)
+                for b in range(TURNED):
+                    nc.tensor.transpose(turned[:, b, :], part[:, P * b : P * (b + 1)], ident[:])
+                for b in range(TURNED):
+                    nc.scalar.activation(scaled[:, r, b, :], turned[:, b, :], ACT.Copy, scale=by_token[:, r, b : b + 1])
+            total = bank(3 + h, TURNED, P)
+            for b in range(TURNED):
                 for r in range(TOP):
-                    nc.tensor.matmul(acc[:, b, :], lhsT=parts[r][:, P * b : P * (b + 1)], rhs=ident[:], is_transpose=True, start=(r == 0), stop=(r == TOP - 1))
-            summed = ring.tile([P, blocks, P], F32, name="summed")
-            nc.scalar.copy(summed[:], acc[:])
-            back = ps_turn.tile([P, blocks, P], F32, name="turned")
-            for b in range(blocks):
-                nc.tensor.transpose(back[:, b, :], summed[:, b, :], ident[:])
-            return back[:].rearrange("p b t -> p (b t)")
+                    nc.tensor.matmul(total[:, b, :], lhsT=scaled[:, r, b, :], rhs=ident[:], is_transpose=True, start=(r == 0), stop=(r == TOP - 1))
+            return total[:].rearrange("p b t -> p (b t)")
 
-        early = keep.tile([P, HALVES, TOP, SPLIT], F32, name="early")
-        first = add_on_tensor([weighted(0, r, 0, SPLIT, early[:, 0, r, :]) for r in range(TOP)])
-        second = add_on_tensor([weighted(1, r, 0, SPLIT, early[:, 1, r, :]) for r in range(TOP)])
-        finish(0, 0, SPLIT, first)
-        late = keep.tile([P, 2 * TOP - 1, T - SPLIT], F32, name="late", tag="o0_0")
-        third = add_on_tensor([weighted(0, r, SPLIT, T, late[:, r, :]) for r in range(TOP)])
-        parts = [weighted(1, r, SPLIT, T, late[:, TOP + r, :]) for r in range(TOP - 1)]
-        finish(1, 0, SPLIT, second)
-        two = keep.tile([P, T - SPLIT], F32, name="two")
-        nc.vector.tensor_tensor(two[:], parts[0], parts[1], ALU.add)
-        last = keep.tile([P, T - SPLIT], F32, name="last", tag="o1_0")
-        weighted(1, TOP - 1, SPLIT, T, last[:])
-        finish(0, SPLIT, T, third)
-        three = keep.tile([P, T - SPLIT], F32, name="three")
+        def finish_turned(h, total):
+            res = keep.tile([P, WIDE], F32, name="res%d" % h)
+            nc.vector.tensor_tensor(res[:], total, o[h][:, 0, :], ALU.mult)
+            nc.sync.dma_start(out=out[P * h : P * (h + 1), 0:WIDE], in_=res[:])
+
+        turn_gates()
+        for h in range(HALVES):
+            output_gate((6, 0)[h], h, [(h, 0, WIDE)])
+        output_gate(6, "rest", [(h, WIDE, T) for h in range(HALVES)])
+        totals = [combine_turned(h) for h in range(HALVES)]
+        parts = keep.tile([P, TOP - 1, HALVES, T - WIDE], F32, name="parts")
+        last = keep.tile([P, HALVES, T - WIDE], F32, name="last", tag="o_0")
+
+        def weighted(r, into):
+            for h in range(HALVES):
+                nc.vector.tensor_tensor(into[:, h, :], y[h][:].indirect(pos[r][:, WIDE // 16 : T // 16]), gates[:, r, :], ALU.mult)
+
+        weighted(0, parts[:, 0])
+        weighted(1, parts[:, 1])
+        two = keep.tile([P, HALVES, T - WIDE], F32, name="two")
+        nc.vector.tensor_tensor(two[:], parts[:, 0], parts[:, 1], ALU.add)
+        finish_turned(0, totals[0])
+        weighted(2, last)
+        three = keep.tile([P, HALVES, T - WIDE], F32, name="three")
         nc.vector.tensor_tensor(three[:], two[:], last[:], ALU.add)
-        finish(1, SPLIT, T, three[:])
+        res = keep.tile([P, HALVES, T - WIDE], F32, name="res_rest")
+        nc.vector.tensor_tensor(res[:], three[:], o["rest"][:], ALU.mult)
+        nc.sync.dma_start(out=out.rearrange("(h p) t -> p h t", p=P)[:, :, WIDE:T], in_=res[:])
+        finish_turned(1, totals[1])

@@ -22,17 +22,26 @@ ACT = mybir.ActivationFunctionType
 ALU = mybir.AluOpType
 
 GROUPS = [(0, 2), (2, 4), (4, 7), (7, 10), (10, 13), (13, 15)]
+SINGLE_FROM = 7
 Y_GROUPS = [(0, 4), (4, 8), (8, 12), (12, 14), (14, 15)]
 W2_GROUPS = [(0, 8), (8, 15)]
 PRE_BANKS = (0, 1, 2)
 TURN_BANKS = (3, 4, 5, 6)
-Y_BANKS = (7, 0, 3, 1, 4, 2, 5, 7, 6, 0)
-TURNED = 4
-WIDE = TURNED * P
+SPARE_BANK = 7
+BLOCKS = 4
+WIDE = BLOCKS * P
 
 
 def group_of(groups, e):
     return [g for g in groups if g[0] <= e < g[1]][0]
+
+
+def pre_bank(e):
+    return PRE_BANKS[e % len(PRE_BANKS)]
+
+
+def turn_bank(e):
+    return TURN_BANKS[e % len(TURN_BANKS)]
 
 
 def tile_moe_ogt_relu2_sigmoid_kernel(tc, x_words, x_scales, wg_words, wg_scales, w1_words, w1_scales, w2_words, w2_scales, gate, offs, pos1, pos2, pos3, out):
@@ -45,20 +54,18 @@ def tile_moe_ogt_relu2_sigmoid_kernel(tc, x_words, x_scales, wg_words, wg_scales
         def bank(b, *shape):
             return psum.tile([P, *shape], F32, name="bank%d" % b)
 
-        def zero(plane):
-            nc.vector.memset(plane.rearrange("p m w -> p (m w)").bitcast(I32), 0)
+        def zero(tile):
+            nc.vector.memset(tile[:].rearrange("p m w -> p (m w)").bitcast(I32), 0)
 
-        def load_scale_rows(plane, rows):
+        def load_scale_rows(tile, rows):
             for r in range(4):
-                nc.sync.dma_start(out=plane[r:P:32].bitcast(I32), in_=rows[r:16:4].bitcast(I32))
+                nc.sync.dma_start(out=tile[r:P:32].bitcast(I32), in_=rows[r:16:4].bitcast(I32))
 
         xs = keep.tile([P, PASSES, T], U8, name="xs", align_bytes=64)
-        zero(xs[:])
+        zero(xs)
         load_scale_rows(xs, x_scales.rearrange("s b t -> b s t"))
-        x_rows = x_words.rearrange("s p t d -> s p (t d)")
-        xw = [keep.tile([P, T], I32, name="xw%d" % s, align_bytes=64) for s in range(PASSES)]
-        for s in range(PASSES):
-            nc.sync.dma_start(out=xw[s][:], in_=x_rows[s].bitcast(I32))
+        xw = keep.tile([P, PASSES, T], I32, name="xw", align_bytes=64)
+        nc.sync.dma_start(out=xw[:], in_=x_words.rearrange("s p t d -> p s (t d)").bitcast(I32))
         slot_list = keep.tile([P, S // 16], U16, name="slot_list")
         nc.sync.dma_start(slot_list[:], offs)
 
@@ -70,64 +77,53 @@ def tile_moe_ogt_relu2_sigmoid_kernel(tc, x_words, x_scales, wg_words, wg_scales
         w1s = {g: keep.tile([P, PASSES * (g[1] - g[0]), H], U8, name="w1s_%d" % g[0], align_bytes=64) for g in GROUPS}
         w2s = keep.tile([P, E, N], U8, name="w2s", align_bytes=64)
         wgs = keep.tile([P, PASSES, N], U8, name="wgs", align_bytes=64)
-        rows = keep.tile([P, TOP, P], F32, name="rows")
-        for plane in [w1s[g] for g in GROUPS] + [w2s, wgs, rows]:
-            zero(plane[:])
+        gate_rows = keep.tile([P, TOP, P], F32, name="gate_rows")
+        for tile in [w1s[g] for g in GROUPS] + [w2s, wgs, gate_rows]:
+            zero(tile)
+
+        def slots(a, b):
+            return slot_list[:, a * C // 16 : b * C // 16]
 
         xg, sg = {}, {}
         for g in GROUPS:
-            offsets = slot_list[:, g[0] * C // 16 : g[1] * C // 16]
             for s in range(PASSES):
                 sg[g, s] = keep.tile([P, (g[1] - g[0]) * C], U8, name="sg%d_%d" % (g[0], s), align_bytes=64)
-                nc.vector.tensor_copy(sg[g, s][:], xs[:, s, :].indirect(offsets))
+                nc.vector.tensor_copy(sg[g, s][:], xs[:, s, :].indirect(slots(*g)))
             for s in range(PASSES):
                 xg[g, s] = keep.tile([P, (g[1] - g[0]) * C], U32, name="xg%d_%d" % (g[0], s), align_bytes=64)
-                nc.vector.tensor_copy(xg[g, s][:], xw[s][:].bitcast(U32).indirect(offsets))
+            for a, b in [(e, e + 1) for e in range(*g)] if g[0] >= SINGLE_FROM else [g]:
+                for s in range(PASSES):
+                    nc.vector.tensor_copy(xg[g, s][:, (a - g[0]) * C : (b - g[0]) * C], xw[:, s, :].bitcast(U32).indirect(slots(a, b)))
 
         w1, w2, pos = {}, {}, []
 
         def load_w1(g):
-            rows_of_g = slice(PASSES * g[0], PASSES * g[1])
-            load_scale_rows(w1s[g], w1_scales.rearrange("e s b i -> b (e s) i")[:, rows_of_g, :])
             w1[g] = keep.tile([P, (g[1] - g[0]) * PASSES, 2 * H], U8, name="w1_%d" % g[0], align_bytes=64)
-            nc.sync.dma_start(out=w1[g][:].bitcast(I32), in_=w1_words.rearrange("e s p b -> p (e s) b")[:, rows_of_g, :].bitcast(I32))
+            nc.sync.dma_start(out=w1[g][:].bitcast(I32), in_=w1_words.rearrange("e s p b -> p (e s) b")[:, PASSES * g[0] : PASSES * g[1], :].bitcast(I32))
 
-        def load_w2(g):
-            w2[g] = keep.tile([P, g[1] - g[0], 2 * N], U8, name="w2_%d" % g[0], align_bytes=64)
-            nc.sync.dma_start(out=w2[g][:].bitcast(I32), in_=w2_words.rearrange("e s p b -> p (e s) b")[:, g[0] : g[1], :].bitcast(I32))
-
-        def load_lists():
-            for r, src in enumerate((pos1, pos2, pos3)):
-                t = keep.tile([P, T // 16], U16, name="pos%d" % r)
-                nc.sync.dma_start(t[:], src)
-                pos.append(t)
-
-        wg = keep.tile([P, PASSES, N], I32, name="wg", align_bytes=64)
-        gates = keep.tile([P, TOP, T - WIDE], F32, name="gates")
-
-        def load_wg():
-            nc.sync.dma_start(out=wg[:], in_=wg_words.rearrange("s p n d -> p s (n d)").bitcast(I32))
-            load_scale_rows(wgs, wg_scales.rearrange("s b n -> b s n"))
-
-        def load_rows():
-            nc.sync.dma_start(out=rows[0:TURNED], in_=gate[:, 0, 0:WIDE].rearrange("r (b p) -> b r p", p=P))
-
-        def load_gates():
-            nc.sync.dma_start(out=gates[:], in_=gate[:, :, WIDE:T].rearrange("r p t -> p r t"))
+        def load_w1_scales(g):
+            load_scale_rows(w1s[g], w1_scales.rearrange("e s b i -> b (e s) i")[:, PASSES * g[0] : PASSES * g[1], :])
 
         load_w1(GROUPS[0])
-        load_w1(GROUPS[1])
-        load_w1(GROUPS[2])
-        load_w1(GROUPS[3])
-        load_w1(GROUPS[4])
-        load_lists()
+        load_w1_scales(GROUPS[0])
+        for g in GROUPS[1:-1]:
+            load_w1_scales(g)
+            load_w1(g)
+        for r, src in enumerate((pos1, pos2, pos3)):
+            pos.append(keep.tile([P, T // 16], U16, name="pos%d" % r))
+            nc.sync.dma_start(pos[r][:], src)
         load_scale_rows(w2s, w2_scales.rearrange("e s b n -> b (e s) n"))
-        load_w1(GROUPS[5])
-        load_w2(W2_GROUPS[0])
-        load_w2(W2_GROUPS[1])
-        load_wg()
-        load_rows()
-        load_gates()
+        load_w1_scales(GROUPS[-1])
+        load_w1(GROUPS[-1])
+        for g in W2_GROUPS:
+            w2[g] = keep.tile([P, g[1] - g[0], 2 * N], U8, name="w2_%d" % g[0], align_bytes=64)
+            nc.sync.dma_start(out=w2[g][:].bitcast(I32), in_=w2_words.rearrange("e s p b -> p (e s) b")[:, g[0] : g[1], :].bitcast(I32))
+        wg = keep.tile([P, PASSES, N], I32, name="wg", align_bytes=64)
+        nc.sync.dma_start(out=wg[:], in_=wg_words.rearrange("s p n d -> p s (n d)").bitcast(I32))
+        load_scale_rows(wgs, wg_scales.rearrange("s b n -> b s n"))
+        nc.sync.dma_start(out=gate_rows[0:BLOCKS], in_=gate[:, 0, 0:WIDE].rearrange("r (b p) -> b r p", p=P))
+        gate_rest = keep.tile([P, TOP, T - WIDE], F32, name="gate_rest")
+        nc.sync.dma_start(out=gate_rest[:], in_=gate[:, :, WIDE:T].rearrange("r p t -> p r t"))
 
         y = [keep.tile([P, S], F32, name="y%d" % h) for h in range(HALVES)]
         hb, hq, hs = {}, {}, {}
@@ -135,7 +131,7 @@ def tile_moe_ogt_relu2_sigmoid_kernel(tc, x_words, x_scales, wg_words, wg_scales
         def hidden(e):
             g, gy = group_of(GROUPS, e), group_of(Y_GROUPS, e)
             cols = slice((e - g[0]) * C, (e - g[0] + 1) * C)
-            pre = bank(PRE_BANKS[e % len(PRE_BANKS)], H)
+            pre = bank(pre_bank(e), H)
             for s in range(PASSES):
                 nc.tensor.matmul_mx(
                     out=pre[:],
@@ -148,21 +144,21 @@ def tile_moe_ogt_relu2_sigmoid_kernel(tc, x_words, x_scales, wg_words, wg_scales
                 )
             relu = ring.tile([P, 4, P], F32, name="relu")
             nc.scalar.activation(relu[:], pre[:].rearrange("u (p d) -> u d p", d=4), ACT.Relu)
-            turned = bank(TURN_BANKS[e % len(TURN_BANKS)], 4, C)
+            turned = bank(turn_bank(e), 4, C)
             for d in range(4):
                 nc.tensor.transpose(turned[:, d, :], relu[:, d, :], ident[:])
-            if gy[0] == e:
-                hb[gy] = keep.tile([P, (gy[1] - gy[0]) * C, 4], BF16, name="hb%d" % e, align_bytes=64)
+            n = (gy[1] - gy[0]) * C
+            if e == gy[0]:
+                hb[gy] = keep.tile([P, n, 4], BF16, name="hb%d" % e, align_bytes=64)
             nc.scalar.activation(hb[gy][:, (e - gy[0]) * C : (e - gy[0] + 1) * C, :], turned[:].rearrange("p d u -> p u d"), ACT.Square)
             if e == gy[1] - 1:
-                n = (gy[1] - gy[0]) * C
                 hq[gy] = keep.tile([P, n], U32, name="hq%d" % e, align_bytes=64)
                 hs[gy] = keep.tile([P, n], U8, name="hs%d" % e, align_bytes=64)
                 nc.vector.quantize_mx(out=hq[gy][:].bitcast(FP8X4), scales=hs[gy][:], in_=hb[gy][:].rearrange("p u d -> p (u d)"))
 
-        def second_product(j, g):
+        def second_product(g, banks):
             for h in range(HALVES):
-                acc = bank(Y_BANKS[HALVES * j + h], (g[1] - g[0]) * C)
+                acc = bank(banks[h], (g[1] - g[0]) * C)
                 for e in range(*g):
                     gw = group_of(W2_GROUPS, e)
                     cols = slice((e - g[0]) * C, (e - g[0] + 1) * C)
@@ -180,79 +176,81 @@ def tile_moe_ogt_relu2_sigmoid_kernel(tc, x_words, x_scales, wg_words, wg_scales
                 else:
                     nc.scalar.copy(y[h][:, g[0] * C : g[1] * C], acc[:])
 
-        by_token = keep.tile([P, TOP, TURNED], F32, name="by_token")
-
-        def turn_gates():
-            turned = bank(7, TOP, P)
-            for r in range(TOP):
-                nc.tensor.transpose(turned[:, r, :], rows[:, r, :], ident[:])
-            nc.scalar.copy(by_token[:], turned[:, :, 0:TURNED])
-
         for e in range(E):
             hidden(e)
-        for j, g in enumerate(Y_GROUPS):
-            second_product(j, g)
+        freed = [SPARE_BANK, turn_bank(E - 4)] + [b for e in range(E - 3, E) for b in (pre_bank(e), turn_bank(e))]
+        y_banks = [[freed[(HALVES * j + h) % len(freed)] for h in range(HALVES)] for j in range(len(Y_GROUPS))]
+        for g, banks in zip(Y_GROUPS, y_banks):
+            second_product(g, banks)
 
-        o = {}
+        turned_rows = bank(y_banks[-2][1], TOP, P)
+        for r in range(TOP):
+            nc.tensor.transpose(turned_rows[:, r, :], gate_rows[:, r, :], ident[:])
+        by_token = keep.tile([P, TOP, BLOCKS], F32, name="by_token")
+        nc.scalar.copy(by_token[:], turned_rows[:, :, 0:BLOCKS])
 
-        def output_gate(b, name, parts):
-            acc = bank(b, len(parts), parts[0][2] - parts[0][1])
-            for j, (h, t0, t1) in enumerate(parts):
+        o = keep.tile([P, HALVES, T], F32, name="o")
+
+        def output_gate(b, halves, t0, t1):
+            acc = bank(b, len(halves), t1 - t0)
+            for j, h in enumerate(halves):
                 for s in range(PASSES):
                     nc.tensor.matmul_mx(
                         out=acc[:, j, :],
                         lhsT=wg[:, s, P * h : P * (h + 1)].bitcast(FP8X4),
                         lhsT_scale=wgs[:, s, P * h : P * (h + 1)],
-                        rhs=xw[s][:, t0:t1].bitcast(FP8X4),
+                        rhs=xw[:, s, t0:t1].bitcast(FP8X4),
                         rhs_scale=xs[:, s, t0:t1],
                         start=(s == 0),
                         stop=(s == PASSES - 1),
                     )
-            o[name] = keep.tile([P, len(parts), parts[0][2] - parts[0][1]], F32, name="o_%s" % name)
-            nc.scalar.activation(o[name][:], acc[:], ACT.Sigmoid)
+            nc.scalar.activation(o[:, halves[0] : halves[-1] + 1, t0:t1], acc[:], ACT.Sigmoid)
+
+        for h in range(HALVES):
+            output_gate(y_banks[-1][h], [h], 0, WIDE)
+        output_gate(y_banks[-1][0], range(HALVES), WIDE, T)
 
         def combine_turned(h):
-            scaled = keep.tile([P, TOP, TURNED, P], F32, name="scaled%d" % h)
+            scaled = keep.tile([P, TOP, BLOCKS, P], F32, name="scaled%d" % h)
             for r in range(TOP):
                 part = keep.tile([P, WIDE], F32, name="part%d_%d" % (h, r))
                 nc.vector.tensor_copy(part[:], y[h][:].indirect(pos[r][:, 0 : WIDE // 16]))
-                turned = bank(1 + (TOP * h + r) % 2, TURNED, P)
-                for b in range(TURNED):
+                turned = bank(PRE_BANKS[1 + (TOP * h + r) % 2], BLOCKS, P)
+                for b in range(BLOCKS):
                     nc.tensor.transpose(turned[:, b, :], part[:, P * b : P * (b + 1)], ident[:])
-                for b in range(TURNED):
+                for b in range(BLOCKS):
                     nc.scalar.activation(scaled[:, r, b, :], turned[:, b, :], ACT.Copy, scale=by_token[:, r, b : b + 1])
-            total = bank(3 + h, TURNED, P)
-            for b in range(TURNED):
+            total = bank(TURN_BANKS[h], BLOCKS, P)
+            for b in range(BLOCKS):
                 for r in range(TOP):
                     nc.tensor.matmul(total[:, b, :], lhsT=scaled[:, r, b, :], rhs=ident[:], is_transpose=True, start=(r == 0), stop=(r == TOP - 1))
             return total[:].rearrange("p b t -> p (b t)")
 
-        def finish_turned(h, total):
-            res = keep.tile([P, WIDE], F32, name="res%d" % h)
-            nc.vector.tensor_tensor(res[:], total, o[h][:, 0, :], ALU.mult)
-            nc.sync.dma_start(out=out[P * h : P * (h + 1), 0:WIDE], in_=res[:])
+        def weighted(h, r, tag):
+            part = keep.tile([P, T - WIDE], F32, name="rest%d_%d" % (h, r), tag=tag)
+            nc.vector.tensor_tensor(part[:], y[h][:].indirect(pos[r][:, WIDE // 16 : T // 16]), gate_rest[:, r, :], ALU.mult)
+            return part
 
-        turn_gates()
-        for h in range(HALVES):
-            output_gate((6, 0)[h], h, [(h, 0, WIDE)])
-        output_gate(6, "rest", [(h, WIDE, T) for h in range(HALVES)])
+        def add(a, b, tag):
+            total = keep.tile([P, T - WIDE], F32, name="sum_%s" % tag, tag=tag)
+            nc.vector.tensor_tensor(total[:], a[:], b[:], ALU.add)
+            return total
+
+        def finish(h, t0, t1, total):
+            res = keep.tile([P, t1 - t0], F32, name="res%d_%d" % (h, t0))
+            nc.vector.tensor_tensor(res[:], total, o[:, h, t0:t1], ALU.mult)
+            nc.sync.dma_start(out=out[P * h : P * (h + 1), t0:t1], in_=res[:])
+
         totals = [combine_turned(h) for h in range(HALVES)]
-        parts = keep.tile([P, TOP - 1, HALVES, T - WIDE], F32, name="parts")
-        last = keep.tile([P, HALVES, T - WIDE], F32, name="last", tag="o_0")
-
-        def weighted(r, into):
-            for h in range(HALVES):
-                nc.vector.tensor_tensor(into[:, h, :], y[h][:].indirect(pos[r][:, WIDE // 16 : T // 16]), gates[:, r, :], ALU.mult)
-
-        weighted(0, parts[:, 0])
-        weighted(1, parts[:, 1])
-        two = keep.tile([P, HALVES, T - WIDE], F32, name="two")
-        nc.vector.tensor_tensor(two[:], parts[:, 0], parts[:, 1], ALU.add)
-        finish_turned(0, totals[0])
-        weighted(2, last)
-        three = keep.tile([P, HALVES, T - WIDE], F32, name="three")
-        nc.vector.tensor_tensor(three[:], two[:], last[:], ALU.add)
-        res = keep.tile([P, HALVES, T - WIDE], F32, name="res_rest")
-        nc.vector.tensor_tensor(res[:], three[:], o["rest"][:], ALU.mult)
-        nc.sync.dma_start(out=out.rearrange("(h p) t -> p h t", p=P)[:, :, WIDE:T], in_=res[:])
-        finish_turned(1, totals[1])
+        first = [weighted(0, r, "first%d" % r) for r in range(TOP)]
+        second = [weighted(1, r, "second%d" % r) for r in range(TOP - 1)]
+        first_two = add(first[0], first[1], "first_two")
+        second_two = add(second[0], second[1], "second_two")
+        first_all = add(first_two, first[2], "first_all")
+        finish(0, 0, WIDE, totals[0])
+        finish(0, WIDE, T, first_all[:])
+        last = weighted(1, TOP - 1, "scaled0")
+        finish(1, 0, WIDE // 2, totals[1][:, 0 : WIDE // 2])
+        second_all = add(second_two, last, "scaled1")
+        finish(1, WIDE // 2, WIDE, totals[1][:, WIDE // 2 : WIDE])
+        finish(1, WIDE, T, second_all[:])

@@ -71,8 +71,6 @@ def tile_moe_ogt_relu2_sigmoid_kernel(tc, x_words, x_scales, wg_words, wg_scales
 
         ident = keep.tile([P, P], F32, name="ident")
         make_identity(nc, ident[:])
-        warm = keep.tile([P, 1], F32, name="warm")
-        nc.scalar.activation(warm[:], ident[:, 0:1], ACT.Sigmoid)
 
         w1s = {g: keep.tile([P, PASSES * (g[1] - g[0]), H], U8, name="w1s_%d" % g[0], align_bytes=64) for g in GROUPS}
         w2s = keep.tile([P, E, N], U8, name="w2s", align_bytes=64)
@@ -189,9 +187,7 @@ def tile_moe_ogt_relu2_sigmoid_kernel(tc, x_words, x_scales, wg_words, wg_scales
         by_token = keep.tile([P, TOP, BLOCKS], F32, name="by_token")
         nc.scalar.copy(by_token[:], turned_rows[:, :, 0:BLOCKS])
 
-        o = keep.tile([P, HALVES, T], F32, name="o")
-
-        def output_gate(b, halves, t0, t1):
+        def gate_product(b, halves, t0, t1):
             acc = bank(b, len(halves), t1 - t0)
             for j, h in enumerate(halves):
                 for s in range(PASSES):
@@ -204,11 +200,16 @@ def tile_moe_ogt_relu2_sigmoid_kernel(tc, x_words, x_scales, wg_words, wg_scales
                         start=(s == 0),
                         stop=(s == PASSES - 1),
                     )
-            nc.scalar.activation(o[:, halves[0] : halves[-1] + 1, t0:t1], acc[:], ACT.Sigmoid)
+            return acc
 
-        for h in range(HALVES):
-            output_gate(y_banks[-1][h], [h], 0, WIDE)
-        output_gate(y_banks[-1][0], range(HALVES), WIDE, T)
+        def sigmoid(acc, shape, tag):
+            o = keep.tile([P, *shape], F32, name="o_%s" % tag, tag=tag)
+            nc.scalar.activation(o[:], acc[:], ACT.Sigmoid)
+            return o
+
+        v_wide = [gate_product(y_banks[-1][h], [h], 0, WIDE) for h in range(HALVES)]
+        v_rest = gate_product(PRE_BANKS[0], range(HALVES), WIDE, T)
+        o_wide = [sigmoid(v_wide[0], (1, WIDE), "gate0")]
 
         def combine_turned(h):
             scaled = keep.tile([P, TOP, BLOCKS, P], F32, name="scaled%d" % h)
@@ -238,10 +239,13 @@ def tile_moe_ogt_relu2_sigmoid_kernel(tc, x_words, x_scales, wg_words, wg_scales
 
         def finish(h, t0, t1, total):
             res = keep.tile([P, t1 - t0], F32, name="res%d_%d" % (h, t0))
-            nc.vector.tensor_tensor(res[:], total, o[:, h, t0:t1], ALU.mult)
+            nc.vector.tensor_tensor(res[:], total, o_wide[h][:, 0, t0:t1] if t0 < WIDE else o_rest[:, h, :], ALU.mult)
             nc.sync.dma_start(out=out[P * h : P * (h + 1), t0:t1], in_=res[:])
 
-        totals = [combine_turned(h) for h in range(HALVES)]
+        totals = [combine_turned(0)]
+        o_wide.append(sigmoid(v_wide[1], (1, WIDE), "part0_%d" % (TOP - 1)))
+        totals.append(combine_turned(1))
+        o_rest = sigmoid(v_rest, (HALVES, T - WIDE), "part1_0")
         first = [weighted(0, r, "first%d" % r) for r in range(TOP)]
         second = [weighted(1, r, "second%d" % r) for r in range(TOP - 1)]
         first_two = add(first[0], first[1], "first_two")

@@ -21,10 +21,27 @@ FP4X4 = mybir.dt.float4_e2m1fn_x4
 ACT = mybir.ActivationFunctionType
 ALU = mybir.AluOpType
 
-GROUPS = [(0, 2), (2, 4), (4, 7), (7, 10), (10, 13), (13, 15)]
-SINGLE_FROM = 7
+GROUPS = [(0, 2), (2, 5), (5, 8), (8, 11), (11, 15)]
+GATHERS = [(0, 1), (1, 2), (2, 3), (3, 6), (6, 9), (9, 12), (12, 15)]
+VECTOR_RELUS = (13, 14)
+WORDS = [(0, 1), (1, 2), (2, 5), (5, 8), (8, 11), (11, 13), (13, 15)]
+RUNS = [(0, 1), (1, 2), (2, 5), (5, 8), (8, 11), (11, 15)]
+HOLD = False
+PLANES = (4, 3, 3)
+PLANE_OF = (0, 1, 2, 1, 0)
+EARLY = 3
+EARLY_WORDS = 4
+WARM = True
+QTAGS = ("hq0", "xg0", "w1_13", "hq12", "hq14")
+Y_BANKS = ((2, 0, 1, 7, 6), (6, 7, 1, 0, 2))
+ROWS_BANK = 3
+TURNED = (0, 7)
+TOTALS = (2, 6)
+V_BANKS = (4, 1, 4)
+V_COPIES = (0, 12, 14)
+SINGLE_FROM = 0
 Y_GROUPS = [(0, 4), (4, 8), (8, 12), (12, 14), (14, 15)]
-W2_GROUPS = [(0, 8), (8, 15)]
+W2_GROUPS = [(0, 4), (4, 8), (8, 14), (14, 15)]
 PRE_BANKS = (0, 1, 2)
 TURN_BANKS = (3, 4, 5, 6)
 SPARE_BANK = 7
@@ -37,7 +54,7 @@ def group_of(groups, e):
 
 
 def pre_bank(e):
-    return PRE_BANKS[e % len(PRE_BANKS)]
+    return SPARE_BANK if e == E - 1 else PRE_BANKS[e % len(PRE_BANKS)]
 
 
 def turn_bank(e):
@@ -62,130 +79,61 @@ def tile_moe_ogt_relu2_sigmoid_kernel(tc, x_words, x_scales, wg_words, wg_scales
                 nc.sync.dma_start(out=tile[r:P:32].bitcast(I32), in_=rows[r:16:4].bitcast(I32))
 
         xs = keep.tile([P, PASSES, T], U8, name="xs", align_bytes=64)
-        zero(xs)
+        nc.gpsimd.memset(xs[:].rearrange("p m w -> p (m w)").bitcast(I32), 0)
+        slot_list = keep.tile([P, S // 16], U16, name="slot_list")
+        nc.sync.dma_start(slot_list[:], offs)
         load_scale_rows(xs, x_scales.rearrange("s b t -> b s t"))
         xw = keep.tile([P, PASSES, T], I32, name="xw", align_bytes=64)
         nc.sync.dma_start(out=xw[:], in_=x_words.rearrange("s p t d -> p s (t d)").bitcast(I32))
-        slot_list = keep.tile([P, S // 16], U16, name="slot_list")
-        nc.sync.dma_start(slot_list[:], offs)
 
         ident = keep.tile([P, P], F32, name="ident")
         make_identity(nc, ident[:])
+        warm = keep.tile([P, 1], F32, name="warm")
+        nc.scalar.activation(warm[:], ident[:, 0:1], ACT.Sigmoid)
 
-        w1s = {g: keep.tile([P, PASSES * (g[1] - g[0]), H], U8, name="w1s_%d" % g[0], align_bytes=64) for g in GROUPS}
-        w2s = keep.tile([P, E, N], U8, name="w2s", align_bytes=64)
+        planes = [keep.tile([P, PASSES * n, H], U8, name="plane%d" % j, align_bytes=64) for j, n in enumerate(PLANES)]
+        small = keep.tile([P, E, N], U8, name="small", align_bytes=64)
         wgs = keep.tile([P, PASSES, N], U8, name="wgs", align_bytes=64)
-        gate_rows = keep.tile([P, TOP, P], F32, name="gate_rows")
-        for tile in [w1s[g] for g in GROUPS] + [w2s, wgs, gate_rows]:
+        gate_rows = keep.tile([P, 1, P], F32, name="gate_rows")
+        for tile in planes + [wgs, gate_rows, small]:
             zero(tile)
+        w1s = {g: planes[j][:, 0 : PASSES * (g[1] - g[0]), :] for j, g in zip(PLANE_OF, GROUPS)}
+        w2s = {(0, E): small[:]}
 
         def slots(a, b):
             return slot_list[:, a * C // 16 : b * C // 16]
 
         xg, sg = {}, {}
-        for g in GROUPS:
-            for s in range(PASSES):
-                sg[g, s] = keep.tile([P, (g[1] - g[0]) * C], U8, name="sg%d_%d" % (g[0], s), align_bytes=64)
-                nc.vector.tensor_copy(sg[g, s][:], xs[:, s, :].indirect(slots(*g)))
-            for s in range(PASSES):
-                xg[g, s] = keep.tile([P, (g[1] - g[0]) * C], U32, name="xg%d_%d" % (g[0], s), align_bytes=64)
-            for a, b in [(e, e + 1) for e in range(*g)] if g[0] >= SINGLE_FROM else [g]:
-                for s in range(PASSES):
-                    nc.vector.tensor_copy(xg[g, s][:, (a - g[0]) * C : (b - g[0]) * C], xw[:, s, :].bitcast(U32).indirect(slots(a, b)))
 
-        w1, w2, pos = {}, {}, []
+        def gather_scales(g, scales):
+            for s in range(PASSES):
+                nc.vector.tensor_copy(scales[:, s, :], xs[:, s, :].indirect(slots(*g)))
+            for e in range(*g):
+                sg[e] = scales[:, :, (e - g[0]) * C : (e - g[0] + 1) * C]
 
-        def load_w1(g):
-            w1[g] = keep.tile([P, (g[1] - g[0]) * PASSES, 2 * H], U8, name="w1_%d" % g[0], align_bytes=64)
-            nc.sync.dma_start(out=w1[g][:].bitcast(I32), in_=w1_words.rearrange("e s p b -> p (e s) b")[:, PASSES * g[0] : PASSES * g[1], :].bitcast(I32))
+        def gather_words(e, words):
+            xg[e] = words
+            for s in range(PASSES):
+                nc.vector.tensor_copy(words[:, s, :], xw[:, s, :].bitcast(U32).indirect(slots(e, e + 1)))
+
+        for e in range(EARLY_WORDS):
+            if e < EARLY:
+                gather_scales((e, e + 1), keep.tile([P, PASSES, C], U8, name="sg%d" % e, align_bytes=64)[:])
+            gather_words(e, keep.tile([P, PASSES, C], U32, name="xg%d" % e, align_bytes=64)[:])
+
+        w1, w2 = {}, {}
+
+        def load_w1(a, b):
+            tile = keep.tile([P, (b - a) * PASSES, 2 * H], U8, name="w1_%d" % a, tag="w1_%d" % a, align_bytes=64)
+            nc.sync.dma_start(out=tile[:].bitcast(I32), in_=w1_words.rearrange("e s p b -> p (e s) b")[:, PASSES * a : PASSES * b, :].bitcast(I32))
+            for e in range(a, b):
+                w1[e] = tile[:, (e - a) * PASSES : (e - a + 1) * PASSES, :]
 
         def load_w1_scales(g):
             load_scale_rows(w1s[g], w1_scales.rearrange("e s b i -> b (e s) i")[:, PASSES * g[0] : PASSES * g[1], :])
 
-        load_w1(GROUPS[0])
-        load_w1_scales(GROUPS[0])
-        for g in GROUPS[1:-1]:
-            load_w1_scales(g)
-            load_w1(g)
-        for r, src in enumerate((pos1, pos2, pos3)):
-            pos.append(keep.tile([P, T // 16], U16, name="pos%d" % r))
-            nc.sync.dma_start(pos[r][:], src)
-        load_scale_rows(w2s, w2_scales.rearrange("e s b n -> b (e s) n"))
-        load_w1_scales(GROUPS[-1])
-        load_w1(GROUPS[-1])
-        for g in W2_GROUPS:
-            w2[g] = keep.tile([P, g[1] - g[0], 2 * N], U8, name="w2_%d" % g[0], align_bytes=64)
-            nc.sync.dma_start(out=w2[g][:].bitcast(I32), in_=w2_words.rearrange("e s p b -> p (e s) b")[:, g[0] : g[1], :].bitcast(I32))
-        wg = keep.tile([P, PASSES, N], I32, name="wg", align_bytes=64)
-        nc.sync.dma_start(out=wg[:], in_=wg_words.rearrange("s p n d -> p s (n d)").bitcast(I32))
-        load_scale_rows(wgs, wg_scales.rearrange("s b n -> b s n"))
-        nc.sync.dma_start(out=gate_rows[0:BLOCKS], in_=gate[:, 0, 0:WIDE].rearrange("r (b p) -> b r p", p=P))
-        gate_rest = keep.tile([P, TOP, T - WIDE], F32, name="gate_rest")
-        nc.sync.dma_start(out=gate_rest[:], in_=gate[:, :, WIDE:T].rearrange("r p t -> p r t"))
-
-        y = [keep.tile([P, S], F32, name="y%d" % h) for h in range(HALVES)]
-        hb, hq, hs = {}, {}, {}
-
-        def hidden(e):
-            g, gy = group_of(GROUPS, e), group_of(Y_GROUPS, e)
-            cols = slice((e - g[0]) * C, (e - g[0] + 1) * C)
-            pre = bank(pre_bank(e), H)
-            for s in range(PASSES):
-                nc.tensor.matmul_mx(
-                    out=pre[:],
-                    lhsT=xg[g, s][:, cols].bitcast(FP8X4),
-                    lhsT_scale=sg[g, s][:, cols],
-                    rhs=w1[g][:, (e - g[0]) * PASSES + s, :].bitcast(FP4X4),
-                    rhs_scale=w1s[g][:, (e - g[0]) * PASSES + s, :],
-                    start=(s == 0),
-                    stop=(s == PASSES - 1),
-                )
-            relu = ring.tile([P, 4, P], F32, name="relu")
-            nc.scalar.activation(relu[:], pre[:].rearrange("u (p d) -> u d p", d=4), ACT.Relu)
-            turned = bank(turn_bank(e), 4, C)
-            for d in range(4):
-                nc.tensor.transpose(turned[:, d, :], relu[:, d, :], ident[:])
-            n = (gy[1] - gy[0]) * C
-            if e == gy[0]:
-                hb[gy] = keep.tile([P, n, 4], BF16, name="hb%d" % e, align_bytes=64)
-            nc.scalar.activation(hb[gy][:, (e - gy[0]) * C : (e - gy[0] + 1) * C, :], turned[:].rearrange("p d u -> p u d"), ACT.Square)
-            if e == gy[1] - 1:
-                hq[gy] = keep.tile([P, n], U32, name="hq%d" % e, align_bytes=64)
-                hs[gy] = keep.tile([P, n], U8, name="hs%d" % e, align_bytes=64)
-                nc.vector.quantize_mx(out=hq[gy][:].bitcast(FP8X4), scales=hs[gy][:], in_=hb[gy][:].rearrange("p u d -> p (u d)"))
-
-        def second_product(g, banks):
-            for h in range(HALVES):
-                acc = bank(banks[h], (g[1] - g[0]) * C)
-                for e in range(*g):
-                    gw = group_of(W2_GROUPS, e)
-                    cols = slice((e - g[0]) * C, (e - g[0] + 1) * C)
-                    nc.tensor.matmul_mx(
-                        out=acc[:, cols],
-                        lhsT=w2[gw][:, e - gw[0], 2 * P * h : 2 * P * (h + 1)].bitcast(FP4X4),
-                        lhsT_scale=w2s[:, e, P * h : P * (h + 1)],
-                        rhs=hq[g][:, cols].bitcast(FP8X4),
-                        rhs_scale=hs[g][:, cols],
-                        start=True,
-                        stop=True,
-                    )
-                if h == 0:
-                    nc.vector.tensor_copy(y[h][:, g[0] * C : g[1] * C], acc[:])
-                else:
-                    nc.scalar.copy(y[h][:, g[0] * C : g[1] * C], acc[:])
-
-        for e in range(E):
-            hidden(e)
-        freed = [SPARE_BANK, turn_bank(E - 4)] + [b for e in range(E - 3, E) for b in (pre_bank(e), turn_bank(e))]
-        y_banks = [[freed[(HALVES * j + h) % len(freed)] for h in range(HALVES)] for j in range(len(Y_GROUPS))]
-        for g, banks in zip(Y_GROUPS, y_banks):
-            second_product(g, banks)
-
-        turned_rows = bank(y_banks[-2][1], TOP, P)
-        for r in range(TOP):
-            nc.tensor.transpose(turned_rows[:, r, :], gate_rows[:, r, :], ident[:])
-        by_token = keep.tile([P, TOP, BLOCKS], F32, name="by_token")
-        nc.scalar.copy(by_token[:], turned_rows[:, :, 0:BLOCKS])
+        def load_w2_scales(g):
+            load_scale_rows(w2s[g], w2_scales.rearrange("e s b n -> b (e s) n")[:, g[0] : g[1], :])
 
         def gate_product(b, halves, t0, t1):
             acc = bank(b, len(halves), t1 - t0)
@@ -207,54 +155,179 @@ def tile_moe_ogt_relu2_sigmoid_kernel(tc, x_words, x_scales, wg_words, wg_scales
             nc.scalar.activation(o[:], acc[:], ACT.Sigmoid)
             return o
 
-        v_wide = [gate_product(y_banks[-1][h], [h], 0, WIDE) for h in range(HALVES)]
-        v_rest = gate_product(PRE_BANKS[0], range(HALVES), WIDE, T)
-        o_wide = [sigmoid(v_wide[0], (1, WIDE), "gate0")]
+        y = [keep.tile([P, S], F32, name="y%d" % h) for h in range(HALVES)]
+        hb, hq, hs = {}, {}, {}
 
-        def combine_turned(h):
-            scaled = keep.tile([P, TOP, BLOCKS, P], F32, name="scaled%d" % h)
-            for r in range(TOP):
-                part = keep.tile([P, WIDE], F32, name="part%d_%d" % (h, r))
-                nc.vector.tensor_copy(part[:], y[h][:].indirect(pos[r][:, 0 : WIDE // 16]))
-                turned = bank(PRE_BANKS[1 + (TOP * h + r) % 2], BLOCKS, P)
-                for b in range(BLOCKS):
-                    nc.tensor.transpose(turned[:, b, :], part[:, P * b : P * (b + 1)], ident[:])
-                for b in range(BLOCKS):
-                    nc.scalar.activation(scaled[:, r, b, :], turned[:, b, :], ACT.Copy, scale=by_token[:, r, b : b + 1])
-            total = bank(TURN_BANKS[h], BLOCKS, P)
+        relus = {}
+
+        def first_product(e):
+            gl = group_of(GROUPS, e)
+            pre = bank(pre_bank(e), H)
+            for s in range(PASSES):
+                nc.tensor.matmul_mx(
+                    out=pre[:],
+                    lhsT=xg[e][:, s, :].bitcast(FP8X4),
+                    lhsT_scale=sg[e][:, s, :],
+                    rhs=w1[e][:, s, :].bitcast(FP4X4),
+                    rhs_scale=w1s[gl][:, (e - gl[0]) * PASSES + s, :],
+                    start=(s == 0),
+                    stop=(s == PASSES - 1),
+                )
+            relu = relus[e] = ring.tile([P, 4, P], F32, name="relu")
+            if e in VECTOR_RELUS:
+                nc.vector.tensor_scalar_max(relu[:], pre[:].rearrange("u (p d) -> u d p", d=4), 0.0)
+            else:
+                nc.scalar.activation(relu[:], pre[:].rearrange("u (p d) -> u d p", d=4), ACT.Relu)
+
+        def square(e):
+            gy, relu = group_of(Y_GROUPS, e), relus[e]
+            turned = bank(turn_bank(e), 4, C)
+            for d in range(4):
+                nc.tensor.transpose(turned[:, d, :], relu[:, d, :], ident[:])
+            n = (gy[1] - gy[0]) * C
+            if e == gy[0]:
+                hb[gy] = keep.tile([P, n, 4], BF16, name="hb%d" % e, align_bytes=64)
+            nc.scalar.activation(hb[gy][:, (e - gy[0]) * C : (e - gy[0] + 1) * C, :], turned[:].rearrange("p d u -> p u d"), ACT.Square)
+
+        def quantize(gy, tag):
+            n = (gy[1] - gy[0]) * C
+            hq[gy] = keep.tile([P, n], U32, name="hq%d" % gy[0], tag=tag, align_bytes=64)
+            hs[gy] = keep.tile([P, n], U8, name="hs%d" % gy[0], align_bytes=64)
+            nc.vector.quantize_mx(out=hq[gy][:].bitcast(FP8X4), scales=hs[gy][:], in_=hb[gy][:].rearrange("p u d -> p (u d)"))
+
+        def second_product(g, h, b):
+            if b >= 0:
+                acc = bank(b, (g[1] - g[0]) * C)
+                for e in range(*g):
+                    gw, gs = group_of(W2_GROUPS, e), group_of(list(w2s), e)
+                    cols = slice((e - g[0]) * C, (e - g[0] + 1) * C)
+                    nc.tensor.matmul_mx(
+                        out=acc[:, cols],
+                        lhsT=w2[gw][:, e - gw[0], 2 * P * h : 2 * P * (h + 1)].bitcast(FP4X4),
+                        lhsT_scale=w2s[gs][:, e - gs[0], P * h : P * (h + 1)],
+                        rhs=hq[g][:, cols].bitcast(FP8X4),
+                        rhs_scale=hs[g][:, cols],
+                        start=True,
+                        stop=True,
+                    )
+                if h == 0 and g[0] in V_COPIES:
+                    nc.vector.tensor_copy(y[h][:, g[0] * C : g[1] * C], acc[:])
+                else:
+                    nc.scalar.copy(y[h][:, g[0] * C : g[1] * C], acc[:])
+
+        def load_group(g):
+            load_w1_scales(g)
+            for w in WORDS:
+                if g[0] < w[1] <= g[1] and w[0] not in w1:
+                    load_w1(*w)
+
+        pos = [keep.tile([P, T // 16], U16, name="pos%d" % r) for r in range(TOP)]
+        load_w1(*WORDS[0])
+        load_group(GROUPS[0])
+        load_group(GROUPS[1])
+        nc.sync.dma_start(pos[0][:], pos1)
+        load_group(GROUPS[2])
+        nc.sync.dma_start(pos[1][:], pos2)
+        first_product(0)
+        square(0)
+        words = keep.tile([P, PASSES, (E - EARLY_WORDS) * C], U32, name="xg_late", tag="xg0", align_bytes=64)
+        scales = keep.tile([P, PASSES, (E - EARLY) * C], U8, name="sg_late", tag="sg0", align_bytes=64)
+        for g in GATHERS[EARLY:]:
+            gather_scales(g, scales[:, :, (g[0] - EARLY) * C : (g[1] - EARLY) * C])
+            for e in range(max(g[0], EARLY_WORDS), g[1]):
+                gather_words(e, words[:, :, (e - EARLY_WORDS) * C : (e - EARLY_WORDS + 1) * C])
+
+        def run(g, last=None):
+            for e in range(*g):
+                first_product(e)
+            for e in range(g[0], last or g[1]):
+                square(e)
+
+        for g in RUNS[1:3]:
+            run(g)
+        load_group(GROUPS[3])
+        nc.sync.dma_start(pos[2][:], pos3)
+        load_w1_scales(GROUPS[4])
+        load_w1(11, 13)
+        load_w1(13, 15)
+        load_scale_rows(wgs, wg_scales.rearrange("s b n -> b s n"))
+        run(RUNS[3])
+
+        def load_w2(g):
+            w2[g] = keep.tile([P, g[1] - g[0], 2 * N], U8, name="w2_%d" % g[0], align_bytes=64)
+            nc.sync.dma_start(out=w2[g][:].bitcast(I32), in_=w2_words.rearrange("e s p b -> p (e s) b")[:, g[0] : g[1], :].bitcast(I32))
+
+        load_w2(W2_GROUPS[0])
+        for g in w2s:
+            load_w2_scales(g)
+        load_w2(W2_GROUPS[1])
+        nc.sync.dma_start(out=gate_rows[0 : TOP * BLOCKS, 0, :], in_=gate[:, 0, 0:WIDE].rearrange("r (b p) -> r b p", p=P))
+        for g in W2_GROUPS[2:]:
+            load_w2(g)
+        run(RUNS[4])
+        wg = keep.tile([P, PASSES, N], I32, name="wg", align_bytes=64)
+        nc.sync.dma_start(out=wg[:], in_=wg_words.rearrange("s p n d -> p s (n d)").bitcast(I32))
+        gate_rest = keep.tile([P, TOP, T - WIDE], F32, name="gate_rest")
+        nc.sync.dma_start(out=gate_rest[:], in_=gate[:, :, WIDE:T].rearrange("r p t -> p r t"))
+        run(RUNS[5], E - 1)
+        if not HOLD:
+            square(E - 1)
+        for j, g in enumerate(Y_GROUPS):
+            quantize(g, QTAGS[j])
+        for h in range(HALVES):
+            for j, g in enumerate(Y_GROUPS):
+                second_product(g, h, Y_BANKS[h][j])
+
+        turned_rows = bank(ROWS_BANK, P)
+        nc.tensor.transpose(turned_rows[:], gate_rows[:, 0, :], ident[:])
+        by_token = keep.tile([P, TOP * BLOCKS], F32, name="by_token")
+        nc.scalar.copy(by_token[:], turned_rows[:, 0 : TOP * BLOCKS])
+
+        scaled = [keep.tile([P, TOP, BLOCKS, P], F32, name="scaled%d" % h) for h in range(HALVES)]
+        totals = {}
+
+        def turn(h, r):
+            part = keep.tile([P, WIDE], F32, name="part%d_%d" % (h, r))
+            nc.vector.tensor_copy(part[:], y[h][:].indirect(pos[r][:, 0 : WIDE // 16]))
+            turned = bank(TURNED[(TOP * h + r) % len(TURNED)], BLOCKS, P)
             for b in range(BLOCKS):
-                for r in range(TOP):
-                    nc.tensor.matmul(total[:, b, :], lhsT=scaled[:, r, b, :], rhs=ident[:], is_transpose=True, start=(r == 0), stop=(r == TOP - 1))
-            return total[:].rearrange("p b t -> p (b t)")
+                nc.tensor.transpose(turned[:, b, :], part[:, P * b : P * (b + 1)], ident[:])
+            for b in range(BLOCKS):
+                nc.scalar.activation(scaled[h][:, r, b, :], turned[:, b, :], ACT.Copy, scale=by_token[:, BLOCKS * r + b : BLOCKS * r + b + 1])
 
-        def weighted(h, r, tag):
-            part = keep.tile([P, T - WIDE], F32, name="rest%d_%d" % (h, r), tag=tag)
-            nc.vector.tensor_tensor(part[:], y[h][:].indirect(pos[r][:, WIDE // 16 : T // 16]), gate_rest[:, r, :], ALU.mult)
-            return part
+        def turn_back(h, r):
+            if r == 0:
+                totals[h] = bank(TOTALS[h], WIDE)
+            for b in range(BLOCKS):
+                nc.tensor.matmul(totals[h][:, P * b : P * (b + 1)], lhsT=scaled[h][:, r, b, :], rhs=ident[:], is_transpose=True, start=(r == 0 and b == 0), stop=(r == TOP - 1 and b == BLOCKS - 1))
 
-        def add(a, b, tag):
-            total = keep.tile([P, T - WIDE], F32, name="sum_%s" % tag, tag=tag)
-            nc.vector.tensor_tensor(total[:], a[:], b[:], ALU.add)
-            return total
+        def finish(h):
+            res = keep.tile([P, WIDE], F32, name="res%d" % h)
+            nc.vector.tensor_tensor(res[:], totals[h][:], o_wide[h][:, 0, :], ALU.mult)
+            nc.sync.dma_start(out=out[P * h : P * (h + 1), 0:WIDE], in_=res[:])
 
-        def finish(h, t0, t1, total):
-            res = keep.tile([P, t1 - t0], F32, name="res%d_%d" % (h, t0))
-            nc.vector.tensor_tensor(res[:], total, o_wide[h][:, 0, t0:t1] if t0 < WIDE else o_rest[:, h, :], ALU.mult)
-            nc.sync.dma_start(out=out[P * h : P * (h + 1), t0:t1], in_=res[:])
-
-        totals = [combine_turned(0)]
-        o_wide.append(sigmoid(v_wide[1], (1, WIDE), "part0_%d" % (TOP - 1)))
-        totals.append(combine_turned(1))
-        o_rest = sigmoid(v_rest, (HALVES, T - WIDE), "part1_0")
-        first = [weighted(0, r, "first%d" % r) for r in range(TOP)]
-        second = [weighted(1, r, "second%d" % r) for r in range(TOP - 1)]
-        first_two = add(first[0], first[1], "first_two")
-        second_two = add(second[0], second[1], "second_two")
-        first_all = add(first_two, first[2], "first_all")
-        finish(0, 0, WIDE, totals[0])
-        finish(0, WIDE, T, first_all[:])
-        last = weighted(1, TOP - 1, "scaled0")
-        finish(1, 0, WIDE // 2, totals[1][:, 0 : WIDE // 2])
-        second_all = add(second_two, last, "scaled1")
-        finish(1, WIDE // 2, WIDE, totals[1][:, WIDE // 2 : WIDE])
-        finish(1, WIDE, T, second_all[:])
+        steps = [(h, r) for h in range(HALVES) for r in range(TOP)]
+        o_wide = []
+        for j, step in enumerate(steps):
+            turn(*step)
+            if j > 0:
+                turn_back(*steps[j - 1])
+            if j in (1, 2):
+                o_wide.append(sigmoid(gate_product(V_BANKS[j - 1], [j - 1], 0, WIDE), (1, WIDE), "part0_%d" % j))
+            if j == 3:
+                o_rest = sigmoid(gate_product(V_BANKS[2], range(HALVES), WIDE, T), (HALVES, T - WIDE), "part0_0")
+        turn_back(*steps[-1])
+        rest = keep.tile([P, TOP, HALVES, T - WIDE], F32, name="rest", tag="part1_0")
+        for r in range(TOP):
+            for h in range(HALVES):
+                nc.vector.tensor_tensor(rest[:, r, h, :], y[h][:].indirect(pos[r][:, WIDE // 16 : T // 16]), gate_rest[:, r, :], ALU.mult)
+            if r == 1:
+                two = keep.tile([P, HALVES, T - WIDE], F32, name="two")
+                nc.vector.tensor_tensor(two[:], rest[:, 0], rest[:, 1], ALU.add)
+        finish(0)
+        three = keep.tile([P, HALVES, T - WIDE], F32, name="three", tag="scaled0")
+        nc.vector.tensor_tensor(three[:], two[:], rest[:, 2], ALU.add)
+        finish(1)
+        res = keep.tile([P, HALVES, T - WIDE], F32, name="res_rest", tag="scaled1")
+        nc.vector.tensor_tensor(res[:], three[:], o_rest[:], ALU.mult)
+        nc.sync.dma_start(out=out[:, WIDE:T].rearrange("(h p) t -> p h t", p=P), in_=res[:])

@@ -21,27 +21,28 @@ FP4X4 = mybir.dt.float4_e2m1fn_x4
 ACT = mybir.ActivationFunctionType
 ALU = mybir.AluOpType
 
-GROUPS = [(0, 2), (2, 5), (5, 8), (8, 11), (11, 15)]
+GROUPS = [(0, 3), (3, 6), (6, 9), (9, 12), (12, 15)]
 GATHERS = [(0, 1), (1, 2), (2, 3), (3, 6), (6, 9), (9, 12), (12, 15)]
-VECTOR_RELUS = (13, 14)
-WORDS = [(0, 1), (1, 2), (2, 5), (5, 8), (8, 11), (11, 13), (13, 15)]
+VECTOR_RELUS = (14,)
+WORDS = [(0, 1), (1, 3), (3, 6), (6, 9), (9, 12), (12, 15)]
 RUNS = [(0, 1), (1, 2), (2, 5), (5, 8), (8, 11), (11, 15)]
 HOLD = False
-PLANES = (4, 3, 3)
-PLANE_OF = (0, 1, 2, 1, 0)
+PLANES = [g[1] - g[0] for g in GROUPS]
+PLANE_OF = range(len(GROUPS))
+NPRE = 3
 EARLY = 3
 EARLY_WORDS = 4
 WARM = True
-QTAGS = ("hq0", "xg0", "w1_13", "hq12", "hq14")
-Y_BANKS = ((2, 0, 1, 7, 6), (6, 7, 1, 0, 2))
+QTAGS = ("hq0", "xg0", "w1_%d" % WORDS[-1][0], "hq12", "hq14")
+Y_BANKS = ((7, 6, 0, 1, 2), (2, 1, 0, 6, 7))
 ROWS_BANK = 3
-TURNED = (0, 7)
-TOTALS = (2, 6)
-V_BANKS = (4, 1, 4)
+TURNED = (6, 1)
+TOTALS = (7, 2)
+V_BANKS = (4, 0, 4)
 V_COPIES = (0, 12, 14)
 SINGLE_FROM = 0
 Y_GROUPS = [(0, 4), (4, 8), (8, 12), (12, 14), (14, 15)]
-W2_GROUPS = [(0, 4), (4, 8), (8, 14), (14, 15)]
+W2_GROUPS = [(0, 4), (4, 8), (8, 12), (12, 15)]
 PRE_BANKS = (0, 1, 2)
 TURN_BANKS = (3, 4, 5, 6)
 SPARE_BANK = 7
@@ -54,7 +55,7 @@ def group_of(groups, e):
 
 
 def pre_bank(e):
-    return SPARE_BANK if e == E - 1 else PRE_BANKS[e % len(PRE_BANKS)]
+    return SPARE_BANK if e == E - 1 and GROUPS[-1][1] - GROUPS[-1][0] > 3 else PRE_BANKS[e % len(PRE_BANKS)]
 
 
 def turn_bank(e):
@@ -74,8 +75,8 @@ def tile_moe_ogt_relu2_sigmoid_kernel(tc, x_words, x_scales, wg_words, wg_scales
         def zero(tile):
             nc.vector.memset(tile[:].rearrange("p m w -> p (m w)").bitcast(I32), 0)
 
-        def load_scale_rows(tile, rows):
-            for r in range(4):
+        def load_scale_rows(tile, rows, which=range(4)):
+            for r in which:
                 nc.sync.dma_start(out=tile[r:P:32].bitcast(I32), in_=rows[r:16:4].bitcast(I32))
 
         xs = keep.tile([P, PASSES, T], U8, name="xs", align_bytes=64)
@@ -223,13 +224,11 @@ def tile_moe_ogt_relu2_sigmoid_kernel(tc, x_words, x_scales, wg_words, wg_scales
 
         pos = [keep.tile([P, T // 16], U16, name="pos%d" % r) for r in range(TOP)]
         load_w1(*WORDS[0])
-        load_group(GROUPS[0])
-        load_group(GROUPS[1])
-        nc.sync.dma_start(pos[0][:], pos1)
-        load_group(GROUPS[2])
-        nc.sync.dma_start(pos[1][:], pos2)
+        for j, g in enumerate(GROUPS):
+            load_group(g)
+            if j > 0:
+                load_scale_rows(wgs, wg_scales.rearrange("s b n -> b s n"), [j - 1])
         first_product(0)
-        square(0)
         words = keep.tile([P, PASSES, (E - EARLY_WORDS) * C], U32, name="xg_late", tag="xg0", align_bytes=64)
         scales = keep.tile([P, PASSES, (E - EARLY) * C], U8, name="sg_late", tag="sg0", align_bytes=64)
         for g in GATHERS[EARLY:]:
@@ -243,15 +242,10 @@ def tile_moe_ogt_relu2_sigmoid_kernel(tc, x_words, x_scales, wg_words, wg_scales
             for e in range(g[0], last or g[1]):
                 square(e)
 
-        for g in RUNS[1:3]:
-            run(g)
-        load_group(GROUPS[3])
-        nc.sync.dma_start(pos[2][:], pos3)
-        load_w1_scales(GROUPS[4])
-        load_w1(11, 13)
-        load_w1(13, 15)
-        load_scale_rows(wgs, wg_scales.rearrange("s b n -> b s n"))
-        run(RUNS[3])
+        for e in range(1, GROUPS[0][1]):
+            first_product(e)
+        for e in range(*GROUPS[0]):
+            square(e)
 
         def load_w2(g):
             w2[g] = keep.tile([P, g[1] - g[0], 2 * N], U8, name="w2_%d" % g[0], align_bytes=64)
@@ -261,17 +255,17 @@ def tile_moe_ogt_relu2_sigmoid_kernel(tc, x_words, x_scales, wg_words, wg_scales
         for g in w2s:
             load_w2_scales(g)
         load_w2(W2_GROUPS[1])
-        nc.sync.dma_start(out=gate_rows[0 : TOP * BLOCKS, 0, :], in_=gate[:, 0, 0:WIDE].rearrange("r (b p) -> r b p", p=P))
         for g in W2_GROUPS[2:]:
             load_w2(g)
-        run(RUNS[4])
+        for r, src in enumerate((pos1, pos2, pos3)):
+            nc.sync.dma_start(pos[r][:], src)
+        nc.sync.dma_start(out=gate_rows[0 : TOP * BLOCKS, 0, :], in_=gate[:, 0, 0:WIDE].rearrange("r (b p) -> r b p", p=P))
         wg = keep.tile([P, PASSES, N], I32, name="wg", align_bytes=64)
         nc.sync.dma_start(out=wg[:], in_=wg_words.rearrange("s p n d -> p s (n d)").bitcast(I32))
         gate_rest = keep.tile([P, TOP, T - WIDE], F32, name="gate_rest")
         nc.sync.dma_start(out=gate_rest[:], in_=gate[:, :, WIDE:T].rearrange("r p t -> p r t"))
-        run(RUNS[5], E - 1)
-        if not HOLD:
-            square(E - 1)
+        for g in GROUPS[1:]:
+            run(g)
         for j, g in enumerate(Y_GROUPS):
             quantize(g, QTAGS[j])
         for h in range(HALVES):

@@ -27,11 +27,14 @@ VECTOR_RELUS = (14,)
 WORDS = [(0, 1), (1, 3), (3, 6), (6, 9), (9, 12), (12, 15)]
 RUNS = [(0, 1), (1, 2), (2, 5), (5, 8), (8, 11), (11, 15)]
 HOLD = False
-PLANES = [g[1] - g[0] for g in GROUPS]
-PLANE_OF = range(len(GROUPS))
+PLANES = (3, 3, 3)
+PLANE_OF = (0, 1, 2, 0, 1)
 NPRE = 3
-EARLY = 3
-EARLY_WORDS = 4
+FIRST_SCALES = [(0, 3)]
+FIRST_WORDS = [(0, 1), (1, 4)]
+LATE_WORDS = [(4, 6), (6, 9), (9, 12), (12, 14), (14, 15)]
+EARLY = FIRST_SCALES[-1][1]
+EARLY_WORDS = FIRST_WORDS[-1][1]
 WARM = True
 QTAGS = ("hq0", "xg0", "w1_%d" % WORDS[-1][0], "hq12", "hq14")
 Y_BANKS = ((7, 6, 0, 1, 2), (2, 1, 0, 6, 7))
@@ -112,15 +115,16 @@ def tile_moe_ogt_relu2_sigmoid_kernel(tc, x_words, x_scales, wg_words, wg_scales
             for e in range(*g):
                 sg[e] = scales[:, :, (e - g[0]) * C : (e - g[0] + 1) * C]
 
-        def gather_words(e, words):
-            xg[e] = words
+        def gather_words(a, b, words):
+            for e in range(a, b):
+                xg[e] = words[:, :, (e - a) * C : (e - a + 1) * C]
             for s in range(PASSES):
-                nc.vector.tensor_copy(words[:, s, :], xw[:, s, :].bitcast(U32).indirect(slots(e, e + 1)))
+                nc.vector.tensor_copy(words[:, s, :], xw[:, s, :].bitcast(U32).indirect(slots(a, b)))
 
-        for e in range(EARLY_WORDS):
-            if e < EARLY:
-                gather_scales((e, e + 1), keep.tile([P, PASSES, C], U8, name="sg%d" % e, align_bytes=64)[:])
-            gather_words(e, keep.tile([P, PASSES, C], U32, name="xg%d" % e, align_bytes=64)[:])
+        for g in FIRST_SCALES:
+            gather_scales(g, keep.tile([P, PASSES, (g[1] - g[0]) * C], U8, name="sg%d" % g[0], align_bytes=64)[:])
+        for g in FIRST_WORDS:
+            gather_words(*g, keep.tile([P, PASSES, (g[1] - g[0]) * C], U32, name="xg%d" % g[0], align_bytes=64)[:])
 
         w1, w2 = {}, {}
 
@@ -224,17 +228,22 @@ def tile_moe_ogt_relu2_sigmoid_kernel(tc, x_words, x_scales, wg_words, wg_scales
 
         pos = [keep.tile([P, T // 16], U16, name="pos%d" % r) for r in range(TOP)]
         load_w1(*WORDS[0])
-        for j, g in enumerate(GROUPS):
-            load_group(g)
-            if j > 0:
-                load_scale_rows(wgs, wg_scales.rearrange("s b n -> b s n"), [j - 1])
+
+        def later_loads(j):
+            load_group(GROUPS[j])
+            load_scale_rows(wgs, wg_scales.rearrange("s b n -> b s n"), [j - 1])
+
+        load_group(GROUPS[0])
+        later_loads(1)
+        later_loads(2)
         first_product(0)
         words = keep.tile([P, PASSES, (E - EARLY_WORDS) * C], U32, name="xg_late", tag="xg0", align_bytes=64)
-        scales = keep.tile([P, PASSES, (E - EARLY) * C], U8, name="sg_late", tag="sg0", align_bytes=64)
-        for g in GATHERS[EARLY:]:
+        scales = keep.tile([P, PASSES, (E - EARLY) * C], U8, name="sg_late", tag="w1_0", align_bytes=64)
+        for g in GATHERS[3:]:
             gather_scales(g, scales[:, :, (g[0] - EARLY) * C : (g[1] - EARLY) * C])
-            for e in range(max(g[0], EARLY_WORDS), g[1]):
-                gather_words(e, words[:, :, (e - EARLY_WORDS) * C : (e - EARLY_WORDS + 1) * C])
+            for a, b in LATE_WORDS:
+                if g[0] < b <= g[1]:
+                    gather_words(a, b, words[:, :, (a - EARLY_WORDS) * C : (b - EARLY_WORDS) * C])
 
         def run(g, last=None):
             for e in range(*g):
@@ -246,6 +255,9 @@ def tile_moe_ogt_relu2_sigmoid_kernel(tc, x_words, x_scales, wg_words, wg_scales
             first_product(e)
         for e in range(*GROUPS[0]):
             square(e)
+        later_loads(3)
+        run(GROUPS[1])
+        later_loads(4)
 
         def load_w2(g):
             w2[g] = keep.tile([P, g[1] - g[0], 2 * N], U8, name="w2_%d" % g[0], align_bytes=64)
@@ -264,7 +276,7 @@ def tile_moe_ogt_relu2_sigmoid_kernel(tc, x_words, x_scales, wg_words, wg_scales
         nc.sync.dma_start(out=wg[:], in_=wg_words.rearrange("s p n d -> p s (n d)").bitcast(I32))
         gate_rest = keep.tile([P, TOP, T - WIDE], F32, name="gate_rest")
         nc.sync.dma_start(out=gate_rest[:], in_=gate[:, :, WIDE:T].rearrange("r p t -> p r t"))
-        for g in GROUPS[1:]:
+        for g in GROUPS[2:]:
             run(g)
         for j, g in enumerate(Y_GROUPS):
             quantize(g, QTAGS[j])

@@ -39,18 +39,19 @@ WARM = True
 QTAGS = ("hq0", "xg0", "w1_%d" % WORDS[-1][0], "hq12", "hq14")
 Y_BANKS = ((7, 6, 0, 1, 2), (2, 1, 0, 6, 7))
 ROWS_BANK = 3
-TURNED = (6, 1)
-TOTALS = (7, 2)
-V_BANKS = (4, 0, 4)
-V_COPIES = (0, 12, 14)
+V_COPIES = ((0, 0), (0, 12), (0, 14), (1, 0), (1, 4))
 SINGLE_FROM = 0
 Y_GROUPS = [(0, 4), (4, 8), (8, 12), (12, 14), (14, 15)]
 W2_GROUPS = [(0, 4), (4, 8), (8, 12), (12, 15)]
 PRE_BANKS = (0, 1, 2)
 TURN_BANKS = (3, 4, 5, 6)
 SPARE_BANK = 7
-BLOCKS = 4
-WIDE = BLOCKS * P
+BLOCKS = 2
+TURNED = BLOCKS * P
+WIDE = 512
+GATE_BANKS = (3, 4, 5)
+PART_BANKS = (6, 1, 0)
+BACK_BANKS = (7, 2)
 
 
 def group_of(groups, e):
@@ -155,11 +156,6 @@ def tile_moe_ogt_relu2_sigmoid_kernel(tc, x_words, x_scales, wg_words, wg_scales
                     )
             return acc
 
-        def sigmoid(acc, shape, tag):
-            o = keep.tile([P, *shape], F32, name="o_%s" % tag, tag=tag)
-            nc.scalar.activation(o[:], acc[:], ACT.Sigmoid)
-            return o
-
         y = [keep.tile([P, S], F32, name="y%d" % h) for h in range(HALVES)]
         hb, hq, hs = {}, {}, {}
 
@@ -215,7 +211,7 @@ def tile_moe_ogt_relu2_sigmoid_kernel(tc, x_words, x_scales, wg_words, wg_scales
                         start=True,
                         stop=True,
                     )
-                if h == 0 and g[0] in V_COPIES:
+                if (h, g[0]) in V_COPIES:
                     nc.vector.tensor_copy(y[h][:, g[0] * C : g[1] * C], acc[:])
                 else:
                     nc.scalar.copy(y[h][:, g[0] * C : g[1] * C], acc[:])
@@ -267,15 +263,17 @@ def tile_moe_ogt_relu2_sigmoid_kernel(tc, x_words, x_scales, wg_words, wg_scales
         for g in w2s:
             load_w2_scales(g)
         load_w2(W2_GROUPS[1])
+        nc.sync.dma_start(out=gate_rows[0 : TOP * BLOCKS, 0, :], in_=gate[:, 0, 0:TURNED].rearrange("r (b p) -> r b p", p=P))
         for g in W2_GROUPS[2:]:
             load_w2(g)
         for r, src in enumerate((pos1, pos2, pos3)):
             nc.sync.dma_start(pos[r][:], src)
-        nc.sync.dma_start(out=gate_rows[0 : TOP * BLOCKS, 0, :], in_=gate[:, 0, 0:WIDE].rearrange("r (b p) -> r b p", p=P))
+        gate_rest = [keep.tile([P, T - TURNED], F32, name="gate_rest%d" % r) for r in range(TOP)]
+        nc.sync.dma_start(out=gate_rest[0][:], in_=gate[0, :, TURNED:T])
         wg = keep.tile([P, PASSES, N], I32, name="wg", align_bytes=64)
         nc.sync.dma_start(out=wg[:], in_=wg_words.rearrange("s p n d -> p s (n d)").bitcast(I32))
-        gate_rest = keep.tile([P, TOP, T - WIDE], F32, name="gate_rest")
-        nc.sync.dma_start(out=gate_rest[:], in_=gate[:, :, WIDE:T].rearrange("r p t -> p r t"))
+        for r in range(1, TOP):
+            nc.sync.dma_start(out=gate_rest[r][:], in_=gate[r, :, TURNED:T])
         for g in GROUPS[2:]:
             run(g)
         for j, g in enumerate(Y_GROUPS):
@@ -284,56 +282,66 @@ def tile_moe_ogt_relu2_sigmoid_kernel(tc, x_words, x_scales, wg_words, wg_scales
             for j, g in enumerate(Y_GROUPS):
                 second_product(g, h, Y_BANKS[h][j])
 
+        o = keep.tile([P, HALVES, T], F32, name="o")
+        for b, halves, t0, t1 in ((GATE_BANKS[0], [0], 0, WIDE), (GATE_BANKS[1], [0, 1], WIDE, T), (GATE_BANKS[2], [1], 0, WIDE)):
+            nc.scalar.activation(o[:, halves[0] : halves[-1] + 1, t0:t1], gate_product(b, halves, t0, t1)[:], ACT.Sigmoid)
         turned_rows = bank(ROWS_BANK, P)
         nc.tensor.transpose(turned_rows[:], gate_rows[:, 0, :], ident[:])
         by_token = keep.tile([P, TOP * BLOCKS], F32, name="by_token")
         nc.scalar.copy(by_token[:], turned_rows[:, 0 : TOP * BLOCKS])
 
-        scaled = [keep.tile([P, TOP, BLOCKS, P], F32, name="scaled%d" % h) for h in range(HALVES)]
-        totals = {}
+        rest = T - TURNED
+        parts = {}
 
-        def turn(h, r):
-            part = keep.tile([P, WIDE], F32, name="part%d_%d" % (h, r))
-            nc.vector.tensor_copy(part[:], y[h][:].indirect(pos[r][:, 0 : WIDE // 16]))
-            turned = bank(TURNED[(TOP * h + r) % len(TURNED)], BLOCKS, P)
-            for b in range(BLOCKS):
-                nc.tensor.transpose(turned[:, b, :], part[:, P * b : P * (b + 1)], ident[:])
-            for b in range(BLOCKS):
-                nc.scalar.activation(scaled[h][:, r, b, :], turned[:, b, :], ACT.Copy, scale=by_token[:, BLOCKS * r + b : BLOCKS * r + b + 1])
+        def scalar_gather(h, r):
+            parts[h, r] = keep.tile([P, TURNED], F32, name="part%d_%d" % (h, r))
+            nc.scalar.activation(parts[h, r][:], y[h][:].indirect(pos[r][:, 0 : TURNED // 16]), ACT.Copy)
 
-        def turn_back(h, r):
+        back = {}
+
+        def weigh(h, r):
+            turned = bank(PART_BANKS[(TOP * h + r) % len(PART_BANKS)], BLOCKS, P)
+            for k in range(BLOCKS):
+                nc.tensor.transpose(turned[:, k, :], parts[h, r][:, P * k : P * (k + 1)], ident[:])
+            weighted = keep.tile([P, BLOCKS, P], F32, name="weighted%d_%d" % (h, r))
+            for k in range(BLOCKS):
+                nc.scalar.activation(weighted[:, k, :], turned[:, k, :], ACT.Copy, scale=by_token[:, BLOCKS * r + k : BLOCKS * r + k + 1])
             if r == 0:
-                totals[h] = bank(TOTALS[h], WIDE)
-            for b in range(BLOCKS):
-                nc.tensor.matmul(totals[h][:, P * b : P * (b + 1)], lhsT=scaled[h][:, r, b, :], rhs=ident[:], is_transpose=True, start=(r == 0 and b == 0), stop=(r == TOP - 1 and b == BLOCKS - 1))
-
-        def finish(h):
-            res = keep.tile([P, WIDE], F32, name="res%d" % h)
-            nc.vector.tensor_tensor(res[:], totals[h][:], o_wide[h][:, 0, :], ALU.mult)
-            nc.sync.dma_start(out=out[P * h : P * (h + 1), 0:WIDE], in_=res[:])
+                back[h] = bank(BACK_BANKS[h], BLOCKS, P)
+            for k in range(BLOCKS):
+                nc.tensor.matmul(back[h][:, k, :], lhsT=weighted[:, k, :], rhs=ident[:], is_transpose=True, start=(r == 0 and k == 0), stop=(r == TOP - 1 and k == BLOCKS - 1))
 
         steps = [(h, r) for h in range(HALVES) for r in range(TOP)]
-        o_wide = []
         for j, step in enumerate(steps):
-            turn(*step)
+            scalar_gather(*step)
             if j > 0:
-                turn_back(*steps[j - 1])
-            if j in (1, 2):
-                o_wide.append(sigmoid(gate_product(V_BANKS[j - 1], [j - 1], 0, WIDE), (1, WIDE), "part0_%d" % j))
-            if j == 3:
-                o_rest = sigmoid(gate_product(V_BANKS[2], range(HALVES), WIDE, T), (HALVES, T - WIDE), "part0_0")
-        turn_back(*steps[-1])
-        rest = keep.tile([P, TOP, HALVES, T - WIDE], F32, name="rest", tag="part1_0")
+                weigh(*steps[j - 1])
+        weigh(*steps[-1])
+
+        terms = [keep.tile([P, TOP, rest], F32, name="terms%d" % h) for h in range(HALVES)]
+        sums = [keep.tile([P, TOP - 1, rest], F32, name="sums%d" % h) for h in range(HALVES)]
+        res = [keep.tile([P, T], F32, name="res%d" % h) for h in range(HALVES)]
+
+        def vector_gather(h, r):
+            nc.vector.tensor_tensor(terms[h][:, r, :], y[h][:].indirect(pos[r][:, TURNED // 16 : T // 16]), gate_rest[r][:], ALU.mult)
+
+        def add(h, r):
+            nc.vector.tensor_tensor(sums[h][:, r - 1, :], terms[h][:, 0, :] if r == 1 else sums[h][:, r - 2, :], terms[h][:, r, :], ALU.add)
+
+        def finish(h, total, t0, t1):
+            nc.vector.tensor_tensor(res[h][:, t0:t1], total, o[:, h, t0:t1], ALU.mult)
+            nc.sync.dma_start(out=out[P * h : P * (h + 1), t0:t1], in_=res[h][:, t0:t1])
+
         for r in range(TOP):
-            for h in range(HALVES):
-                nc.vector.tensor_tensor(rest[:, r, h, :], y[h][:].indirect(pos[r][:, WIDE // 16 : T // 16]), gate_rest[:, r, :], ALU.mult)
-            if r == 1:
-                two = keep.tile([P, HALVES, T - WIDE], F32, name="two")
-                nc.vector.tensor_tensor(two[:], rest[:, 0], rest[:, 1], ALU.add)
-        finish(0)
-        three = keep.tile([P, HALVES, T - WIDE], F32, name="three", tag="scaled0")
-        nc.vector.tensor_tensor(three[:], two[:], rest[:, 2], ALU.add)
-        finish(1)
-        res = keep.tile([P, HALVES, T - WIDE], F32, name="res_rest", tag="scaled1")
-        nc.vector.tensor_tensor(res[:], three[:], o_rest[:], ALU.mult)
-        nc.sync.dma_start(out=out[:, WIDE:T].rearrange("(h p) t -> p h t", p=P), in_=res[:])
+            vector_gather(0, r)
+        add(0, 1)
+        vector_gather(1, 0)
+        add(0, 2)
+        vector_gather(1, 1)
+        finish(0, sums[0][:, 1, :], TURNED, T)
+        vector_gather(1, 2)
+        add(1, 1)
+        finish(0, back[0][:].rearrange("p k t -> p (k t)"), 0, TURNED)
+        add(1, 2)
+        finish(1, back[1][:].rearrange("p k t -> p (k t)"), 0, TURNED)
+        finish(1, sums[1][:, 1, :], TURNED, T)

@@ -32,7 +32,7 @@ PLANE_OF = (0, 1, 2, 0, 1)
 NPRE = 3
 FIRST_SCALES = [(0, 3)]
 FIRST_WORDS = [(0, 1), (1, 4)]
-LATE_WORDS = [(4, 6), (6, 9), (9, 12), (12, 14), (14, 15)]
+LATE_WORDS = [(4, 6), (6, 7), (7, 9), (9, 10), (10, 12), (12, 13), (13, 14), (14, 15)]
 EARLY = FIRST_SCALES[-1][1]
 EARLY_WORDS = FIRST_WORDS[-1][1]
 WARM = True
@@ -339,9 +339,9 @@ def tile_moe_ogt_relu2_sigmoid_kernel(tc, x_words, x_scales, wg_words, wg_scales
         add(0, 2)
         vector_gather(1, 1)
         finish(0, sums[0][:, 1, :], TURNED, T)
-        vector_gather(1, 2)
         add(1, 1)
+        vector_gather(1, 2)
         finish(0, back[0][:].rearrange("p k t -> p (k t)"), 0, TURNED)
         add(1, 2)
-        finish(1, back[1][:].rearrange("p k t -> p (k t)"), 0, TURNED)
         finish(1, sums[1][:, 1, :], TURNED, T)
+        finish(1, back[1][:].rearrange("p k t -> p (k t)"), 0, TURNED)

@@ -39,7 +39,7 @@ WARM = True
 QTAGS = ("hq0", "xg0", "w1_%d" % WORDS[-1][0], "hq12", "hq14")
 Y_BANKS = ((7, 6, 0, 1, 2), (2, 1, 0, 6, 7))
 ROWS_BANK = 3
-V_COPIES = ((0, 0), (0, 12), (0, 14), (1, 0), (1, 4))
+V_COPIES = ((0, 0), (0, 12), (0, 14), (1, 0))
 SINGLE_FROM = 0
 Y_GROUPS = [(0, 4), (4, 8), (8, 12), (12, 14), (14, 15)]
 W2_GROUPS = [(0, 4), (4, 8), (8, 12), (12, 15)]
@@ -100,8 +100,10 @@ def tile_moe_ogt_relu2_sigmoid_kernel(tc, x_words, x_scales, wg_words, wg_scales
         small = keep.tile([P, E, N], U8, name="small", align_bytes=64)
         wgs = keep.tile([P, PASSES, N], U8, name="wgs", align_bytes=64)
         gate_rows = keep.tile([P, 1, P], F32, name="gate_rows")
-        for tile in planes + [wgs, gate_rows, small]:
+        for tile in planes:
             zero(tile)
+        for tile in (wgs, small, gate_rows):
+            nc.gpsimd.memset(tile[:].rearrange("p m w -> p (m w)").bitcast(I32), 0)
         w1s = {g: planes[j][:, 0 : PASSES * (g[1] - g[0]), :] for j, g in zip(PLANE_OF, GROUPS)}
         w2s = {(0, E): small[:]}
 
@@ -266,13 +268,12 @@ def tile_moe_ogt_relu2_sigmoid_kernel(tc, x_words, x_scales, wg_words, wg_scales
         nc.sync.dma_start(out=gate_rows[0 : TOP * BLOCKS, 0, :], in_=gate[:, 0, 0:TURNED].rearrange("r (b p) -> r b p", p=P))
         for g in W2_GROUPS[2:]:
             load_w2(g)
+        wg = keep.tile([P, PASSES, N], I32, name="wg", align_bytes=64)
+        nc.sync.dma_start(out=wg[:], in_=wg_words.rearrange("s p n d -> p s (n d)").bitcast(I32))
         for r, src in enumerate((pos1, pos2, pos3)):
             nc.sync.dma_start(pos[r][:], src)
         gate_rest = [keep.tile([P, T - TURNED], F32, name="gate_rest%d" % r) for r in range(TOP)]
-        nc.sync.dma_start(out=gate_rest[0][:], in_=gate[0, :, TURNED:T])
-        wg = keep.tile([P, PASSES, N], I32, name="wg", align_bytes=64)
-        nc.sync.dma_start(out=wg[:], in_=wg_words.rearrange("s p n d -> p s (n d)").bitcast(I32))
-        for r in range(1, TOP):
+        for r in range(TOP):
             nc.sync.dma_start(out=gate_rest[r][:], in_=gate[r, :, TURNED:T])
         for g in GROUPS[2:]:
             run(g)

@@ -31,8 +31,8 @@ PLANES = (3, 3, 3)
 PLANE_OF = (0, 1, 2, 0, 1)
 NPRE = 3
 FIRST_SCALES = [(0, 3)]
-FIRST_WORDS = [(0, 1), (1, 4)]
-LATE_WORDS = [(4, 6), (6, 7), (7, 9), (9, 10), (10, 12), (12, 13), (13, 14), (14, 15)]
+FIRST_WORDS = [(0, 1), (1, 4), (4, 6)]
+LATE_WORDS = [(6, 7), (7, 9), (9, 10), (10, 12), (12, 13), (13, 14), (14, 15)]
 EARLY = FIRST_SCALES[-1][1]
 EARLY_WORDS = FIRST_WORDS[-1][1]
 WARM = True

@@ -31,8 +31,8 @@ PLANES = (3, 3, 3)
 PLANE_OF = (0, 1, 2, 0, 1)
 NPRE = 3
 FIRST_SCALES = [(0, 3)]
-FIRST_WORDS = [(0, 1), (1, 4), (4, 6)]
-LATE_WORDS = [(6, 7), (7, 9), (9, 10), (10, 12), (12, 13), (13, 14), (14, 15)]
+FIRST_WORDS = [(0, 1), (1, 4), (4, 7)]
+LATE_WORDS = [(7, 10), (10, 13), (13, 14), (14, 15)]
 EARLY = FIRST_SCALES[-1][1]
 EARLY_WORDS = FIRST_WORDS[-1][1]
 WARM = True
@@ -100,9 +100,9 @@ def tile_moe_ogt_relu2_sigmoid_kernel(tc, x_words, x_scales, wg_words, wg_scales
         small = keep.tile([P, E, N], U8, name="small", align_bytes=64)
         wgs = keep.tile([P, PASSES, N], U8, name="wgs", align_bytes=64)
         gate_rows = keep.tile([P, 1, P], F32, name="gate_rows")
-        for tile in planes:
+        for tile in planes[:2]:
             zero(tile)
-        for tile in (wgs, small, gate_rows):
+        for tile in (planes[2], wgs, small, gate_rows):
             nc.gpsimd.memset(tile[:].rearrange("p m w -> p (m w)").bitcast(I32), 0)
         w1s = {g: planes[j][:, 0 : PASSES * (g[1] - g[0]), :] for j, g in zip(PLANE_OF, GROUPS)}
         w2s = {(0, E): small[:]}
@@ -204,12 +204,14 @@ def tile_moe_ogt_relu2_sigmoid_kernel(tc, x_words, x_scales, wg_words, wg_scales
                 for e in range(*g):
                     gw, gs = group_of(W2_GROUPS, e), group_of(list(w2s), e)
                     cols = slice((e - g[0]) * C, (e - g[0] + 1) * C)
+                    gq = group_of(Y_GROUPS, e)
+                    own = slice((e - gq[0]) * C, (e - gq[0] + 1) * C)
                     nc.tensor.matmul_mx(
                         out=acc[:, cols],
                         lhsT=w2[gw][:, e - gw[0], 2 * P * h : 2 * P * (h + 1)].bitcast(FP4X4),
                         lhsT_scale=w2s[gs][:, e - gs[0], P * h : P * (h + 1)],
-                        rhs=hq[g][:, cols].bitcast(FP8X4),
-                        rhs_scale=hs[g][:, cols],
+                        rhs=hq[gq][:, own].bitcast(FP8X4),
+                        rhs_scale=hs[gq][:, own],
                         start=True,
                         stop=True,
                     )
@@ -240,7 +242,7 @@ def tile_moe_ogt_relu2_sigmoid_kernel(tc, x_words, x_scales, wg_words, wg_scales
         for g in GATHERS[3:]:
             gather_scales(g, scales[:, :, (g[0] - EARLY) * C : (g[1] - EARLY) * C])
             for a, b in LATE_WORDS:
-                if g[0] < b <= g[1]:
+                if g[0] <= a < g[1]:
                     gather_words(a, b, words[:, :, (a - EARLY_WORDS) * C : (b - EARLY_WORDS) * C])
 
         def run(g, last=None):
@@ -280,7 +282,7 @@ def tile_moe_ogt_relu2_sigmoid_kernel(tc, x_words, x_scales, wg_words, wg_scales
         for j, g in enumerate(Y_GROUPS):
             quantize(g, QTAGS[j])
         for h in range(HALVES):
-            for j, g in enumerate(Y_GROUPS):
+            for j, g in enumerate(W2_GROUPS if h else Y_GROUPS):
                 second_product(g, h, Y_BANKS[h][j])
 
         o = keep.tile([P, HALVES, T], F32, name="o")

@@ -38,8 +38,8 @@ EARLY_WORDS = FIRST_WORDS[-1][1]
 WARM = True
 QTAGS = ("hq0", "xg0", "w1_%d" % WORDS[-1][0], "hq12", "hq14")
 Y_BANKS = ((7, 6, 0, 1, 2), (2, 1, 0, 6, 7))
-ROWS_BANK = 3
-V_COPIES = ((0, 0), (0, 12), (0, 14), (1, 0))
+ROWS_BANK = 6
+V_COPIES = ((0, 0), (0, 12), (0, 14))
 SINGLE_FROM = 0
 Y_GROUPS = [(0, 4), (4, 8), (8, 12), (12, 14), (14, 15)]
 W2_GROUPS = [(0, 4), (4, 8), (8, 12), (12, 15)]
@@ -143,20 +143,17 @@ def tile_moe_ogt_relu2_sigmoid_kernel(tc, x_words, x_scales, wg_words, wg_scales
         def load_w2_scales(g):
             load_scale_rows(w2s[g], w2_scales.rearrange("e s b n -> b (e s) n")[:, g[0] : g[1], :])
 
-        def gate_product(b, halves, t0, t1):
-            acc = bank(b, len(halves), t1 - t0)
-            for j, h in enumerate(halves):
-                for s in range(PASSES):
-                    nc.tensor.matmul_mx(
-                        out=acc[:, j, :],
-                        lhsT=wg[:, s, P * h : P * (h + 1)].bitcast(FP8X4),
-                        lhsT_scale=wgs[:, s, P * h : P * (h + 1)],
-                        rhs=xw[:, s, t0:t1].bitcast(FP8X4),
-                        rhs_scale=xs[:, s, t0:t1],
-                        start=(s == 0),
-                        stop=(s == PASSES - 1),
-                    )
-            return acc
+        def gate_product(acc, h, t0, t1):
+            for s in range(PASSES):
+                nc.tensor.matmul_mx(
+                    out=acc,
+                    lhsT=wg[:, s, P * h : P * (h + 1)].bitcast(FP8X4),
+                    lhsT_scale=wgs[:, s, P * h : P * (h + 1)],
+                    rhs=xw[:, s, t0:t1].bitcast(FP8X4),
+                    rhs_scale=xs[:, s, t0:t1],
+                    start=(s == 0),
+                    stop=(s == PASSES - 1),
+                )
 
         y = [keep.tile([P, S], F32, name="y%d" % h) for h in range(HALVES)]
         hb, hq, hs = {}, {}, {}
@@ -285,9 +282,17 @@ def tile_moe_ogt_relu2_sigmoid_kernel(tc, x_words, x_scales, wg_words, wg_scales
             for j, g in enumerate(W2_GROUPS if h else Y_GROUPS):
                 second_product(g, h, Y_BANKS[h][j])
 
-        o = keep.tile([P, HALVES, T], F32, name="o")
-        for b, halves, t0, t1 in ((GATE_BANKS[0], [0], 0, WIDE), (GATE_BANKS[1], [0, 1], WIDE, T), (GATE_BANKS[2], [1], 0, WIDE)):
-            nc.scalar.activation(o[:, halves[0] : halves[-1] + 1, t0:t1], gate_product(b, halves, t0, t1)[:], ACT.Sigmoid)
+        last = T - WIDE
+        logits = [bank(b, n) for b, n in zip(GATE_BANKS, (WIDE, last + TURNED, T - TURNED))]
+        gate_product(logits[0][:], 0, 0, WIDE)
+        gate_product(logits[1][:, 0:last], 0, WIDE, T)
+        gate_product(logits[1][:, last : last + TURNED], 1, 0, TURNED)
+        gate_product(logits[2][:, 0 : WIDE - TURNED], 1, TURNED, WIDE)
+        gate_product(logits[2][:, WIDE - TURNED : T - TURNED], 1, WIDE, T)
+        o_first = keep.tile([P, T], F32, name="o_first")
+        nc.scalar.activation(o_first[:, 0:WIDE], logits[0][:], ACT.Sigmoid)
+        nc.scalar.activation(o_first[:, WIDE:T], logits[1][:, 0:last], ACT.Sigmoid)
+        o = {(0, 0): o_first[:, 0:TURNED], (0, TURNED): o_first[:, TURNED:T]}
         turned_rows = bank(ROWS_BANK, P)
         nc.tensor.transpose(turned_rows[:], gate_rows[:, 0, :], ident[:])
         by_token = keep.tile([P, TOP * BLOCKS], F32, name="by_token")
@@ -319,21 +324,28 @@ def tile_moe_ogt_relu2_sigmoid_kernel(tc, x_words, x_scales, wg_words, wg_scales
             scalar_gather(*step)
             if j > 0:
                 weigh(*steps[j - 1])
+        late = keep.tile([P, rest], F32, name="o_rest", tag="part1_1")
+        nc.scalar.activation(late[:], logits[2][:], ACT.Sigmoid)
+        o[1, TURNED] = late[:]
         weigh(*steps[-1])
+        late = keep.tile([P, TURNED], F32, name="o_turned", tag="part1_2")
+        nc.scalar.activation(late[:], logits[1][:, last : last + TURNED], ACT.Sigmoid)
+        o[1, 0] = late[:]
 
-        terms = [keep.tile([P, TOP, rest], F32, name="terms%d" % h) for h in range(HALVES)]
+        terms = {}
         sums = [keep.tile([P, TOP - 1, rest], F32, name="sums%d" % h) for h in range(HALVES)]
-        res = [keep.tile([P, T], F32, name="res%d" % h) for h in range(HALVES)]
 
         def vector_gather(h, r):
-            nc.vector.tensor_tensor(terms[h][:, r, :], y[h][:].indirect(pos[r][:, TURNED // 16 : T // 16]), gate_rest[r][:], ALU.mult)
+            terms[h, r] = keep.tile([P, rest], F32, name="term%d" % r)
+            nc.vector.tensor_tensor(terms[h, r][:], y[h][:].indirect(pos[r][:, TURNED // 16 : T // 16]), gate_rest[r][:], ALU.mult)
 
         def add(h, r):
-            nc.vector.tensor_tensor(sums[h][:, r - 1, :], terms[h][:, 0, :] if r == 1 else sums[h][:, r - 2, :], terms[h][:, r, :], ALU.add)
+            nc.vector.tensor_tensor(sums[h][:, r - 1, :], terms[h, 0][:] if r == 1 else sums[h][:, r - 2, :], terms[h, r][:], ALU.add)
 
         def finish(h, total, t0, t1):
-            nc.vector.tensor_tensor(res[h][:, t0:t1], total, o[:, h, t0:t1], ALU.mult)
-            nc.sync.dma_start(out=out[P * h : P * (h + 1), t0:t1], in_=res[h][:, t0:t1])
+            res = keep.tile([P, t1 - t0], F32, name="res%d_%d" % (h, t0), tag="sums1" if (h, t0) == (1, 0) else "res%d_%d" % (h, t0))
+            nc.vector.tensor_tensor(res[:], total, o[h, t0], ALU.mult)
+            nc.sync.dma_start(out=out[P * h : P * (h + 1), t0:t1], in_=res[:])
 
         for r in range(TOP):
             vector_gather(0, r)
@@ -342,8 +354,8 @@ def tile_moe_ogt_relu2_sigmoid_kernel(tc, x_words, x_scales, wg_words, wg_scales
         add(0, 2)
         vector_gather(1, 1)
         finish(0, sums[0][:, 1, :], TURNED, T)
-        add(1, 1)
         vector_gather(1, 2)
+        add(1, 1)
         finish(0, back[0][:].rearrange("p k t -> p (k t)"), 0, TURNED)
         add(1, 2)
         finish(1, sums[1][:, 1, :], TURNED, T)

@@ -21,35 +21,24 @@ FP4X4 = mybir.dt.float4_e2m1fn_x4
 ACT = mybir.ActivationFunctionType
 ALU = mybir.AluOpType
 
-GROUPS = [(0, 3), (3, 6), (6, 9), (9, 12), (12, 15)]
-GATHERS = [(0, 1), (1, 2), (2, 3), (3, 6), (6, 9), (9, 12), (12, 15)]
-VECTOR_RELUS = (14,)
-WORDS = [(0, 1), (1, 3), (3, 6), (6, 9), (9, 12), (12, 15)]
-RUNS = [(0, 1), (1, 2), (2, 5), (5, 8), (8, 11), (11, 15)]
-HOLD = False
-PLANES = (3, 3, 3)
-PLANE_OF = (0, 1, 2, 0, 1)
-NPRE = 3
-FIRST_SCALES = [(0, 3)]
-FIRST_WORDS = [(0, 1), (1, 4), (4, 7)]
-LATE_WORDS = [(7, 10), (10, 13), (13, 14), (14, 15)]
-EARLY = FIRST_SCALES[-1][1]
-EARLY_WORDS = FIRST_WORDS[-1][1]
-WARM = True
-QTAGS = ("hq0", "xg0", "w1_%d" % WORDS[-1][0], "hq12", "hq14")
-Y_BANKS = ((7, 6, 0, 1, 2), (2, 1, 0, 6, 7))
-ROWS_BANK = 6
-V_COPIES = ((0, 0), (0, 12), (0, 14))
-SINGLE_FROM = 0
-Y_GROUPS = [(0, 4), (4, 8), (8, 12), (12, 14), (14, 15)]
+RUN = 3
+RUNS = [(a, a + RUN) for a in range(0, E, RUN)]
+SCALE_TILES = 3
+EARLY_WORDS = [(0, 1), (1, 3), (3, 5)]
+AHEAD = EARLY_WORDS[-1][1]
+H_GROUPS = [(0, 4), (4, 8), (8, 12), (12, 14), (14, 15)]
 W2_GROUPS = [(0, 4), (4, 8), (8, 12), (12, 15)]
+Y_GROUPS = (H_GROUPS, W2_GROUPS)
+Y_BANKS = ((7, 6, 0, 1, 2), (2, 1, 0, 6))
+VECTOR_Y = (H_GROUPS[0], H_GROUPS[3], H_GROUPS[4])
 PRE_BANKS = (0, 1, 2)
 TURN_BANKS = (3, 4, 5, 6)
-SPARE_BANK = 7
 BLOCKS = 2
 TURNED = BLOCKS * P
-WIDE = 512
+REST = T - TURNED
+BANK = 512
 GATE_BANKS = (3, 4, 5)
+ROWS_BANK = 6
 PART_BANKS = (6, 1, 0)
 BACK_BANKS = (7, 2)
 
@@ -58,33 +47,25 @@ def group_of(groups, e):
     return [g for g in groups if g[0] <= e < g[1]][0]
 
 
-def pre_bank(e):
-    return SPARE_BANK if e == E - 1 and GROUPS[-1][1] - GROUPS[-1][0] > 3 else PRE_BANKS[e % len(PRE_BANKS)]
-
-
-def turn_bank(e):
-    return TURN_BANKS[e % len(TURN_BANKS)]
-
-
 def tile_moe_ogt_relu2_sigmoid_kernel(tc, x_words, x_scales, wg_words, wg_scales, w1_words, w1_scales, w2_words, w2_scales, gate, offs, pos1, pos2, pos3, out):
     nc = tc.nc
     with ExitStack() as ctx:
         keep = ctx.enter_context(tc.tile_pool(name="keep", bufs=1))
-        ring = ctx.enter_context(tc.tile_pool(name="ring", bufs=4))
+        ring = ctx.enter_context(tc.tile_pool(name="ring", bufs=RUN + 1))
         psum = ctx.enter_context(tc.psum_pool(name="psum", bufs=1))
 
         def bank(b, *shape):
             return psum.tile([P, *shape], F32, name="bank%d" % b)
 
-        def zero(tile):
-            nc.vector.memset(tile[:].rearrange("p m w -> p (m w)").bitcast(I32), 0)
+        def zero(engine, tile):
+            engine.memset(tile[:].rearrange("p m w -> p (m w)").bitcast(I32), 0)
 
         def load_scale_rows(tile, rows, which=range(4)):
             for r in which:
                 nc.sync.dma_start(out=tile[r:P:32].bitcast(I32), in_=rows[r:16:4].bitcast(I32))
 
         xs = keep.tile([P, PASSES, T], U8, name="xs", align_bytes=64)
-        nc.gpsimd.memset(xs[:].rearrange("p m w -> p (m w)").bitcast(I32), 0)
+        zero(nc.gpsimd, xs)
         slot_list = keep.tile([P, S // 16], U16, name="slot_list")
         nc.sync.dma_start(slot_list[:], offs)
         load_scale_rows(xs, x_scales.rearrange("s b t -> b s t"))
@@ -96,52 +77,159 @@ def tile_moe_ogt_relu2_sigmoid_kernel(tc, x_words, x_scales, wg_words, wg_scales
         warm = keep.tile([P, 1], F32, name="warm")
         nc.scalar.activation(warm[:], ident[:, 0:1], ACT.Sigmoid)
 
-        planes = [keep.tile([P, PASSES * n, H], U8, name="plane%d" % j, align_bytes=64) for j, n in enumerate(PLANES)]
-        small = keep.tile([P, E, N], U8, name="small", align_bytes=64)
+        w1_scale_tiles = [keep.tile([P, PASSES * RUN, H], U8, name="plane%d" % j, align_bytes=64) for j in range(SCALE_TILES)]
+        w2s = keep.tile([P, E, N], U8, name="small", align_bytes=64)
         wgs = keep.tile([P, PASSES, N], U8, name="wgs", align_bytes=64)
         gate_rows = keep.tile([P, 1, P], F32, name="gate_rows")
-        for tile in planes[:2]:
-            zero(tile)
-        for tile in (planes[2], wgs, small, gate_rows):
-            nc.gpsimd.memset(tile[:].rearrange("p m w -> p (m w)").bitcast(I32), 0)
-        w1s = {g: planes[j][:, 0 : PASSES * (g[1] - g[0]), :] for j, g in zip(PLANE_OF, GROUPS)}
-        w2s = {(0, E): small[:]}
+        for tile in w1_scale_tiles[:2]:
+            zero(nc.vector, tile)
+        for tile in (w1_scale_tiles[2], wgs, w2s, gate_rows):
+            zero(nc.gpsimd, tile)
+        w1s = {g: w1_scale_tiles[j % SCALE_TILES] for j, g in enumerate(RUNS)}
 
         def slots(a, b):
             return slot_list[:, a * C // 16 : b * C // 16]
 
         xg, sg = {}, {}
 
-        def gather_scales(g, scales):
+        def gather_scales(a, b, scales):
             for s in range(PASSES):
-                nc.vector.tensor_copy(scales[:, s, :], xs[:, s, :].indirect(slots(*g)))
-            for e in range(*g):
-                sg[e] = scales[:, :, (e - g[0]) * C : (e - g[0] + 1) * C]
+                nc.vector.tensor_copy(scales[:, s, :], xs[:, s, :].indirect(slots(a, b)))
+            for e in range(a, b):
+                sg[e] = scales[:, :, (e - a) * C : (e - a + 1) * C]
 
         def gather_words(a, b, words):
-            for e in range(a, b):
-                xg[e] = words[:, :, (e - a) * C : (e - a + 1) * C]
             for s in range(PASSES):
                 nc.vector.tensor_copy(words[:, s, :], xw[:, s, :].bitcast(U32).indirect(slots(a, b)))
+            for e in range(a, b):
+                xg[e] = words[:, :, (e - a) * C : (e - a + 1) * C]
 
-        for g in FIRST_SCALES:
-            gather_scales(g, keep.tile([P, PASSES, (g[1] - g[0]) * C], U8, name="sg%d" % g[0], align_bytes=64)[:])
-        for g in FIRST_WORDS:
-            gather_words(*g, keep.tile([P, PASSES, (g[1] - g[0]) * C], U32, name="xg%d" % g[0], align_bytes=64)[:])
+        gather_scales(0, RUN, keep.tile([P, PASSES, RUN * C], U8, name="sg0", align_bytes=64)[:])
+        for a, b in EARLY_WORDS:
+            gather_words(a, b, keep.tile([P, PASSES, (b - a) * C], U32, name="xg%d" % a, align_bytes=64)[:])
 
         w1, w2 = {}, {}
 
         def load_w1(a, b):
-            tile = keep.tile([P, (b - a) * PASSES, 2 * H], U8, name="w1_%d" % a, tag="w1_%d" % a, align_bytes=64)
+            tile = keep.tile([P, (b - a) * PASSES, 2 * H], U8, name="w1_%d" % a, align_bytes=64)
             nc.sync.dma_start(out=tile[:].bitcast(I32), in_=w1_words.rearrange("e s p b -> p (e s) b")[:, PASSES * a : PASSES * b, :].bitcast(I32))
             for e in range(a, b):
                 w1[e] = tile[:, (e - a) * PASSES : (e - a + 1) * PASSES, :]
 
-        def load_w1_scales(g):
-            load_scale_rows(w1s[g], w1_scales.rearrange("e s b i -> b (e s) i")[:, PASSES * g[0] : PASSES * g[1], :])
+        def load_run(j):
+            a, b = RUNS[j]
+            load_scale_rows(w1s[a, b], w1_scales.rearrange("e s b i -> b (e s) i")[:, PASSES * a : PASSES * b, :])
+            load_w1(max(a, 1), b)
+            if j > 0:
+                load_scale_rows(wgs, wg_scales.rearrange("s b n -> b s n"), [j - 1])
 
-        def load_w2_scales(g):
-            load_scale_rows(w2s[g], w2_scales.rearrange("e s b n -> b (e s) n")[:, g[0] : g[1], :])
+        def load_w2(g):
+            w2[g] = keep.tile([P, g[1] - g[0], 2 * N], U8, name="w2_%d" % g[0], align_bytes=64)
+            nc.sync.dma_start(out=w2[g][:].bitcast(I32), in_=w2_words.rearrange("e s p b -> p (e s) b")[:, g[0] : g[1], :].bitcast(I32))
+
+        y = [keep.tile([P, S], F32, name="y%d" % h) for h in range(HALVES)]
+        relus, hb, hq, hs = {}, {}, {}, {}
+
+        def first_product(e):
+            g = group_of(RUNS, e)
+            pre = bank(PRE_BANKS[e % len(PRE_BANKS)], H)
+            for s in range(PASSES):
+                nc.tensor.matmul_mx(
+                    out=pre[:],
+                    lhsT=xg[e][:, s, :].bitcast(FP8X4),
+                    lhsT_scale=sg[e][:, s, :],
+                    rhs=w1[e][:, s, :].bitcast(FP4X4),
+                    rhs_scale=w1s[g][:, (e - g[0]) * PASSES + s, :],
+                    start=(s == 0),
+                    stop=(s == PASSES - 1),
+                )
+            relus[e] = ring.tile([P, 4, P], F32, name="relu")
+            if e == E - 1:
+                nc.vector.tensor_scalar_max(relus[e][:], pre[:].rearrange("u (p d) -> u d p", d=4), 0.0)
+            else:
+                nc.scalar.activation(relus[e][:], pre[:].rearrange("u (p d) -> u d p", d=4), ACT.Relu)
+
+        def square(e):
+            g = group_of(H_GROUPS, e)
+            turned = bank(TURN_BANKS[e % len(TURN_BANKS)], 4, C)
+            for d in range(4):
+                nc.tensor.transpose(turned[:, d, :], relus[e][:, d, :], ident[:])
+            if e == g[0]:
+                hb[g] = keep.tile([P, (g[1] - g[0]) * C, 4], BF16, name="hb%d" % e, align_bytes=64)
+            nc.scalar.activation(hb[g][:, (e - g[0]) * C : (e - g[0] + 1) * C, :], turned[:].rearrange("p d u -> p u d"), ACT.Square)
+
+        def run(g, first=None):
+            for e in range(first or g[0], g[1]):
+                first_product(e)
+            for e in range(*g):
+                square(e)
+
+        def quantize(g, tag):
+            n = (g[1] - g[0]) * C
+            hq[g] = keep.tile([P, n], U32, name="hq%d" % g[0], tag=tag, align_bytes=64)
+            hs[g] = keep.tile([P, n], U8, name="hs%d" % g[0], align_bytes=64)
+            nc.vector.quantize_mx(out=hq[g][:].bitcast(FP8X4), scales=hs[g][:], in_=hb[g][:].rearrange("p u d -> p (u d)"))
+
+        def second_product(g, h, b):
+            acc = bank(b, (g[1] - g[0]) * C)
+            for e in range(*g):
+                gw, gq = group_of(W2_GROUPS, e), group_of(H_GROUPS, e)
+                own = slice((e - gq[0]) * C, (e - gq[0] + 1) * C)
+                nc.tensor.matmul_mx(
+                    out=acc[:, (e - g[0]) * C : (e - g[0] + 1) * C],
+                    lhsT=w2[gw][:, e - gw[0], 2 * P * h : 2 * P * (h + 1)].bitcast(FP4X4),
+                    lhsT_scale=w2s[:, e, P * h : P * (h + 1)],
+                    rhs=hq[gq][:, own].bitcast(FP8X4),
+                    rhs_scale=hs[gq][:, own],
+                    start=True,
+                    stop=True,
+                )
+            if h == 0 and g in VECTOR_Y:
+                nc.vector.tensor_copy(y[h][:, g[0] * C : g[1] * C], acc[:])
+            else:
+                nc.scalar.copy(y[h][:, g[0] * C : g[1] * C], acc[:])
+
+        pos = [keep.tile([P, T // 16], U16, name="pos%d" % r) for r in range(TOP)]
+        load_w1(0, 1)
+        for j in range(SCALE_TILES):
+            load_run(j)
+        first_product(0)
+        late_words = keep.tile([P, PASSES, (E - AHEAD) * C], U32, name="xg_late", tag="xg0", align_bytes=64)
+        late_scales = keep.tile([P, PASSES, (E - RUN) * C], U8, name="sg_late", tag="w1_0", align_bytes=64)
+        have = AHEAD
+        for a, b in RUNS[1:]:
+            gather_scales(a, b, late_scales[:, :, (a - RUN) * C : (b - RUN) * C])
+            for upto in range(a + 1, b + 1) if b == E else [min(b + 1, E - RUN)]:
+                gather_words(have, upto, late_words[:, :, (have - AHEAD) * C : (upto - AHEAD) * C])
+                have = upto
+
+        run(RUNS[0], first=1)
+        load_run(SCALE_TILES)
+        run(RUNS[1])
+        load_run(SCALE_TILES + 1)
+
+        load_w2(W2_GROUPS[0])
+        load_scale_rows(w2s, w2_scales.rearrange("e s b n -> b (e s) n"))
+        load_w2(W2_GROUPS[1])
+        nc.sync.dma_start(out=gate_rows[0 : TOP * BLOCKS, 0, :], in_=gate[:, 0, 0:TURNED].rearrange("r (b p) -> r b p", p=P))
+        for g in W2_GROUPS[2:]:
+            load_w2(g)
+        wg = keep.tile([P, PASSES, N], I32, name="wg", align_bytes=64)
+        nc.sync.dma_start(out=wg[:], in_=wg_words.rearrange("s p n d -> p s (n d)").bitcast(I32))
+        for r, src in enumerate((pos1, pos2, pos3)):
+            nc.sync.dma_start(pos[r][:], src)
+        gate_rest = [keep.tile([P, REST], F32, name="gate_rest%d" % r) for r in range(TOP)]
+        for r in range(TOP):
+            nc.sync.dma_start(out=gate_rest[r][:], in_=gate[r, :, TURNED:T])
+
+        for g in RUNS[2:]:
+            run(g)
+        held = {H_GROUPS[1]: "xg0", H_GROUPS[2]: "w1_%d" % RUNS[-1][0]}
+        for g in H_GROUPS:
+            quantize(g, held.get(g, "hq%d" % g[0]))
+        for h in range(HALVES):
+            for g, b in zip(Y_GROUPS[h], Y_BANKS[h]):
+                second_product(g, h, b)
 
         def gate_product(acc, h, t0, t1):
             for s in range(PASSES):
@@ -155,159 +243,29 @@ def tile_moe_ogt_relu2_sigmoid_kernel(tc, x_words, x_scales, wg_words, wg_scales
                     stop=(s == PASSES - 1),
                 )
 
-        y = [keep.tile([P, S], F32, name="y%d" % h) for h in range(HALVES)]
-        hb, hq, hs = {}, {}, {}
-
-        relus = {}
-
-        def first_product(e):
-            gl = group_of(GROUPS, e)
-            pre = bank(pre_bank(e), H)
-            for s in range(PASSES):
-                nc.tensor.matmul_mx(
-                    out=pre[:],
-                    lhsT=xg[e][:, s, :].bitcast(FP8X4),
-                    lhsT_scale=sg[e][:, s, :],
-                    rhs=w1[e][:, s, :].bitcast(FP4X4),
-                    rhs_scale=w1s[gl][:, (e - gl[0]) * PASSES + s, :],
-                    start=(s == 0),
-                    stop=(s == PASSES - 1),
-                )
-            relu = relus[e] = ring.tile([P, 4, P], F32, name="relu")
-            if e in VECTOR_RELUS:
-                nc.vector.tensor_scalar_max(relu[:], pre[:].rearrange("u (p d) -> u d p", d=4), 0.0)
-            else:
-                nc.scalar.activation(relu[:], pre[:].rearrange("u (p d) -> u d p", d=4), ACT.Relu)
-
-        def square(e):
-            gy, relu = group_of(Y_GROUPS, e), relus[e]
-            turned = bank(turn_bank(e), 4, C)
-            for d in range(4):
-                nc.tensor.transpose(turned[:, d, :], relu[:, d, :], ident[:])
-            n = (gy[1] - gy[0]) * C
-            if e == gy[0]:
-                hb[gy] = keep.tile([P, n, 4], BF16, name="hb%d" % e, align_bytes=64)
-            nc.scalar.activation(hb[gy][:, (e - gy[0]) * C : (e - gy[0] + 1) * C, :], turned[:].rearrange("p d u -> p u d"), ACT.Square)
-
-        def quantize(gy, tag):
-            n = (gy[1] - gy[0]) * C
-            hq[gy] = keep.tile([P, n], U32, name="hq%d" % gy[0], tag=tag, align_bytes=64)
-            hs[gy] = keep.tile([P, n], U8, name="hs%d" % gy[0], align_bytes=64)
-            nc.vector.quantize_mx(out=hq[gy][:].bitcast(FP8X4), scales=hs[gy][:], in_=hb[gy][:].rearrange("p u d -> p (u d)"))
-
-        def second_product(g, h, b):
-            if b >= 0:
-                acc = bank(b, (g[1] - g[0]) * C)
-                for e in range(*g):
-                    gw, gs = group_of(W2_GROUPS, e), group_of(list(w2s), e)
-                    cols = slice((e - g[0]) * C, (e - g[0] + 1) * C)
-                    gq = group_of(Y_GROUPS, e)
-                    own = slice((e - gq[0]) * C, (e - gq[0] + 1) * C)
-                    nc.tensor.matmul_mx(
-                        out=acc[:, cols],
-                        lhsT=w2[gw][:, e - gw[0], 2 * P * h : 2 * P * (h + 1)].bitcast(FP4X4),
-                        lhsT_scale=w2s[gs][:, e - gs[0], P * h : P * (h + 1)],
-                        rhs=hq[gq][:, own].bitcast(FP8X4),
-                        rhs_scale=hs[gq][:, own],
-                        start=True,
-                        stop=True,
-                    )
-                if (h, g[0]) in V_COPIES:
-                    nc.vector.tensor_copy(y[h][:, g[0] * C : g[1] * C], acc[:])
-                else:
-                    nc.scalar.copy(y[h][:, g[0] * C : g[1] * C], acc[:])
-
-        def load_group(g):
-            load_w1_scales(g)
-            for w in WORDS:
-                if g[0] < w[1] <= g[1] and w[0] not in w1:
-                    load_w1(*w)
-
-        pos = [keep.tile([P, T // 16], U16, name="pos%d" % r) for r in range(TOP)]
-        load_w1(*WORDS[0])
-
-        def later_loads(j):
-            load_group(GROUPS[j])
-            load_scale_rows(wgs, wg_scales.rearrange("s b n -> b s n"), [j - 1])
-
-        load_group(GROUPS[0])
-        later_loads(1)
-        later_loads(2)
-        first_product(0)
-        words = keep.tile([P, PASSES, (E - EARLY_WORDS) * C], U32, name="xg_late", tag="xg0", align_bytes=64)
-        scales = keep.tile([P, PASSES, (E - EARLY) * C], U8, name="sg_late", tag="w1_0", align_bytes=64)
-        for g in GATHERS[3:]:
-            gather_scales(g, scales[:, :, (g[0] - EARLY) * C : (g[1] - EARLY) * C])
-            for a, b in LATE_WORDS:
-                if g[0] <= a < g[1]:
-                    gather_words(a, b, words[:, :, (a - EARLY_WORDS) * C : (b - EARLY_WORDS) * C])
-
-        def run(g, last=None):
-            for e in range(*g):
-                first_product(e)
-            for e in range(g[0], last or g[1]):
-                square(e)
-
-        for e in range(1, GROUPS[0][1]):
-            first_product(e)
-        for e in range(*GROUPS[0]):
-            square(e)
-        later_loads(3)
-        run(GROUPS[1])
-        later_loads(4)
-
-        def load_w2(g):
-            w2[g] = keep.tile([P, g[1] - g[0], 2 * N], U8, name="w2_%d" % g[0], align_bytes=64)
-            nc.sync.dma_start(out=w2[g][:].bitcast(I32), in_=w2_words.rearrange("e s p b -> p (e s) b")[:, g[0] : g[1], :].bitcast(I32))
-
-        load_w2(W2_GROUPS[0])
-        for g in w2s:
-            load_w2_scales(g)
-        load_w2(W2_GROUPS[1])
-        nc.sync.dma_start(out=gate_rows[0 : TOP * BLOCKS, 0, :], in_=gate[:, 0, 0:TURNED].rearrange("r (b p) -> r b p", p=P))
-        for g in W2_GROUPS[2:]:
-            load_w2(g)
-        wg = keep.tile([P, PASSES, N], I32, name="wg", align_bytes=64)
-        nc.sync.dma_start(out=wg[:], in_=wg_words.rearrange("s p n d -> p s (n d)").bitcast(I32))
-        for r, src in enumerate((pos1, pos2, pos3)):
-            nc.sync.dma_start(pos[r][:], src)
-        gate_rest = [keep.tile([P, T - TURNED], F32, name="gate_rest%d" % r) for r in range(TOP)]
-        for r in range(TOP):
-            nc.sync.dma_start(out=gate_rest[r][:], in_=gate[r, :, TURNED:T])
-        for g in GROUPS[2:]:
-            run(g)
-        for j, g in enumerate(Y_GROUPS):
-            quantize(g, QTAGS[j])
-        for h in range(HALVES):
-            for j, g in enumerate(W2_GROUPS if h else Y_GROUPS):
-                second_product(g, h, Y_BANKS[h][j])
-
-        last = T - WIDE
-        logits = [bank(b, n) for b, n in zip(GATE_BANKS, (WIDE, last + TURNED, T - TURNED))]
-        gate_product(logits[0][:], 0, 0, WIDE)
-        gate_product(logits[1][:, 0:last], 0, WIDE, T)
-        gate_product(logits[1][:, last : last + TURNED], 1, 0, TURNED)
-        gate_product(logits[2][:, 0 : WIDE - TURNED], 1, TURNED, WIDE)
-        gate_product(logits[2][:, WIDE - TURNED : T - TURNED], 1, WIDE, T)
+        over = T - BANK
+        logits = [bank(b, n) for b, n in zip(GATE_BANKS, (BANK, over + TURNED, REST))]
+        gate_product(logits[0][:], 0, 0, BANK)
+        gate_product(logits[1][:, 0:over], 0, BANK, T)
+        gate_product(logits[1][:, over : over + TURNED], 1, 0, TURNED)
+        gate_product(logits[2][:, 0 : BANK - TURNED], 1, TURNED, BANK)
+        gate_product(logits[2][:, BANK - TURNED : REST], 1, BANK, T)
         o_first = keep.tile([P, T], F32, name="o_first")
-        nc.scalar.activation(o_first[:, 0:WIDE], logits[0][:], ACT.Sigmoid)
-        nc.scalar.activation(o_first[:, WIDE:T], logits[1][:, 0:last], ACT.Sigmoid)
-        o = {(0, 0): o_first[:, 0:TURNED], (0, TURNED): o_first[:, TURNED:T]}
+        nc.scalar.activation(o_first[:, 0:BANK], logits[0][:], ACT.Sigmoid)
+        nc.scalar.activation(o_first[:, BANK:T], logits[1][:, 0:over], ACT.Sigmoid)
+
         turned_rows = bank(ROWS_BANK, P)
         nc.tensor.transpose(turned_rows[:], gate_rows[:, 0, :], ident[:])
         by_token = keep.tile([P, TOP * BLOCKS], F32, name="by_token")
         nc.scalar.copy(by_token[:], turned_rows[:, 0 : TOP * BLOCKS])
 
-        rest = T - TURNED
-        parts = {}
+        parts, back = {}, {}
 
-        def scalar_gather(h, r):
+        def gather_part(h, r):
             parts[h, r] = keep.tile([P, TURNED], F32, name="part%d_%d" % (h, r))
             nc.scalar.activation(parts[h, r][:], y[h][:].indirect(pos[r][:, 0 : TURNED // 16]), ACT.Copy)
 
-        back = {}
-
-        def weigh(h, r):
+        def weigh_part(h, r):
             turned = bank(PART_BANKS[(TOP * h + r) % len(PART_BANKS)], BLOCKS, P)
             for k in range(BLOCKS):
                 nc.tensor.transpose(turned[:, k, :], parts[h, r][:, P * k : P * (k + 1)], ident[:])
@@ -321,42 +279,40 @@ def tile_moe_ogt_relu2_sigmoid_kernel(tc, x_words, x_scales, wg_words, wg_scales
 
         steps = [(h, r) for h in range(HALVES) for r in range(TOP)]
         for j, step in enumerate(steps):
-            scalar_gather(*step)
+            gather_part(*step)
             if j > 0:
-                weigh(*steps[j - 1])
-        late = keep.tile([P, rest], F32, name="o_rest", tag="part1_1")
-        nc.scalar.activation(late[:], logits[2][:], ACT.Sigmoid)
-        o[1, TURNED] = late[:]
-        weigh(*steps[-1])
-        late = keep.tile([P, TURNED], F32, name="o_turned", tag="part1_2")
-        nc.scalar.activation(late[:], logits[1][:, last : last + TURNED], ACT.Sigmoid)
-        o[1, 0] = late[:]
+                weigh_part(*steps[j - 1])
+        o_rest = keep.tile([P, REST], F32, name="o_rest", tag="part1_1")
+        nc.scalar.activation(o_rest[:], logits[2][:], ACT.Sigmoid)
+        weigh_part(*steps[-1])
+        o_turned = keep.tile([P, TURNED], F32, name="o_turned", tag="part1_2")
+        nc.scalar.activation(o_turned[:], logits[1][:, over : over + TURNED], ACT.Sigmoid)
 
         terms = {}
-        sums = [keep.tile([P, TOP - 1, rest], F32, name="sums%d" % h) for h in range(HALVES)]
+        sums = [keep.tile([P, TOP - 1, REST], F32, name="sums%d" % h) for h in range(HALVES)]
 
-        def vector_gather(h, r):
-            terms[h, r] = keep.tile([P, rest], F32, name="term%d" % r)
+        def gather_term(h, r):
+            terms[h, r] = keep.tile([P, REST], F32, name="term%d" % r)
             nc.vector.tensor_tensor(terms[h, r][:], y[h][:].indirect(pos[r][:, TURNED // 16 : T // 16]), gate_rest[r][:], ALU.mult)
 
-        def add(h, r):
+        def add_term(h, r):
             nc.vector.tensor_tensor(sums[h][:, r - 1, :], terms[h, 0][:] if r == 1 else sums[h][:, r - 2, :], terms[h, r][:], ALU.add)
 
-        def finish(h, total, t0, t1):
-            res = keep.tile([P, t1 - t0], F32, name="res%d_%d" % (h, t0), tag="sums1" if (h, t0) == (1, 0) else "res%d_%d" % (h, t0))
-            nc.vector.tensor_tensor(res[:], total, o[h, t0], ALU.mult)
+        def finish(h, t0, t1, total, o, tag):
+            res = keep.tile([P, t1 - t0], F32, name="res%d_%d" % (h, t0), tag=tag)
+            nc.vector.tensor_tensor(res[:], total, o, ALU.mult)
             nc.sync.dma_start(out=out[P * h : P * (h + 1), t0:t1], in_=res[:])
 
         for r in range(TOP):
-            vector_gather(0, r)
-        add(0, 1)
-        vector_gather(1, 0)
-        add(0, 2)
-        vector_gather(1, 1)
-        finish(0, sums[0][:, 1, :], TURNED, T)
-        vector_gather(1, 2)
-        add(1, 1)
-        finish(0, back[0][:].rearrange("p k t -> p (k t)"), 0, TURNED)
-        add(1, 2)
-        finish(1, sums[1][:, 1, :], TURNED, T)
-        finish(1, back[1][:].rearrange("p k t -> p (k t)"), 0, TURNED)
+            gather_term(0, r)
+        add_term(0, 1)
+        gather_term(1, 0)
+        add_term(0, 2)
+        gather_term(1, 1)
+        gather_term(1, 2)
+        add_term(1, 1)
+        finish(0, TURNED, T, sums[0][:, TOP - 2, :], o_first[:, TURNED:T], "res0_rest")
+        add_term(1, 2)
+        finish(0, 0, TURNED, back[0][:].rearrange("p k t -> p (k t)"), o_first[:, 0:TURNED], "res0_turned")
+        finish(1, TURNED, T, sums[1][:, TOP - 2, :], o_rest[:], "res1_rest")
+        finish(1, 0, TURNED, back[1][:].rearrange("p k t -> p (k t)"), o_turned[:], "sums1")

from contextlib import ExitStack

import concourse.mybir as mybir
from concourse.masks import make_identity

K, T, E, C, H, N, TOP = 1024, 640, 15, 128, 512, 256, 3
S = E * C
P = 128
PASSES = K // 512
HALVES = N // P
FLOPS = 2 * K * N * T + 2 * S * (K * H + H * N)

F32 = mybir.dt.float32
BF16 = mybir.dt.bfloat16
I32 = mybir.dt.int32
U32 = mybir.dt.uint32
U16 = mybir.dt.uint16
U8 = mybir.dt.uint8
FP8X4 = mybir.dt.float8_e4m3fn_x4
FP4X4 = mybir.dt.float4_e2m1fn_x4
ACT = mybir.ActivationFunctionType
ALU = mybir.AluOpType

RUN = 3
RUNS = [(a, a + RUN) for a in range(0, E, RUN)]
SCALE_TILES = 3
EARLY_WORDS = [(0, 1), (1, 3), (3, 5)]
AHEAD = EARLY_WORDS[-1][1]
H_GROUPS = [(0, 4), (4, 8), (8, 12), (12, 14), (14, 15)]
W2_GROUPS = [(0, 4), (4, 8), (8, 12), (12, 15)]
Y_GROUPS = (H_GROUPS, W2_GROUPS)
Y_BANKS = ((7, 6, 0, 1, 2), (2, 1, 0, 6))
VECTOR_Y = (H_GROUPS[0], H_GROUPS[3], H_GROUPS[4])
PRE_BANKS = (0, 1, 2)
TURN_BANKS = (3, 4, 5, 6)
BLOCKS = 2
TURNED = BLOCKS * P
REST = T - TURNED
BANK = 512
GATE_BANKS = (3, 4, 5)
ROWS_BANK = 6
PART_BANKS = (6, 1, 0)
BACK_BANKS = (7, 2)


def group_of(groups, e):
    return [g for g in groups if g[0] <= e < g[1]][0]


def tile_moe_ogt_relu2_sigmoid_kernel(tc, x_words, x_scales, wg_words, wg_scales, w1_words, w1_scales, w2_words, w2_scales, gate, offs, pos1, pos2, pos3, out):
    nc = tc.nc
    with ExitStack() as ctx:
        keep = ctx.enter_context(tc.tile_pool(name="keep", bufs=1))
        ring = ctx.enter_context(tc.tile_pool(name="ring", bufs=RUN + 1))
        psum = ctx.enter_context(tc.psum_pool(name="psum", bufs=1))

        def bank(b, *shape):
            return psum.tile([P, *shape], F32, name="bank%d" % b)

        def zero(engine, tile):
            engine.memset(tile[:].rearrange("p m w -> p (m w)").bitcast(I32), 0)

        def load_scale_rows(tile, rows, which=range(4)):
            for r in which:
                nc.sync.dma_start(out=tile[r:P:32].bitcast(I32), in_=rows[r:16:4].bitcast(I32))

        xs = keep.tile([P, PASSES, T], U8, name="xs", align_bytes=64)
        zero(nc.gpsimd, xs)
        slot_list = keep.tile([P, S // 16], U16, name="slot_list")
        nc.sync.dma_start(slot_list[:], offs)
        load_scale_rows(xs, x_scales.rearrange("s b t -> b s t"))
        xw = keep.tile([P, PASSES, T], I32, name="xw", align_bytes=64)
        nc.sync.dma_start(out=xw[:], in_=x_words.rearrange("s p t d -> p s (t d)").bitcast(I32))

        ident = keep.tile([P, P], F32, name="ident")
        make_identity(nc, ident[:])
        warm = keep.tile([P, 1], F32, name="warm")
        nc.scalar.activation(warm[:], ident[:, 0:1], ACT.Sigmoid)

        w1_scale_tiles = [keep.tile([P, PASSES * RUN, H], U8, name="plane%d" % j, align_bytes=64) for j in range(SCALE_TILES)]
        w2s = keep.tile([P, E, N], U8, name="small", align_bytes=64)
        wgs = keep.tile([P, PASSES, N], U8, name="wgs", align_bytes=64)
        gate_rows = keep.tile([P, 1, P], F32, name="gate_rows")
        for tile in w1_scale_tiles[:2]:
            zero(nc.vector, tile)
        for tile in (w1_scale_tiles[2], wgs, w2s, gate_rows):
            zero(nc.gpsimd, tile)
        w1s = {g: w1_scale_tiles[j % SCALE_TILES] for j, g in enumerate(RUNS)}

        def slots(a, b):
            return slot_list[:, a * C // 16 : b * C // 16]

        xg, sg = {}, {}

        def gather_scales(a, b, scales):
            for s in range(PASSES):
                nc.vector.tensor_copy(scales[:, s, :], xs[:, s, :].indirect(slots(a, b)))
            for e in range(a, b):
                sg[e] = scales[:, :, (e - a) * C : (e - a + 1) * C]

        def gather_words(a, b, words):
            for s in range(PASSES):
                nc.vector.tensor_copy(words[:, s, :], xw[:, s, :].bitcast(U32).indirect(slots(a, b)))
            for e in range(a, b):
                xg[e] = words[:, :, (e - a) * C : (e - a + 1) * C]

        gather_scales(0, RUN, keep.tile([P, PASSES, RUN * C], U8, name="sg0", align_bytes=64)[:])
        for a, b in EARLY_WORDS:
            gather_words(a, b, keep.tile([P, PASSES, (b - a) * C], U32, name="xg%d" % a, align_bytes=64)[:])

        w1, w2 = {}, {}

        def load_w1(a, b):
            tile = keep.tile([P, (b - a) * PASSES, 2 * H], U8, name="w1_%d" % a, align_bytes=64)
            nc.sync.dma_start(out=tile[:].bitcast(I32), in_=w1_words.rearrange("e s p b -> p (e s) b")[:, PASSES * a : PASSES * b, :].bitcast(I32))
            for e in range(a, b):
                w1[e] = tile[:, (e - a) * PASSES : (e - a + 1) * PASSES, :]

        def load_run(j):
            a, b = RUNS[j]
            load_scale_rows(w1s[a, b], w1_scales.rearrange("e s b i -> b (e s) i")[:, PASSES * a : PASSES * b, :])
            load_w1(max(a, 1), b)
            if j > 0:
                load_scale_rows(wgs, wg_scales.rearrange("s b n -> b s n"), [j - 1])

        def load_w2(g):
            w2[g] = keep.tile([P, g[1] - g[0], 2 * N], U8, name="w2_%d" % g[0], align_bytes=64)
            nc.sync.dma_start(out=w2[g][:].bitcast(I32), in_=w2_words.rearrange("e s p b -> p (e s) b")[:, g[0] : g[1], :].bitcast(I32))

        y = [keep.tile([P, S], F32, name="y%d" % h) for h in range(HALVES)]
        relus, hb, hq, hs = {}, {}, {}, {}

        def first_product(e):
            g = group_of(RUNS, e)
            pre = bank(PRE_BANKS[e % len(PRE_BANKS)], H)
            for s in range(PASSES):
                nc.tensor.matmul_mx(
                    out=pre[:],
                    lhsT=xg[e][:, s, :].bitcast(FP8X4),
                    lhsT_scale=sg[e][:, s, :],
                    rhs=w1[e][:, s, :].bitcast(FP4X4),
                    rhs_scale=w1s[g][:, (e - g[0]) * PASSES + s, :],
                    start=(s == 0),
                    stop=(s == PASSES - 1),
                )
            relus[e] = ring.tile([P, 4, P], F32, name="relu")
            if e == E - 1:
                nc.vector.tensor_scalar_max(relus[e][:], pre[:].rearrange("u (p d) -> u d p", d=4), 0.0)
            else:
                nc.scalar.activation(relus[e][:], pre[:].rearrange("u (p d) -> u d p", d=4), ACT.Relu)

        def square(e):
            g = group_of(H_GROUPS, e)
            turned = bank(TURN_BANKS[e % len(TURN_BANKS)], 4, C)
            for d in range(4):
                nc.tensor.transpose(turned[:, d, :], relus[e][:, d, :], ident[:])
            if e == g[0]:
                hb[g] = keep.tile([P, (g[1] - g[0]) * C, 4], BF16, name="hb%d" % e, align_bytes=64)
            nc.scalar.activation(hb[g][:, (e - g[0]) * C : (e - g[0] + 1) * C, :], turned[:].rearrange("p d u -> p u d"), ACT.Square)

        def run(g, first=None):
            for e in range(first or g[0], g[1]):
                first_product(e)
            for e in range(*g):
                square(e)

        def quantize(g, tag):
            n = (g[1] - g[0]) * C
            hq[g] = keep.tile([P, n], U32, name="hq%d" % g[0], tag=tag, align_bytes=64)
            hs[g] = keep.tile([P, n], U8, name="hs%d" % g[0], align_bytes=64)
            nc.vector.quantize_mx(out=hq[g][:].bitcast(FP8X4), scales=hs[g][:], in_=hb[g][:].rearrange("p u d -> p (u d)"))

        def second_product(g, h, b):
            acc = bank(b, (g[1] - g[0]) * C)
            for e in range(*g):
                gw, gq = group_of(W2_GROUPS, e), group_of(H_GROUPS, e)
                own = slice((e - gq[0]) * C, (e - gq[0] + 1) * C)
                nc.tensor.matmul_mx(
                    out=acc[:, (e - g[0]) * C : (e - g[0] + 1) * C],
                    lhsT=w2[gw][:, e - gw[0], 2 * P * h : 2 * P * (h + 1)].bitcast(FP4X4),
                    lhsT_scale=w2s[:, e, P * h : P * (h + 1)],
                    rhs=hq[gq][:, own].bitcast(FP8X4),
                    rhs_scale=hs[gq][:, own],
                    start=True,
                    stop=True,
                )
            if h == 0 and g in VECTOR_Y:
                nc.vector.tensor_copy(y[h][:, g[0] * C : g[1] * C], acc[:])
            else:
                nc.scalar.copy(y[h][:, g[0] * C : g[1] * C], acc[:])

        pos = [keep.tile([P, T // 16], U16, name="pos%d" % r) for r in range(TOP)]
        load_w1(0, 1)
        for j in range(SCALE_TILES):
            load_run(j)
        first_product(0)
        late_words = keep.tile([P, PASSES, (E - AHEAD) * C], U32, name="xg_late", tag="xg0", align_bytes=64)
        late_scales = keep.tile([P, PASSES, (E - RUN) * C], U8, name="sg_late", tag="w1_0", align_bytes=64)
        have = AHEAD
        for a, b in RUNS[1:]:
            gather_scales(a, b, late_scales[:, :, (a - RUN) * C : (b - RUN) * C])
            for upto in range(a + 1, b + 1) if b == E else [min(b + 1, E - RUN)]:
                gather_words(have, upto, late_words[:, :, (have - AHEAD) * C : (upto - AHEAD) * C])
                have = upto

        run(RUNS[0], first=1)
        load_run(SCALE_TILES)
        run(RUNS[1])
        load_run(SCALE_TILES + 1)

        load_w2(W2_GROUPS[0])
        load_scale_rows(w2s, w2_scales.rearrange("e s b n -> b (e s) n"))
        load_w2(W2_GROUPS[1])
        nc.sync.dma_start(out=gate_rows[0 : TOP * BLOCKS, 0, :], in_=gate[:, 0, 0:TURNED].rearrange("r (b p) -> r b p", p=P))
        for g in W2_GROUPS[2:]:
            load_w2(g)
        wg = keep.tile([P, PASSES, N], I32, name="wg", align_bytes=64)
        nc.sync.dma_start(out=wg[:], in_=wg_words.rearrange("s p n d -> p s (n d)").bitcast(I32))
        for r, src in enumerate((pos1, pos2, pos3)):
            nc.sync.dma_start(pos[r][:], src)
        gate_rest = [keep.tile([P, REST], F32, name="gate_rest%d" % r) for r in range(TOP)]
        for r in range(TOP):
            nc.sync.dma_start(out=gate_rest[r][:], in_=gate[r, :, TURNED:T])

        for g in RUNS[2:]:
            run(g)
        held = {H_GROUPS[1]: "xg0", H_GROUPS[2]: "w1_%d" % RUNS[-1][0]}
        for g in H_GROUPS:
            quantize(g, held.get(g, "hq%d" % g[0]))
        for h in range(HALVES):
            for g, b in zip(Y_GROUPS[h], Y_BANKS[h]):
                second_product(g, h, b)

        def gate_product(acc, h, t0, t1):
            for s in range(PASSES):
                nc.tensor.matmul_mx(
                    out=acc,
                    lhsT=wg[:, s, P * h : P * (h + 1)].bitcast(FP8X4),
                    lhsT_scale=wgs[:, s, P * h : P * (h + 1)],
                    rhs=xw[:, s, t0:t1].bitcast(FP8X4),
                    rhs_scale=xs[:, s, t0:t1],
                    start=(s == 0),
                    stop=(s == PASSES - 1),
                )

        over = T - BANK
        logits = [bank(b, n) for b, n in zip(GATE_BANKS, (BANK, over + TURNED, REST))]
        gate_product(logits[0][:], 0, 0, BANK)
        gate_product(logits[1][:, 0:over], 0, BANK, T)
        gate_product(logits[1][:, over : over + TURNED], 1, 0, TURNED)
        gate_product(logits[2][:, 0 : BANK - TURNED], 1, TURNED, BANK)
        gate_product(logits[2][:, BANK - TURNED : REST], 1, BANK, T)
        o_first = keep.tile([P, T], F32, name="o_first")
        nc.scalar.activation(o_first[:, 0:BANK], logits[0][:], ACT.Sigmoid)
        nc.scalar.activation(o_first[:, BANK:T], logits[1][:, 0:over], ACT.Sigmoid)

        turned_rows = bank(ROWS_BANK, P)
        nc.tensor.transpose(turned_rows[:], gate_rows[:, 0, :], ident[:])
        by_token = keep.tile([P, TOP * BLOCKS], F32, name="by_token")
        nc.scalar.copy(by_token[:], turned_rows[:, 0 : TOP * BLOCKS])

        parts, back = {}, {}

        def gather_part(h, r):
            parts[h, r] = keep.tile([P, TURNED], F32, name="part%d_%d" % (h, r))
            nc.scalar.activation(parts[h, r][:], y[h][:].indirect(pos[r][:, 0 : TURNED // 16]), ACT.Copy)

        def weigh_part(h, r):
            turned = bank(PART_BANKS[(TOP * h + r) % len(PART_BANKS)], BLOCKS, P)
            for k in range(BLOCKS):
                nc.tensor.transpose(turned[:, k, :], parts[h, r][:, P * k : P * (k + 1)], ident[:])
            weighted = keep.tile([P, BLOCKS, P], F32, name="weighted%d_%d" % (h, r))
            for k in range(BLOCKS):
                nc.scalar.activation(weighted[:, k, :], turned[:, k, :], ACT.Copy, scale=by_token[:, BLOCKS * r + k : BLOCKS * r + k + 1])
            if r == 0:
                back[h] = bank(BACK_BANKS[h], BLOCKS, P)
            for k in range(BLOCKS):
                nc.tensor.matmul(back[h][:, k, :], lhsT=weighted[:, k, :], rhs=ident[:], is_transpose=True, start=(r == 0 and k == 0), stop=(r == TOP - 1 and k == BLOCKS - 1))

        steps = [(h, r) for h in range(HALVES) for r in range(TOP)]
        for j, step in enumerate(steps):
            gather_part(*step)
            if j > 0:
                weigh_part(*steps[j - 1])
        o_rest = keep.tile([P, REST], F32, name="o_rest", tag="part1_1")
        nc.scalar.activation(o_rest[:], logits[2][:], ACT.Sigmoid)
        weigh_part(*steps[-1])
        o_turned = keep.tile([P, TURNED], F32, name="o_turned", tag="part1_2")
        nc.scalar.activation(o_turned[:], logits[1][:, over : over + TURNED], ACT.Sigmoid)

        terms = {}
        sums = [keep.tile([P, TOP - 1, REST], F32, name="sums%d" % h) for h in range(HALVES)]

        def gather_term(h, r):
            terms[h, r] = keep.tile([P, REST], F32, name="term%d" % r)
            nc.vector.tensor_tensor(terms[h, r][:], y[h][:].indirect(pos[r][:, TURNED // 16 : T // 16]), gate_rest[r][:], ALU.mult)

        def add_term(h, r):
            nc.vector.tensor_tensor(sums[h][:, r - 1, :], terms[h, 0][:] if r == 1 else sums[h][:, r - 2, :], terms[h, r][:], ALU.add)

        def finish(h, t0, t1, total, o, tag):
            res = keep.tile([P, t1 - t0], F32, name="res%d_%d" % (h, t0), tag=tag)
            nc.vector.tensor_tensor(res[:], total, o, ALU.mult)
            nc.sync.dma_start(out=out[P * h : P * (h + 1), t0:t1], in_=res[:])

        for r in range(TOP):
            gather_term(0, r)
        add_term(0, 1)
        gather_term(1, 0)
        add_term(0, 2)
        gather_term(1, 1)
        gather_term(1, 2)
        add_term(1, 1)
        finish(0, TURNED, T, sums[0][:, TOP - 2, :], o_first[:, TURNED:T], "res0_rest")
        add_term(1, 2)
        finish(0, 0, TURNED, back[0][:].rearrange("p k t -> p (k t)"), o_first[:, 0:TURNED], "res0_turned")
        finish(1, TURNED, T, sums[1][:, TOP - 2, :], o_rest[:], "res1_rest")
        finish(1, 0, TURNED, back[1][:].rearrange("p k t -> p (k t)"), o_turned[:], "sums1")
